import numpy as np
import ml_dtypes


def mxq(x, axis, fmt="e4m3"):
    dtype, down = {"e4m3": (ml_dtypes.float8_e4m3fn, 7), "e5m2": (ml_dtypes.float8_e5m2, 14)}[fmt]
    v = np.moveaxis(np.asarray(x, np.float32).astype(ml_dtypes.bfloat16).astype(np.float64), axis, -1)
    blocks = v.reshape(v.shape[:-1] + (-1, 32))
    amax = np.abs(blocks).max(-1, keepdims=True)
    byte = np.maximum(np.where(amax > 0, np.frexp(amax)[1] - 1 + 127, 0) - down, 1)
    scale = np.exp2(byte - 127.0)
    codes = (blocks / scale).astype(np.float32).astype(dtype).astype(np.float64)
    return np.moveaxis((codes * scale).reshape(v.shape), -1, axis)


WIDE = False


def mx_kscale(k):
    if not WIDE:
        return np.ones(k)
    levels = np.array([10, -10, 5, -5, 0])
    if k % 512:
        return np.exp2(np.random.permutation(np.resize(levels, k // 32))).repeat(32)
    a = np.empty((k // 512, 16))
    for p in range(k // 512):
        a[p, :8] = np.random.permutation(np.resize(levels, 8))
        for g in range(8):
            far = levels[np.abs(levels - a[p, g]) >= 10]
            a[p, g + 8] = far[np.random.randint(len(far))]
    return np.exp2(a.ravel()).repeat(32)


def f64(x):
    return np.asarray(x).astype(np.float64)


def striped(idx):
    return np.tile(idx.reshape(-1, 16).T, (8, 1)).astype(np.uint16)


def unstriped(offs):
    return offs[:16].T.reshape(-1).astype(np.int64)


E2M1 = np.array([0.0, 0.5, 1.0, 1.5, 2.0, 3.0, 4.0, 6.0, -0.0, -0.5, -1.0, -1.5, -2.0, -3.0, -4.0, -6.0])


def pack_weight(w, fmt):
    k, n = w.shape
    w = f64(np.asarray(w, np.float32).astype(ml_dtypes.bfloat16)).reshape(k // 32, 32, n)
    amax = np.abs(w).max(1)
    if fmt == "e4m3":
        byte = np.frexp(amax)[1] - 1 + 127 - 7
    else:
        mant, ex = np.frexp(amax / 6.0)
        byte = np.where(mant > 0.5, ex, ex - 1) + 127
    byte = np.clip(np.where(amax > 0, byte, 1), 1, 254)
    scaled = (w * np.exp2(127.0 - byte)[:, None, :]).reshape(k, n).astype(np.float32)
    by_word = np.ascontiguousarray(scaled.reshape(k // 512, 128, 4, n).transpose(0, 1, 3, 2))
    if fmt == "e4m3":
        words = by_word.astype(ml_dtypes.float8_e4m3fn).view(np.uint8)
    else:
        c = by_word.astype(ml_dtypes.float4_e2m1fn).view(np.uint8) & 0xF
        words = (c[..., 0::2] | (c[..., 1::2] << 4)).reshape(k // 512, 128, 2 * n)
    return np.ascontiguousarray(words), np.ascontiguousarray(byte.astype(np.uint8).reshape(k // 512, 16, n))


def unpack_weight(words, scales, fmt):
    g, _, n = scales.shape
    words = np.ascontiguousarray(words).reshape(g, 128, n, -1)
    if fmt == "e4m3":
        vals = words.view(ml_dtypes.float8_e4m3fn).astype(np.float64)
    else:
        nib = np.empty((g, 128, n, 4), np.uint8)
        nib[..., 0::2] = words & 0xF
        nib[..., 1::2] = words >> 4
        vals = E2M1[nib]
    vals = vals * np.repeat(np.exp2(scales.astype(np.float64) - 127.0), 8, axis=1)[..., None]
    return vals.transpose(0, 1, 3, 2).reshape(g * 512, n)


def gelu(v):
    return 0.5 * v * (1.0 + np.tanh(np.sqrt(2.0 / np.pi) * (v + 0.044715 * v**3)))


K, K2, H, N, T, S, T2 = 1024, 512, 1024, 512, 2048, 1024, 2048

def setup_inputs():
    n = np.random.standard_normal
    s = mx_kscale(K)[:, None]
    s2 = mx_kscale(K2)[:, None]
    u = mx_kscale(H)[:, None]
    tab_words, tab_scales = pack_weight(n((K, T)) * s, "e4m3")
    tab2_words, tab2_scales = pack_weight(n((K2, T)) * s2, "e4m3")
    w1_words, w1_scales = pack_weight(n((K, H)) / np.sqrt(K) / s, "e2m1")
    w2 = (n((K2, H)) / np.sqrt(K2) / s2).astype(np.float32)
    w3_words, w3_scales = pack_weight(n((H, N)) / np.sqrt(H) / u, "e4m3")
    resp = (np.exp(0.3 * n((H, T2))) * np.sqrt(u)).astype(np.float32)
    perm = np.random.permutation(T2)
    return {"tab_words": tab_words, "tab_scales": tab_scales,
            "tab2_words": tab2_words, "tab2_scales": tab2_scales,
            "w1_words": w1_words, "w1_scales": w1_scales, "w2": w2,
            "w3_words": w3_words, "w3_scales": w3_scales, "resp": resp,
            "wg1": np.exp(0.3 * n((128, S))).astype(np.float32),
            "wg2": np.exp(0.3 * n((128, S))).astype(np.float32),
            "offs": striped(np.random.permutation(T)[:S]),
            "offs2": striped(np.random.permutation(T)[:S]),
            "offs3": striped(perm[:S]), "offs4": striped(perm[S:])}

def reference(tab_words, tab_scales, tab2_words, tab2_scales, w1_words, w1_scales, w2,
              w3_words, w3_scales, resp, wg1, wg2, offs, offs2, offs3, offs4):
    v = unpack_weight(tab_words, tab_scales, "e4m3")[:, unstriped(offs)]
    v2 = unpack_weight(tab2_words, tab2_scales, "e4m3")[:, unstriped(offs2)]
    w1 = unpack_weight(w1_words, w1_scales, "e2m1")
    h1 = np.maximum(w1.T @ v, 0.0)
    h2 = np.square(mxq(f64(w2), 0, "e4m3").T @ v2)
    page = np.zeros((H, T2))
    page[:, unstriped(offs3)] = np.tile(f64(wg1), (H // 128, 1)) * h1
    page[:, unstriped(offs4)] = np.tile(f64(wg2), (H // 128, 1)) * h2
    z = page * (f64(resp) * f64(resp))
    w3 = unpack_weight(w3_words, w3_scales, "e4m3")
    return w3.T @ mxq(z, 0, "e4m3")

@@ -1,0 +1,273 @@
+from contextlib import ExitStack
+
+import concourse.mybir as mybir
+
+K, K2, H, N, T, S, T2 = 1024, 512, 1024, 512, 2048, 1024, 2048
+FLOPS = 2 * (K * H * S + K2 * H * S + H * N * T2)
+
+F32 = mybir.dt.float32
+BF16 = mybir.dt.bfloat16
+I32 = mybir.dt.int32
+U32 = mybir.dt.uint32
+U16 = mybir.dt.uint16
+U8 = mybir.dt.uint8
+FP8X4 = mybir.dt.float8_e4m3fn_x4
+FP4X4 = mybir.dt.float4_e2m1fn_x4
+ACT = mybir.ActivationFunctionType
+MULT = mybir.AluOpType.mult
+
+P = 128
+PACK = 4
+K_PASS = P * PACK
+BANK = 512
+QUAD = 32
+PAGES = H // P
+PAGE_SLOTS = 3
+RESP_SLOTS = 3
+FEAT_SLOTS = 6
+AHEAD = 4
+HALF = T2 // 2
+
+
+def tile_list_shower_deposit_weave_kernel(
+    tc, tab_words, tab_scales, tab2_words, tab2_scales, w1_words, w1_scales, w2,
+    w3_words, w3_scales, resp, wg1, wg2, offs, offs2, offs3, offs4, out,
+):
+    nc = tc.nc
+    with ExitStack() as ctx:
+        sb = ctx.enter_context(tc.tile_pool(name="sb", bufs=1))
+        ps = ctx.enter_context(tc.psum_pool(name="ps", bufs=1))
+
+        def slot(name, shape, dtype, tag=None):
+            return sb.tile(shape, dtype, name=name, tag=tag or name, align_bytes=64)
+
+        def load_list(name, src):
+            lst = slot(name, [P, S // 16], U16)
+            nc.sync.dma_start(lst[:], src)
+            return lst
+
+        def zero(engine, plane):
+            engine.memset(plane.bitcast(I32), 0)
+
+        banks = [ps.tile([P, BANK], F32, name="bank%d" % j, tag="bank%d" % j) for j in range(8)]
+
+        tab2_sc = slot("tab2_sc", [P, T], U8)
+        tab_sc = slot("tab_sc", [P, T], U8)
+        w1_sc_raw = slot("w1_sc_raw", [P, 2 * H], U8)
+        v1_sc_b = slot("v1_sc_b", [P, S], U8)
+        w3_sc = slot("w3_sc", [P, 2 * N], U8)
+        zero(nc.vector, tab2_sc[:])
+        zero(nc.vector, tab_sc[:])
+        zero(nc.gpsimd, w1_sc_raw[:])
+        zero(nc.gpsimd, v1_sc_b[:])
+        zero(nc.gpsimd, w3_sc[:])
+
+        idx2 = load_list("idx2", offs2)
+        idx1 = load_list("idx1", offs)
+        for q in range(4):
+            nc.sync.dma_start(tab2_sc[QUAD * q : QUAD * q + 4, :].bitcast(I32),
+                              tab2_scales[0, 4 * q : 4 * q + 4, :].bitcast(I32))
+        for q in range(4):
+            nc.sync.dma_start(tab_sc[QUAD * q : QUAD * q + 8, :].bitcast(I32),
+                              tab_scales[:, 4 * q : 4 * q + 4, :].bitcast(I32))
+        for q in range(4):
+            nc.sync.dma_start(w1_sc_raw[QUAD * q : QUAD * q + 4, :].bitcast(I32).rearrange("r (a n) -> r a n", a=2),
+                              w1_scales[:, 4 * q : 4 * q + 4, :].rearrange("a r n -> r a n").bitcast(I32))
+
+        def load_words(name, src, tag=None):
+            words = slot(name, [P, T], I32, tag)
+            nc.sync.dma_start(words[:], src.rearrange("p n i -> p (n i)").bitcast(I32))
+            return words
+
+        def load_w2(b):
+            raw = slot("w2_raw%d" % b, [P, PACK, K_PASS], F32, "resp1" if b == 0 else "tab2_w")
+            nc.sync.dma_start(raw[:], w2[:, K_PASS * b : K_PASS * (b + 1)].rearrange("(p j) c -> p j c", j=PACK))
+            return raw
+
+        def load_wg(name, src, half):
+            wg = slot("%s_%d" % (name, half), [P, 2, S], F32)
+            rows = src.rearrange("(m t) j -> m t j", t=PACK)[:, 2 * half : 2 * half + 2, :]
+            for q in range(4):
+                nc.sync.dma_start(wg[QUAD * q : QUAD * (q + 1), :, :], rows)
+            return wg
+
+        def load_resp(i):
+            b, t = divmod(i, PACK)
+            r = slot("resp_%d" % i, [P, T2], F32, "resp%d" % (i % RESP_SLOTS))
+            nc.sync.dma_start(r[:], resp[K_PASS * b : K_PASS * (b + 1), :].rearrange("(p t) n -> p t n", t=PACK)[:, t, :])
+            for h in range(2):
+                cols = slice(HALF * h, HALF * (h + 1))
+                nc.scalar.activation(r[:, cols], r[:, cols], ACT.Square)
+            return r
+
+        tab2_w = load_words("tab2_w", tab2_words[0])
+        w2_raw = [load_w2(0)]
+        w1_raw = slot("w1_raw", [P, 2 * 2 * H], U8)
+        nc.sync.dma_start(w1_raw[:].bitcast(I32).rearrange("p (a n) -> p a n", a=2),
+                          w1_words.rearrange("a p n -> p a n").bitcast(I32))
+        tab_w = [load_words("tab_w%d" % a, tab_words[a], "planes%d" % a) for a in range(2)]
+        wg = {("had", 0): load_wg("wg2", wg2, 0)}
+        idx4 = load_list("idx4", offs4)
+        idx3 = load_list("idx3", offs3)
+
+        def gather(name, window, lst, dtype):
+            picked = slot(name, [P, S], dtype)
+            nc.vector.tensor_copy(picked[:], window.indirect(lst[:]))
+            return picked
+
+        v2_sc = gather("v2_sc", tab2_sc[:], idx2, U8)
+        v1_sc_a = gather("v1_sc_a", tab_sc[:], idx1, U8)
+        v2_w = gather("v2_w", tab2_w[:].bitcast(U32), idx2, U32)
+
+        w2_codes = slot("w2_codes", [P, H], U32)
+        w2_sc = slot("w2_sc", [P, H], U8)
+
+        def quantize_w2(b):
+            grouped = slot("w2_bf%d" % b, [P, K_PASS * PACK], BF16, "woven%d" % b)
+            nc.scalar.copy(grouped[:].rearrange("p (t m j) -> p m t j", t=PACK, j=PACK),
+                           w2_raw[b][:].rearrange("p j (m t) -> p m t j", t=PACK))
+            cols = slice(K_PASS * b, K_PASS * (b + 1))
+            nc.vector.quantize_mx(out=w2_codes[:, cols].bitcast(FP8X4), scales=w2_sc[:, cols], in_=grouped[:])
+
+        quantize_w2(0)
+        v1_w = [gather("v1_w%d" % a, tab_w[a][:].bitcast(U32), idx1, U32) for a in range(2)]
+        w1_codes = slot("w1_codes", [P, 2 * 2 * H], U8)
+        nc.vector.tensor_copy(w1_codes[:].bitcast(U16).rearrange("p (g t m) -> p g t m", g=4, t=PACK),
+                              w1_raw[:].bitcast(U16).rearrange("p (g m t) -> p g t m", g=4, t=PACK))
+        w1_sc = slot("w1_sc", [P, 2 * H], U8)
+        nc.vector.tensor_copy(w1_sc[:].rearrange("p (g t m) -> p g t m", g=4, t=PACK),
+                              w1_sc_raw[:].rearrange("p (g m t) -> p g t m", g=4, t=PACK))
+        for q in range(4):
+            nc.gpsimd.dma_start(v1_sc_b[QUAD * q : QUAD * q + 4, :].bitcast(I32),
+                              v1_sc_a[QUAD * q + 4 : QUAD * q + 8, :].bitcast(I32))
+        v1_sc = [v1_sc_a, v1_sc_b]
+
+        wg[("pho", 0)] = load_wg("wg1", wg1, 0)
+        wg[("had", 1)] = load_wg("wg2", wg2, 1)
+        wg[("pho", 1)] = load_wg("wg1", wg1, 1)
+        w2_raw.append(load_w2(1))
+        quantize_w2(1)
+        resp2 = {}
+        w3_codes = slot("w3_codes", [P, 2 * N], I32)
+        nc.sync.dma_start(w3_codes[:].rearrange("p (a n) -> p a n", a=2),
+                          w3_words.rearrange("a p n i -> p a (n i)").bitcast(I32))
+        for q in range(4):
+            nc.sync.dma_start(w3_sc[QUAD * q : QUAD * q + 4, :].bitcast(I32).rearrange("r (a n) -> r a n", a=2),
+                              w3_scales[:, 4 * q : 4 * q + 4, :].rearrange("a r n -> r a n").bitcast(I32))
+
+        units = [("had", 0)]
+        for i in range(1, PAGES):
+            units += [("had", i), ("pho", i - 1)]
+        units.append(("pho", PAGES - 1))
+
+        feats = {}
+        raws = {}
+
+        def produce(u):
+            stream, i = units[u]
+            t = i % PACK
+            m0 = P * i
+            feat = slot("feat_%d" % u, [P, S], F32, "feat%d" % (u % FEAT_SLOTS))
+            host, half = divmod(u - 3, 2)
+            if host not in raws:
+                raws[host] = slot("raw_%d" % (host + 2), [P, 2 * S], F32, "resp%d" % (host % RESP_SLOTS))
+            raw = raws[host][:, S * half : S * (half + 1)]
+            for c in range(S // BANK):
+                cols = slice(BANK * c, BANK * (c + 1))
+                if stream == "had":
+                    bank = banks[c]
+                    nc.tensor.matmul_mx(out=bank[:], lhsT=w2_codes[:, m0 : m0 + P].bitcast(FP8X4),
+                                        lhsT_scale=w2_sc[:, m0 : m0 + P],
+                                        rhs=v2_w[:, cols].bitcast(FP8X4), rhs_scale=v2_sc[:, cols],
+                                        start=True, stop=True)
+                    nc.scalar.activation(raw[:, cols], bank[:], ACT.Square)
+                else:
+                    bank = banks[2 + c]
+                    for a in range(2):
+                        c0 = H * a + m0
+                        nc.tensor.matmul_mx(out=bank[:], lhsT=w1_codes[:, 2 * c0 : 2 * (c0 + P)].bitcast(FP4X4),
+                                            lhsT_scale=w1_sc[:, c0 : c0 + P],
+                                            rhs=v1_w[a][:, cols].bitcast(FP8X4), rhs_scale=v1_sc[a][:, cols],
+                                            start=(a == 0), stop=(a == 1))
+                    nc.scalar.activation(raw[:, cols], bank[:], ACT.Relu)
+            gain = wg[(stream, t // 2)][:, t % 2, :]
+            nc.gpsimd.tensor_tensor(feat[:], raw, gain, MULT)
+            feats[u] = (feat, gain)
+
+        pages = {}
+        planes = {}
+        z_codes = slot("z_codes", [P, 2 * T2], U32)
+        z_sc = slot("z_sc", [P, 2 * T2], U8)
+
+        def scatter(u):
+            stream, i = units[u]
+            if stream == "had":
+                pages[i] = slot("page_%d" % i, [P, T2], F32, "page%d" % (i % PAGE_SLOTS))
+            lst = idx4 if stream == "had" else idx3
+            feat, gain = feats[u]
+            nc.vector.tensor_copy(pages[i][:].indirect(lst[:]), feat[:])
+
+        def weigh(engine, i, cols):
+            b, t = divmod(i, PACK)
+            engine.tensor_tensor(planes[b][:, t, cols], pages[i][:, cols], resp2[i][:, cols], MULT)
+
+        def weave(copy, b, woven, cols):
+            copy(woven.rearrange("p (c i t) -> p c t i", t=PACK, i=4),
+                 planes[b][:, :, cols].rearrange("p t (c i) -> p c t i", i=4))
+
+        def quantize_z(b, woven, cols):
+            at = slice(T2 * b + cols.start, T2 * b + cols.stop)
+            nc.vector.quantize_mx(out=z_codes[:, at].bitcast(FP8X4), scales=z_sc[:, at], in_=woven)
+
+        for u in range(AHEAD):
+            produce(u)
+        for u in range(len(units)):
+            if u + AHEAD < len(units):
+                produce(u + AHEAD)
+            if u % 2 == 0:
+                resp2[u // 2] = load_resp(u // 2)
+            scatter(u)
+            stream, i = units[u]
+            if stream == "pho" and i < PAGES - 1:
+                b, t = divmod(i, PACK)
+                if t == 0:
+                    planes[b] = slot("planes_%d" % b, [P, PACK, T2], BF16, "planes%d" % b)
+                for h in range(2):
+                    weigh(nc.gpsimd, i, slice(HALF * h, HALF * (h + 1)))
+                if i == PACK - 1:
+                    for h in range(2):
+                        cols = slice(HALF * h, HALF * (h + 1))
+                        woven = slot("woven_0_%d" % h, [P, HALF * PACK], BF16, "woven%d" % h)
+                        weave(nc.scalar.copy, 0, woven[:], cols)
+                        quantize_z(0, woven[:], cols)
+
+        last = PAGES - 1
+        woven = [slot("woven_1_%d" % h, [P, HALF * PACK], BF16, "woven%d" % h) for h in range(2)]
+        stage = [slot("stage%d" % j, [P, S], F32, "feat%d" % j) for j in range(FEAT_SLOTS)]
+        stage.append(slot("stage_r", [P, T2], F32, "resp%d" % ((last - 1) % RESP_SLOTS)))
+        chunks = T2 // BANK
+        for c in range(chunks):
+            cols = slice(BANK * c, BANK * (c + 1))
+            part = woven[c // 2][:, (c % 2) * BANK * PACK : (c % 2 + 1) * BANK * PACK]
+            weigh(nc.vector, last, cols)
+            weave(nc.vector.tensor_copy, 1, part, cols)
+            quantize_z(1, part, cols)
+            for n in range(N // P):
+                bank = banks[4 * ((c + 1) % 2) + n]
+                for b in range(2):
+                    w0 = N * b + P * n
+                    z0 = T2 * b + BANK * c
+                    nc.tensor.matmul_mx(out=bank[:], lhsT=w3_codes[:, w0 : w0 + P].bitcast(FP8X4),
+                                        lhsT_scale=w3_sc[:, w0 : w0 + P],
+                                        rhs=z_codes[:, z0 : z0 + BANK].bitcast(FP8X4), rhs_scale=z_sc[:, z0 : z0 + BANK],
+                                        start=(b == 0), stop=(b == 1))
+                j = 4 * c + n
+                if j < 2 * FEAT_SLOTS:
+                    res = stage[j // 2][:, BANK * (j % 2) : BANK * (j % 2 + 1)]
+                else:
+                    res = stage[FEAT_SLOTS][:, BANK * (j - 2 * FEAT_SLOTS) : BANK * (j - 2 * FEAT_SLOTS + 1)]
+                if c == chunks - 1 and n % 2 == 1:
+                    nc.vector.tensor_copy(res, bank[:])
+                else:
+                    nc.scalar.copy(res, bank[:])
+                nc.sync.dma_start(out[P * n : P * (n + 1), cols], res)

@@ -56,23 +56,16 @@ def tile_list_shower_deposit_weave_kernel(
         w1_sc_raw = slot("w1_sc_raw", [P, 2 * H], U8)
         v1_sc_b = slot("v1_sc_b", [P, S], U8)
         w3_sc = slot("w3_sc", [P, 2 * N], U8)
-        zero(nc.vector, tab2_sc[:])
-        zero(nc.vector, tab_sc[:])
-        zero(nc.gpsimd, w1_sc_raw[:])
-        zero(nc.gpsimd, v1_sc_b[:])
-        zero(nc.gpsimd, w3_sc[:])
+        zero(nc.gpsimd, tab2_sc[:])
+        zero(nc.gpsimd, tab_sc[:])
+        zero(nc.vector, w1_sc_raw[:])
+        zero(nc.vector, v1_sc_b[:])
+        zero(nc.vector, w3_sc[:])
 
         idx2 = load_list("idx2", offs2)
-        idx1 = load_list("idx1", offs)
         for q in range(4):
             nc.sync.dma_start(tab2_sc[QUAD * q : QUAD * q + 4, :].bitcast(I32),
                               tab2_scales[0, 4 * q : 4 * q + 4, :].bitcast(I32))
-        for q in range(4):
-            nc.sync.dma_start(tab_sc[QUAD * q : QUAD * q + 8, :].bitcast(I32),
-                              tab_scales[:, 4 * q : 4 * q + 4, :].bitcast(I32))
-        for q in range(4):
-            nc.sync.dma_start(w1_sc_raw[QUAD * q : QUAD * q + 4, :].bitcast(I32).rearrange("r (a n) -> r a n", a=2),
-                              w1_scales[:, 4 * q : 4 * q + 4, :].rearrange("a r n -> r a n").bitcast(I32))
 
         def load_words(name, src, tag=None):
             words = slot(name, [P, T], I32, tag)
@@ -80,15 +73,15 @@ def tile_list_shower_deposit_weave_kernel(
             return words
 
         def load_w2(b):
-            raw = slot("w2_raw%d" % b, [P, PACK, K_PASS], F32, "resp1" if b == 0 else "tab2_w")
+            raw = slot("w2_raw%d" % b, [P, PACK, K_PASS], F32, "resp%d" % (1 - b))
             nc.sync.dma_start(raw[:], w2[:, K_PASS * b : K_PASS * (b + 1)].rearrange("(p j) c -> p j c", j=PACK))
             return raw
 
-        def load_wg(name, src, half):
-            wg = slot("%s_%d" % (name, half), [P, 2, S], F32)
-            rows = src.rearrange("(m t) j -> m t j", t=PACK)[:, 2 * half : 2 * half + 2, :]
+        def load_wg(name, src, t):
+            wg = slot("%s_%d" % (name, t), [P, S], F32)
+            rows = src.rearrange("(m t) j -> m t j", t=PACK)[:, t, :]
             for q in range(4):
-                nc.sync.dma_start(wg[QUAD * q : QUAD * (q + 1), :, :], rows)
+                nc.sync.dma_start(wg[QUAD * q : QUAD * (q + 1), :], rows)
             return wg
 
         def load_resp(i):
@@ -101,13 +94,22 @@ def tile_list_shower_deposit_weave_kernel(
             return r
 
         tab2_w = load_words("tab2_w", tab2_words[0])
+        idx1 = load_list("idx1", offs)
         w2_raw = [load_w2(0)]
+        for q in range(4):
+            nc.sync.dma_start(tab_sc[QUAD * q : QUAD * q + 8, :].bitcast(I32),
+                              tab_scales[:, 4 * q : 4 * q + 4, :].bitcast(I32))
+        tab_w = [load_words("tab_w0", tab_words[0], "planes0")]
+        w2_raw.append(load_w2(1))
+        tab_w.append(load_words("tab_w1", tab_words[1], "planes1"))
         w1_raw = slot("w1_raw", [P, 2 * 2 * H], U8)
         nc.sync.dma_start(w1_raw[:].bitcast(I32).rearrange("p (a n) -> p a n", a=2),
                           w1_words.rearrange("a p n -> p a n").bitcast(I32))
-        tab_w = [load_words("tab_w%d" % a, tab_words[a], "planes%d" % a) for a in range(2)]
-        wg = {("had", 0): load_wg("wg2", wg2, 0)}
         idx4 = load_list("idx4", offs4)
+        wg = {("had", 0): load_wg("wg2", wg2, 0)}
+        for q in range(4):
+            nc.sync.dma_start(w1_sc_raw[QUAD * q : QUAD * q + 4, :].bitcast(I32).rearrange("r (a n) -> r a n", a=2),
+                              w1_scales[:, 4 * q : 4 * q + 4, :].rearrange("a r n -> r a n").bitcast(I32))
         idx3 = load_list("idx3", offs3)
 
         def gather(name, window, lst, dtype):
@@ -123,7 +125,7 @@ def tile_list_shower_deposit_weave_kernel(
         w2_sc = slot("w2_sc", [P, H], U8)
 
         def quantize_w2(b):
-            grouped = slot("w2_bf%d" % b, [P, K_PASS * PACK], BF16, "woven%d" % b)
+            grouped = slot("w2_bf%d" % b, [P, K_PASS * PACK], BF16, "v1_w0" if b == 0 else "woven1")
             nc.scalar.copy(grouped[:].rearrange("p (t m j) -> p m t j", t=PACK, j=PACK),
                            w2_raw[b][:].rearrange("p j (m t) -> p m t j", t=PACK))
             cols = slice(K_PASS * b, K_PASS * (b + 1))
@@ -137,16 +139,16 @@ def tile_list_shower_deposit_weave_kernel(
         w1_sc = slot("w1_sc", [P, 2 * H], U8)
         nc.vector.tensor_copy(w1_sc[:].rearrange("p (g t m) -> p g t m", g=4, t=PACK),
                               w1_sc_raw[:].rearrange("p (g m t) -> p g t m", g=4, t=PACK))
-        for q in range(4):
-            nc.gpsimd.dma_start(v1_sc_b[QUAD * q : QUAD * q + 4, :].bitcast(I32),
-                              v1_sc_a[QUAD * q + 4 : QUAD * q + 8, :].bitcast(I32))
         v1_sc = [v1_sc_a, v1_sc_b]
 
-        wg[("pho", 0)] = load_wg("wg1", wg1, 0)
-        wg[("had", 1)] = load_wg("wg2", wg2, 1)
-        wg[("pho", 1)] = load_wg("wg1", wg1, 1)
-        w2_raw.append(load_w2(1))
         quantize_w2(1)
+        for q in range(4):
+            nc.sync.dma_start(v1_sc_b[QUAD * q : QUAD * q + 4, :].bitcast(I32),
+                              v1_sc_a[QUAD * q + 4 : QUAD * q + 8, :].bitcast(I32))
+        for t in range(1, PACK):
+            wg[("had", t)] = load_wg("wg2", wg2, t)
+            wg[("pho", t - 1)] = load_wg("wg1", wg1, t - 1)
+        wg[("pho", PACK - 1)] = load_wg("wg1", wg1, PACK - 1)
         resp2 = {}
         w3_codes = slot("w3_codes", [P, 2 * N], I32)
         nc.sync.dma_start(w3_codes[:].rearrange("p (a n) -> p a n", a=2),
@@ -190,7 +192,7 @@ def tile_list_shower_deposit_weave_kernel(
                                             rhs=v1_w[a][:, cols].bitcast(FP8X4), rhs_scale=v1_sc[a][:, cols],
                                             start=(a == 0), stop=(a == 1))
                     nc.scalar.activation(raw[:, cols], bank[:], ACT.Relu)
-            gain = wg[(stream, t // 2)][:, t % 2, :]
+            gain = wg[(stream, t)][:]
             nc.gpsimd.tensor_tensor(feat[:], raw, gain, MULT)
             feats[u] = (feat, gain)
 
@@ -242,32 +244,49 @@ def tile_list_shower_deposit_weave_kernel(
                         quantize_z(0, woven[:], cols)
 
         last = PAGES - 1
-        woven = [slot("woven_1_%d" % h, [P, HALF * PACK], BF16, "woven%d" % h) for h in range(2)]
-        stage = [slot("stage%d" % j, [P, S], F32, "feat%d" % j) for j in range(FEAT_SLOTS)]
-        stage.append(slot("stage_r", [P, T2], F32, "resp%d" % ((last - 1) % RESP_SLOTS)))
-        chunks = T2 // BANK
-        for c in range(chunks):
-            cols = slice(BANK * c, BANK * (c + 1))
-            part = woven[c // 2][:, (c % 2) * BANK * PACK : (c % 2 + 1) * BANK * PACK]
-            weigh(nc.vector, last, cols)
-            weave(nc.vector.tensor_copy, 1, part, cols)
-            quantize_z(1, part, cols)
+        woven = slot("woven_1", [P, T2 * PACK], BF16, "planes0")
+        stage = [slot("stage%d" % n, [P, T2], F32, tag) for n, tag in enumerate(("page0", "page2", "resp0", "resp2"))]
+        edges = [0, 256, 768, 1280, 1792, 2048]
+        spans = [slice(lo, hi) for lo, hi in zip(edges, edges[1:])]
+
+        def part(c):
+            return woven[:, PACK * spans[c].start : PACK * spans[c].stop]
+
+        def accumulate(c, b):
+            lo, hi = spans[c].start, spans[c].stop
             for n in range(N // P):
-                bank = banks[4 * ((c + 1) % 2) + n]
-                for b in range(2):
-                    w0 = N * b + P * n
-                    z0 = T2 * b + BANK * c
-                    nc.tensor.matmul_mx(out=bank[:], lhsT=w3_codes[:, w0 : w0 + P].bitcast(FP8X4),
-                                        lhsT_scale=w3_sc[:, w0 : w0 + P],
-                                        rhs=z_codes[:, z0 : z0 + BANK].bitcast(FP8X4), rhs_scale=z_sc[:, z0 : z0 + BANK],
-                                        start=(b == 0), stop=(b == 1))
-                j = 4 * c + n
-                if j < 2 * FEAT_SLOTS:
-                    res = stage[j // 2][:, BANK * (j % 2) : BANK * (j % 2 + 1)]
+                w0 = N * b + P * n
+                z0 = T2 * b
+                nc.tensor.matmul_mx(out=banks[4 * ((c + 1) % 2) + n][:, 0 : hi - lo],
+                                    lhsT=w3_codes[:, w0 : w0 + P].bitcast(FP8X4), lhsT_scale=w3_sc[:, w0 : w0 + P],
+                                    rhs=z_codes[:, z0 + lo : z0 + hi].bitcast(FP8X4), rhs_scale=z_sc[:, z0 + lo : z0 + hi],
+                                    start=(b == 0), stop=(b == 1))
+
+        def finish(c):
+            quantize_z(1, part(c), spans[c])
+            accumulate(c, 1)
+            for n in range(N // P):
+                acc = banks[4 * ((c + 1) % 2) + n][:, 0 : spans[c].stop - spans[c].start]
+                res = stage[n][:, spans[c]]
+                if c >= len(spans) - 2 and n % 2 == 1:
+                    nc.vector.tensor_copy(res, acc)
                 else:
-                    res = stage[FEAT_SLOTS][:, BANK * (j - 2 * FEAT_SLOTS) : BANK * (j - 2 * FEAT_SLOTS + 1)]
-                if c == chunks - 1 and n % 2 == 1:
-                    nc.vector.tensor_copy(res, bank[:])
-                else:
-                    nc.scalar.copy(res, bank[:])
-                nc.sync.dma_start(out[P * n : P * (n + 1), cols], res)
+                    nc.scalar.copy(res, acc)
+                nc.sync.dma_start(out[P * n : P * (n + 1), spans[c]], res)
+            if c + 2 < len(spans):
+                accumulate(c + 2, 0)
+
+        accumulate(0, 0)
+        accumulate(1, 0)
+        weigh(nc.vector, last, spans[0])
+        weigh(nc.vector, last, spans[1])
+        weave(nc.vector.tensor_copy, 1, part(0), spans[0])
+        weave(nc.scalar.copy, 1, part(1), spans[1])
+        weigh(nc.vector, last, spans[2])
+        finish(0)
+        for c in range(2, len(spans)):
+            weave(nc.vector.tensor_copy, 1, part(c), spans[c])
+            if c + 1 < len(spans):
+                weigh(nc.vector, last, spans[c + 1])
+            finish(c - 1)
+        finish(len(spans) - 1)

@@ -53,13 +53,15 @@ def tile_list_shower_deposit_weave_kernel(
 
         tab2_sc = slot("tab2_sc", [P, T], U8)
         tab_sc = slot("tab_sc", [P, T], U8)
-        w1_sc_raw = slot("w1_sc_raw", [P, 2 * H], U8)
+        w1_sc_raw = slot("w1_sc_raw", [P, H], U8)
+        w1_sc_b = slot("w1_sc_b", [P, H], U8)
         v1_sc_b = slot("v1_sc_b", [P, S], U8)
         w3_sc = slot("w3_sc", [P, 2 * N], U8)
         zero(nc.gpsimd, tab2_sc[:])
         zero(nc.gpsimd, tab_sc[:])
         zero(nc.vector, w1_sc_raw[:])
         zero(nc.vector, v1_sc_b[:])
+        zero(nc.vector, w1_sc_b[:])
         zero(nc.vector, w3_sc[:])
 
         idx2 = load_list("idx2", offs2)
@@ -99,49 +101,52 @@ def tile_list_shower_deposit_weave_kernel(
         for q in range(4):
             nc.sync.dma_start(tab_sc[QUAD * q : QUAD * q + 8, :].bitcast(I32),
                               tab_scales[:, 4 * q : 4 * q + 4, :].bitcast(I32))
-        tab_w = [load_words("tab_w0", tab_words[0], "planes0")]
-        w2_raw.append(load_w2(1))
-        tab_w.append(load_words("tab_w1", tab_words[1], "planes1"))
         w1_raw = slot("w1_raw", [P, 2 * 2 * H], U8)
         nc.sync.dma_start(w1_raw[:].bitcast(I32).rearrange("p (a n) -> p a n", a=2),
                           w1_words.rearrange("a p n -> p a n").bitcast(I32))
+        for q in range(4):
+            nc.sync.dma_start(w1_sc_raw[QUAD * q : QUAD * q + 8, :].bitcast(I32),
+                              w1_scales[:, 4 * q : 4 * q + 4, :].bitcast(I32))
+        w2_raw.append(load_w2(1))
         idx4 = load_list("idx4", offs4)
         wg = {("had", 0): load_wg("wg2", wg2, 0)}
-        for q in range(4):
-            nc.sync.dma_start(w1_sc_raw[QUAD * q : QUAD * q + 4, :].bitcast(I32).rearrange("r (a n) -> r a n", a=2),
-                              w1_scales[:, 4 * q : 4 * q + 4, :].rearrange("a r n -> r a n").bitcast(I32))
+        tab_w = [load_words("tab_w%d" % a, tab_words[a], "page%d" % (1 - a)) for a in range(2)]
         idx3 = load_list("idx3", offs3)
 
-        def gather(name, window, lst, dtype):
-            picked = slot(name, [P, S], dtype)
+        def gather(name, window, lst, dtype, tag=None):
+            picked = slot(name, [P, S], dtype, tag)
             nc.vector.tensor_copy(picked[:], window.indirect(lst[:]))
             return picked
 
-        v2_sc = gather("v2_sc", tab2_sc[:], idx2, U8)
-        v1_sc_a = gather("v1_sc_a", tab_sc[:], idx1, U8)
         v2_w = gather("v2_w", tab2_w[:].bitcast(U32), idx2, U32)
+        v2_sc = gather("v2_sc", tab2_sc[:], idx2, U8, "tab2_w")
+        v1_sc_a = gather("v1_sc_a", tab_sc[:], idx1, U8, "tab2_sc")
 
         w2_codes = slot("w2_codes", [P, H], U32)
         w2_sc = slot("w2_sc", [P, H], U8)
 
         def quantize_w2(b):
-            grouped = slot("w2_bf%d" % b, [P, K_PASS * PACK], BF16, "v1_w0" if b == 0 else "woven1")
+            grouped = slot("w2_bf%d" % b, [P, K_PASS * PACK], BF16, "v1_w%d" % (1 - b))
             nc.scalar.copy(grouped[:].rearrange("p (t m j) -> p m t j", t=PACK, j=PACK),
                            w2_raw[b][:].rearrange("p j (m t) -> p m t j", t=PACK))
             cols = slice(K_PASS * b, K_PASS * (b + 1))
             nc.vector.quantize_mx(out=w2_codes[:, cols].bitcast(FP8X4), scales=w2_sc[:, cols], in_=grouped[:])
 
         quantize_w2(0)
-        v1_w = [gather("v1_w%d" % a, tab_w[a][:].bitcast(U32), idx1, U32) for a in range(2)]
         w1_codes = slot("w1_codes", [P, 2 * 2 * H], U8)
         nc.vector.tensor_copy(w1_codes[:].bitcast(U16).rearrange("p (g t m) -> p g t m", g=4, t=PACK),
                               w1_raw[:].bitcast(U16).rearrange("p (g m t) -> p g t m", g=4, t=PACK))
-        w1_sc = slot("w1_sc", [P, 2 * H], U8)
-        nc.vector.tensor_copy(w1_sc[:].rearrange("p (g t m) -> p g t m", g=4, t=PACK),
-                              w1_sc_raw[:].rearrange("p (g m t) -> p g t m", g=4, t=PACK))
+        w1_sc_a = slot("w1_sc_a", [P, H], U8)
+        nc.vector.tensor_copy(w1_sc_a[:].rearrange("p (g t m) -> p g t m", g=2, t=PACK),
+                              w1_sc_raw[:].rearrange("p (g m t) -> p g t m", g=2, t=PACK))
+        w1_sc = [w1_sc_a, w1_sc_b]
         v1_sc = [v1_sc_a, v1_sc_b]
 
         quantize_w2(1)
+        v1_w = [gather("v1_w%d" % a, tab_w[a][:].bitcast(U32), idx1, U32) for a in range(2)]
+        for q in range(4):
+            nc.sync.dma_start(w1_sc_b[QUAD * q : QUAD * q + 4, :].bitcast(I32),
+                              w1_sc_a[QUAD * q + 4 : QUAD * q + 8, :].bitcast(I32))
         for q in range(4):
             nc.sync.dma_start(v1_sc_b[QUAD * q : QUAD * q + 4, :].bitcast(I32),
                               v1_sc_a[QUAD * q + 4 : QUAD * q + 8, :].bitcast(I32))
@@ -188,7 +193,7 @@ def tile_list_shower_deposit_weave_kernel(
                     for a in range(2):
                         c0 = H * a + m0
                         nc.tensor.matmul_mx(out=bank[:], lhsT=w1_codes[:, 2 * c0 : 2 * (c0 + P)].bitcast(FP4X4),
-                                            lhsT_scale=w1_sc[:, c0 : c0 + P],
+                                            lhsT_scale=w1_sc[a][:, m0 : m0 + P],
                                             rhs=v1_w[a][:, cols].bitcast(FP8X4), rhs_scale=v1_sc[a][:, cols],
                                             start=(a == 0), stop=(a == 1))
                     nc.scalar.activation(raw[:, cols], bank[:], ACT.Relu)
@@ -198,7 +203,8 @@ def tile_list_shower_deposit_weave_kernel(
 
         pages = {}
         planes = {}
-        z_codes = slot("z_codes", [P, 2 * T2], U32)
+        z_codes = {1: slot("z_codes1", [P, T2], U32)}
+        early = []
         z_sc = slot("z_sc", [P, 2 * T2], U8)
 
         def scatter(u):
@@ -219,7 +225,7 @@ def tile_list_shower_deposit_weave_kernel(
 
         def quantize_z(b, woven, cols):
             at = slice(T2 * b + cols.start, T2 * b + cols.stop)
-            nc.vector.quantize_mx(out=z_codes[:, at].bitcast(FP8X4), scales=z_sc[:, at], in_=woven)
+            nc.vector.quantize_mx(out=z_codes[b][:, cols].bitcast(FP8X4), scales=z_sc[:, at], in_=woven)
 
         for u in range(AHEAD):
             produce(u)
@@ -241,11 +247,11 @@ def tile_list_shower_deposit_weave_kernel(
                         cols = slice(HALF * h, HALF * (h + 1))
                         woven = slot("woven_0_%d" % h, [P, HALF * PACK], BF16, "woven%d" % h)
                         weave(nc.scalar.copy, 0, woven[:], cols)
-                        quantize_z(0, woven[:], cols)
+                        early.append((woven, cols))
 
         last = PAGES - 1
         woven = slot("woven_1", [P, T2 * PACK], BF16, "planes0")
-        stage = [slot("stage%d" % n, [P, T2], F32, tag) for n, tag in enumerate(("page0", "page2", "resp0", "resp2"))]
+        stage = [slot("stage%d" % n, [P, T2], F32, tag) for n, tag in enumerate(("page0", "page2", "tab2_w", "resp2"))]
         edges = [0, 256, 768, 1280, 1792, 2048]
         spans = [slice(lo, hi) for lo, hi in zip(edges, edges[1:])]
 
@@ -259,7 +265,7 @@ def tile_list_shower_deposit_weave_kernel(
                 z0 = T2 * b
                 nc.tensor.matmul_mx(out=banks[4 * ((c + 1) % 2) + n][:, 0 : hi - lo],
                                     lhsT=w3_codes[:, w0 : w0 + P].bitcast(FP8X4), lhsT_scale=w3_sc[:, w0 : w0 + P],
-                                    rhs=z_codes[:, z0 + lo : z0 + hi].bitcast(FP8X4), rhs_scale=z_sc[:, z0 + lo : z0 + hi],
+                                    rhs=z_codes[b][:, lo:hi].bitcast(FP8X4), rhs_scale=z_sc[:, z0 + lo : z0 + hi],
                                     start=(b == 0), stop=(b == 1))
 
         def finish(c):
@@ -276,13 +282,16 @@ def tile_list_shower_deposit_weave_kernel(
             if c + 2 < len(spans):
                 accumulate(c + 2, 0)
 
-        accumulate(0, 0)
-        accumulate(1, 0)
+        z_codes[0] = slot("z_codes0", [P, T2], U32, "resp%d" % ((last - 1) % RESP_SLOTS))
         weigh(nc.vector, last, spans[0])
         weigh(nc.vector, last, spans[1])
         weave(nc.vector.tensor_copy, 1, part(0), spans[0])
         weave(nc.scalar.copy, 1, part(1), spans[1])
+        quantize_z(0, early[0][0][:], early[0][1])
+        accumulate(0, 0)
+        accumulate(1, 0)
         weigh(nc.vector, last, spans[2])
+        quantize_z(0, early[1][0][:], early[1][1])
         finish(0)
         for c in range(2, len(spans)):
             weave(nc.vector.tensor_copy, 1, part(c), spans[c])

@@ -21,12 +21,17 @@ PACK = 4
 K_PASS = P * PACK
 BANK = 512
 QUAD = 32
+QUADS = P // QUAD
+ROWS = 4
+PASSES = 2
 PAGES = H // P
+HALF = T2 // 2
+
 PAGE_SLOTS = 3
 RESP_SLOTS = 3
 FEAT_SLOTS = 6
 AHEAD = 4
-HALF = T2 // 2
+EDGES = [0, 256, 768, 1280, 1792, 2048]
 
 
 def tile_list_shower_deposit_weave_kernel(
@@ -46,8 +51,8 @@ def tile_list_shower_deposit_weave_kernel(
             nc.sync.dma_start(lst[:], src)
             return lst
 
-        def zero(engine, plane):
-            engine.memset(plane.bitcast(I32), 0)
+        def quad_rows(tile, q, first, count):
+            return tile[QUAD * q + first : QUAD * q + first + count, :].bitcast(I32)
 
         banks = [ps.tile([P, BANK], F32, name="bank%d" % j, tag="bank%d" % j) for j in range(8)]
 
@@ -56,61 +61,60 @@ def tile_list_shower_deposit_weave_kernel(
         w1_sc_raw = slot("w1_sc_raw", [P, H], U8)
         w1_sc_b = slot("w1_sc_b", [P, H], U8)
         v1_sc_b = slot("v1_sc_b", [P, S], U8)
-        w3_sc = slot("w3_sc", [P, 2 * N], U8)
-        zero(nc.gpsimd, tab2_sc[:])
-        zero(nc.gpsimd, tab_sc[:])
-        zero(nc.vector, w1_sc_raw[:])
-        zero(nc.vector, v1_sc_b[:])
-        zero(nc.vector, w1_sc_b[:])
-        zero(nc.vector, w3_sc[:])
-
-        idx2 = load_list("idx2", offs2)
-        for q in range(4):
-            nc.sync.dma_start(tab2_sc[QUAD * q : QUAD * q + 4, :].bitcast(I32),
-                              tab2_scales[0, 4 * q : 4 * q + 4, :].bitcast(I32))
+        w3_sc = slot("w3_sc", [P, PASSES * N], U8)
+        for tile in (tab2_sc, tab_sc):
+            nc.gpsimd.memset(tile[:].bitcast(I32), 0)
+        for tile in (w1_sc_raw, v1_sc_b, w1_sc_b, w3_sc):
+            nc.vector.memset(tile[:].bitcast(I32), 0)
 
         def load_words(name, src, tag=None):
             words = slot(name, [P, T], I32, tag)
             nc.sync.dma_start(words[:], src.rearrange("p n i -> p (n i)").bitcast(I32))
             return words
 
+        def load_two_pass_scales(tile, src):
+            for q in range(QUADS):
+                nc.sync.dma_start(quad_rows(tile, q, 0, PASSES * ROWS),
+                                  src[:, ROWS * q : ROWS * (q + 1), :].bitcast(I32))
+
         def load_w2(b):
             raw = slot("w2_raw%d" % b, [P, PACK, K_PASS], F32, "resp%d" % (1 - b))
             nc.sync.dma_start(raw[:], w2[:, K_PASS * b : K_PASS * (b + 1)].rearrange("(p j) c -> p j c", j=PACK))
             return raw
 
-        def load_wg(name, src, t):
-            wg = slot("%s_%d" % (name, t), [P, S], F32)
+        def load_gain(name, src, t):
+            gain = slot("%s_%d" % (name, t), [P, S], F32)
             rows = src.rearrange("(m t) j -> m t j", t=PACK)[:, t, :]
-            for q in range(4):
-                nc.sync.dma_start(wg[QUAD * q : QUAD * (q + 1), :], rows)
-            return wg
+            for q in range(QUADS):
+                nc.sync.dma_start(gain[QUAD * q : QUAD * (q + 1), :], rows)
+            return gain
 
-        def load_resp(i):
+        def load_squared_resp(i):
             b, t = divmod(i, PACK)
-            r = slot("resp_%d" % i, [P, T2], F32, "resp%d" % (i % RESP_SLOTS))
-            nc.sync.dma_start(r[:], resp[K_PASS * b : K_PASS * (b + 1), :].rearrange("(p t) n -> p t n", t=PACK)[:, t, :])
+            tile = slot("resp_%d" % i, [P, T2], F32, "resp%d" % (i % RESP_SLOTS))
+            rows = resp[K_PASS * b : K_PASS * (b + 1), :].rearrange("(p t) n -> p t n", t=PACK)[:, t, :]
+            nc.sync.dma_start(tile[:], rows)
             for h in range(2):
                 cols = slice(HALF * h, HALF * (h + 1))
-                nc.scalar.activation(r[:, cols], r[:, cols], ACT.Square)
-            return r
+                nc.scalar.activation(tile[:, cols], tile[:, cols], ACT.Square)
+            return tile
 
+        idx2 = load_list("idx2", offs2)
+        for q in range(QUADS):
+            nc.sync.dma_start(quad_rows(tab2_sc, q, 0, ROWS), tab2_scales[0, ROWS * q : ROWS * (q + 1), :].bitcast(I32))
         tab2_w = load_words("tab2_w", tab2_words[0])
         idx1 = load_list("idx1", offs)
         w2_raw = [load_w2(0)]
-        for q in range(4):
-            nc.sync.dma_start(tab_sc[QUAD * q : QUAD * q + 8, :].bitcast(I32),
-                              tab_scales[:, 4 * q : 4 * q + 4, :].bitcast(I32))
-        w1_raw = slot("w1_raw", [P, 2 * 2 * H], U8)
-        nc.sync.dma_start(w1_raw[:].bitcast(I32).rearrange("p (a n) -> p a n", a=2),
+        load_two_pass_scales(tab_sc, tab_scales)
+        w1_raw = slot("w1_raw", [P, PASSES * 2 * H], U8)
+        nc.sync.dma_start(w1_raw[:].bitcast(I32).rearrange("p (a n) -> p a n", a=PASSES),
                           w1_words.rearrange("a p n -> p a n").bitcast(I32))
-        for q in range(4):
-            nc.sync.dma_start(w1_sc_raw[QUAD * q : QUAD * q + 8, :].bitcast(I32),
-                              w1_scales[:, 4 * q : 4 * q + 4, :].bitcast(I32))
+        load_two_pass_scales(w1_sc_raw, w1_scales)
         w2_raw.append(load_w2(1))
+        tab_w = [load_words("tab_w0", tab_words[0], "page1")]
         idx4 = load_list("idx4", offs4)
-        wg = {("had", 0): load_wg("wg2", wg2, 0)}
-        tab_w = [load_words("tab_w%d" % a, tab_words[a], "page%d" % (1 - a)) for a in range(2)]
+        gains = {("had", 0): load_gain("wg2", wg2, 0)}
+        tab_w.append(load_words("tab_w1", tab_words[1], "page0"))
         idx3 = load_list("idx3", offs3)
 
         def gather(name, window, lst, dtype, tag=None):
@@ -132,35 +136,36 @@ def tile_list_shower_deposit_weave_kernel(
             cols = slice(K_PASS * b, K_PASS * (b + 1))
             nc.vector.quantize_mx(out=w2_codes[:, cols].bitcast(FP8X4), scales=w2_sc[:, cols], in_=grouped[:])
 
+        def reorder_columns(dst, src):
+            nc.vector.tensor_copy(dst.rearrange("p (g t m) -> p g t m", t=PACK, m=P),
+                                  src.rearrange("p (g m t) -> p g t m", t=PACK, m=P))
+
+        def second_pass_scales(dst, src):
+            for q in range(QUADS):
+                nc.sync.dma_start(quad_rows(dst, q, 0, ROWS), quad_rows(src, q, ROWS, ROWS))
+
         quantize_w2(0)
-        w1_codes = slot("w1_codes", [P, 2 * 2 * H], U8)
-        nc.vector.tensor_copy(w1_codes[:].bitcast(U16).rearrange("p (g t m) -> p g t m", g=4, t=PACK),
-                              w1_raw[:].bitcast(U16).rearrange("p (g m t) -> p g t m", g=4, t=PACK))
-        w1_sc_a = slot("w1_sc_a", [P, H], U8)
-        nc.vector.tensor_copy(w1_sc_a[:].rearrange("p (g t m) -> p g t m", g=2, t=PACK),
-                              w1_sc_raw[:].rearrange("p (g m t) -> p g t m", g=2, t=PACK))
+        w1_sc_a = slot("w1_sc_a", [P, H], U8, "tab_sc")
+        reorder_columns(w1_sc_a[:], w1_sc_raw[:])
+        w1_codes = slot("w1_codes", [P, PASSES * 2 * H], U8, "w1_sc_raw")
+        reorder_columns(w1_codes[:].bitcast(U16), w1_raw[:].bitcast(U16))
+        quantize_w2(1)
+        v1_w = [gather("v1_w%d" % a, tab_w[a][:].bitcast(U32), idx1, U32) for a in range(PASSES)]
+        second_pass_scales(w1_sc_b, w1_sc_a)
+        second_pass_scales(v1_sc_b, v1_sc_a)
         w1_sc = [w1_sc_a, w1_sc_b]
         v1_sc = [v1_sc_a, v1_sc_b]
 
-        quantize_w2(1)
-        v1_w = [gather("v1_w%d" % a, tab_w[a][:].bitcast(U32), idx1, U32) for a in range(2)]
-        for q in range(4):
-            nc.sync.dma_start(w1_sc_b[QUAD * q : QUAD * q + 4, :].bitcast(I32),
-                              w1_sc_a[QUAD * q + 4 : QUAD * q + 8, :].bitcast(I32))
-        for q in range(4):
-            nc.sync.dma_start(v1_sc_b[QUAD * q : QUAD * q + 4, :].bitcast(I32),
-                              v1_sc_a[QUAD * q + 4 : QUAD * q + 8, :].bitcast(I32))
         for t in range(1, PACK):
-            wg[("had", t)] = load_wg("wg2", wg2, t)
-            wg[("pho", t - 1)] = load_wg("wg1", wg1, t - 1)
-        wg[("pho", PACK - 1)] = load_wg("wg1", wg1, PACK - 1)
-        resp2 = {}
-        w3_codes = slot("w3_codes", [P, 2 * N], I32)
-        nc.sync.dma_start(w3_codes[:].rearrange("p (a n) -> p a n", a=2),
+            gains[("had", t)] = load_gain("wg2", wg2, t)
+            gains[("pho", t - 1)] = load_gain("wg1", wg1, t - 1)
+        gains[("pho", PACK - 1)] = load_gain("wg1", wg1, PACK - 1)
+        w3_codes = slot("w3_codes", [P, PASSES * N], I32)
+        nc.sync.dma_start(w3_codes[:].rearrange("p (a n) -> p a n", a=PASSES),
                           w3_words.rearrange("a p n i -> p a (n i)").bitcast(I32))
-        for q in range(4):
-            nc.sync.dma_start(w3_sc[QUAD * q : QUAD * q + 4, :].bitcast(I32).rearrange("r (a n) -> r a n", a=2),
-                              w3_scales[:, 4 * q : 4 * q + 4, :].rearrange("a r n -> r a n").bitcast(I32))
+        for q in range(QUADS):
+            nc.sync.dma_start(quad_rows(w3_sc, q, 0, ROWS).rearrange("r (a n) -> r a n", a=PASSES),
+                              w3_scales[:, ROWS * q : ROWS * (q + 1), :].rearrange("a r n -> r a n").bitcast(I32))
 
         units = [("had", 0)]
         for i in range(1, PAGES):
@@ -172,7 +177,6 @@ def tile_list_shower_deposit_weave_kernel(
 
         def produce(u):
             stream, i = units[u]
-            t = i % PACK
             m0 = P * i
             feat = slot("feat_%d" % u, [P, S], F32, "feat%d" % (u % FEAT_SLOTS))
             host, half = divmod(u - 3, 2)
@@ -190,94 +194,93 @@ def tile_list_shower_deposit_weave_kernel(
                     nc.scalar.activation(raw[:, cols], bank[:], ACT.Square)
                 else:
                     bank = banks[2 + c]
-                    for a in range(2):
+                    for a in range(PASSES):
                         c0 = H * a + m0
                         nc.tensor.matmul_mx(out=bank[:], lhsT=w1_codes[:, 2 * c0 : 2 * (c0 + P)].bitcast(FP4X4),
                                             lhsT_scale=w1_sc[a][:, m0 : m0 + P],
                                             rhs=v1_w[a][:, cols].bitcast(FP8X4), rhs_scale=v1_sc[a][:, cols],
-                                            start=(a == 0), stop=(a == 1))
+                                            start=(a == 0), stop=(a == PASSES - 1))
                     nc.scalar.activation(raw[:, cols], bank[:], ACT.Relu)
-            gain = wg[(stream, t)][:]
-            nc.gpsimd.tensor_tensor(feat[:], raw, gain, MULT)
-            feats[u] = (feat, gain)
+            nc.gpsimd.tensor_tensor(feat[:], raw, gains[(stream, i % PACK)][:], MULT)
+            feats[u] = feat
 
         pages = {}
+        resp2 = {}
         planes = {}
         z_codes = {1: slot("z_codes1", [P, T2], U32)}
-        early = []
-        z_sc = slot("z_sc", [P, 2 * T2], U8)
+        z_sc = slot("z_sc", [P, PASSES * T2], U8)
 
         def scatter(u):
             stream, i = units[u]
             if stream == "had":
                 pages[i] = slot("page_%d" % i, [P, T2], F32, "page%d" % (i % PAGE_SLOTS))
             lst = idx4 if stream == "had" else idx3
-            feat, gain = feats[u]
-            nc.vector.tensor_copy(pages[i][:].indirect(lst[:]), feat[:])
+            nc.vector.tensor_copy(pages[i][:].indirect(lst[:]), feats[u][:])
 
         def weigh(engine, i, cols):
             b, t = divmod(i, PACK)
             engine.tensor_tensor(planes[b][:, t, cols], pages[i][:, cols], resp2[i][:, cols], MULT)
 
-        def weave(copy, b, woven, cols):
-            copy(woven.rearrange("p (c i t) -> p c t i", t=PACK, i=4),
+        def weave(copy, b, dst, cols):
+            copy(dst.rearrange("p (c i t) -> p c t i", t=PACK, i=4),
                  planes[b][:, :, cols].rearrange("p t (c i) -> p c t i", i=4))
 
-        def quantize_z(b, woven, cols):
+        def quantize_z(b, src, cols):
             at = slice(T2 * b + cols.start, T2 * b + cols.stop)
-            nc.vector.quantize_mx(out=z_codes[b][:, cols].bitcast(FP8X4), scales=z_sc[:, at], in_=woven)
+            nc.vector.quantize_mx(out=z_codes[b][:, cols].bitcast(FP8X4), scales=z_sc[:, at], in_=src)
 
+        last = PAGES - 1
+        halves = [slice(HALF * h, HALF * (h + 1)) for h in range(2)]
+        woven_first = []
         for u in range(AHEAD):
             produce(u)
         for u in range(len(units)):
             if u + AHEAD < len(units):
                 produce(u + AHEAD)
             if u % 2 == 0:
-                resp2[u // 2] = load_resp(u // 2)
+                resp2[u // 2] = load_squared_resp(u // 2)
             scatter(u)
             stream, i = units[u]
-            if stream == "pho" and i < PAGES - 1:
+            if stream == "pho" and i < last:
                 b, t = divmod(i, PACK)
                 if t == 0:
                     planes[b] = slot("planes_%d" % b, [P, PACK, T2], BF16, "planes%d" % b)
-                for h in range(2):
-                    weigh(nc.gpsimd, i, slice(HALF * h, HALF * (h + 1)))
-                if i == PACK - 1:
-                    for h in range(2):
-                        cols = slice(HALF * h, HALF * (h + 1))
-                        woven = slot("woven_0_%d" % h, [P, HALF * PACK], BF16, "woven%d" % h)
-                        weave(nc.scalar.copy, 0, woven[:], cols)
-                        early.append((woven, cols))
+                for cols in halves:
+                    weigh(nc.gpsimd, i, cols)
+                if t == PACK - 1:
+                    for h, cols in enumerate(halves):
+                        woven_first.append(slot("woven_0_%d" % h, [P, HALF * PACK], BF16, "woven%d" % h))
+                        weave(nc.scalar.copy, b, woven_first[h][:], cols)
 
-        last = PAGES - 1
-        woven = slot("woven_1", [P, T2 * PACK], BF16, "planes0")
+        woven_last = slot("woven_1", [P, T2 * PACK], BF16, "planes0")
         stage = [slot("stage%d" % n, [P, T2], F32, tag) for n, tag in enumerate(("page0", "page2", "tab2_w", "resp2"))]
-        edges = [0, 256, 768, 1280, 1792, 2048]
-        spans = [slice(lo, hi) for lo, hi in zip(edges, edges[1:])]
+        spans = [slice(lo, hi) for lo, hi in zip(EDGES, EDGES[1:])]
 
         def part(c):
-            return woven[:, PACK * spans[c].start : PACK * spans[c].stop]
+            return woven_last[:, PACK * spans[c].start : PACK * spans[c].stop]
+
+        def sums(c, n):
+            return banks[4 * ((c + 1) % 2) + n][:, 0 : spans[c].stop - spans[c].start]
 
         def accumulate(c, b):
             lo, hi = spans[c].start, spans[c].stop
             for n in range(N // P):
                 w0 = N * b + P * n
-                z0 = T2 * b
-                nc.tensor.matmul_mx(out=banks[4 * ((c + 1) % 2) + n][:, 0 : hi - lo],
+                nc.tensor.matmul_mx(out=sums(c, n),
                                     lhsT=w3_codes[:, w0 : w0 + P].bitcast(FP8X4), lhsT_scale=w3_sc[:, w0 : w0 + P],
-                                    rhs=z_codes[b][:, lo:hi].bitcast(FP8X4), rhs_scale=z_sc[:, z0 + lo : z0 + hi],
-                                    start=(b == 0), stop=(b == 1))
+                                    rhs=z_codes[b][:, lo:hi].bitcast(FP8X4),
+                                    rhs_scale=z_sc[:, T2 * b + lo : T2 * b + hi],
+                                    start=(b == 0), stop=(b == PASSES - 1))
 
         def finish(c):
             quantize_z(1, part(c), spans[c])
             accumulate(c, 1)
             for n in range(N // P):
-                acc = banks[4 * ((c + 1) % 2) + n][:, 0 : spans[c].stop - spans[c].start]
                 res = stage[n][:, spans[c]]
                 if c >= len(spans) - 2 and n % 2 == 1:
-                    nc.vector.tensor_copy(res, acc)
+                    nc.vector.tensor_copy(res, sums(c, n))
                 else:
-                    nc.scalar.copy(res, acc)
+                    nc.scalar.copy(res, sums(c, n))
                 nc.sync.dma_start(out[P * n : P * (n + 1), spans[c]], res)
             if c + 2 < len(spans):
                 accumulate(c + 2, 0)
@@ -287,11 +290,11 @@ def tile_list_shower_deposit_weave_kernel(
         weigh(nc.vector, last, spans[1])
         weave(nc.vector.tensor_copy, 1, part(0), spans[0])
         weave(nc.scalar.copy, 1, part(1), spans[1])
-        quantize_z(0, early[0][0][:], early[0][1])
+        quantize_z(0, woven_first[0][:], halves[0])
         accumulate(0, 0)
         accumulate(1, 0)
         weigh(nc.vector, last, spans[2])
-        quantize_z(0, early[1][0][:], early[1][1])
+        quantize_z(0, woven_first[1][:], halves[1])
         finish(0)
         for c in range(2, len(spans)):
             weave(nc.vector.tensor_copy, 1, part(c), spans[c])

@@ -20,18 +20,24 @@ P = 128
 PACK = 4
 K_PASS = P * PACK
 BANK = 512
+BANKS = 8
 QUAD = 32
 QUADS = P // QUAD
 ROWS = 4
 PASSES = 2
 PAGES = H // P
 HALF = T2 // 2
+PER_COL = 16
 
-PAGE_SLOTS = 3
+LAG = 2
+PAGE_SLOTS = LAG + 2
 RESP_SLOTS = 3
 FEAT_SLOTS = 6
-AHEAD = 4
-EDGES = [0, 256, 768, 1280, 1792, 2048]
+AHEAD = 2
+CHUNK = 256
+CHUNKS = T2 // CHUNK
+OPEN = BANKS // 2
+LAST_CUT = 768
 
 
 def tile_list_shower_deposit_weave_kernel(
@@ -47,47 +53,53 @@ def tile_list_shower_deposit_weave_kernel(
             return sb.tile(shape, dtype, name=name, tag=tag or name, align_bytes=64)
 
         def load_list(name, src):
-            lst = slot(name, [P, S // 16], U16)
+            lst = slot(name, [P, S // PER_COL], U16)
             nc.sync.dma_start(lst[:], src)
             return lst
 
-        def quad_rows(tile, q, first, count):
-            return tile[QUAD * q + first : QUAD * q + first + count, :].bitcast(I32)
+        def rows_i32(tile, first, count):
+            return tile[first : first + count, :].bitcast(I32)
 
-        banks = [ps.tile([P, BANK], F32, name="bank%d" % j, tag="bank%d" % j) for j in range(8)]
+        banks = [ps.tile([P, BANK], F32, name="bank%d" % j, tag="bank%d" % j) for j in range(BANKS)]
 
         tab2_sc = slot("tab2_sc", [P, T], U8)
         tab_sc = slot("tab_sc", [P, T], U8)
-        w1_sc_raw = slot("w1_sc_raw", [P, H], U8)
-        w1_sc_b = slot("w1_sc_b", [P, H], U8)
-        v1_sc_b = slot("v1_sc_b", [P, S], U8)
+        v1_sc = slot("v1_sc", [P, PASSES * S], U8)
+        w1_sc_raw = slot("w1_sc_raw", [P, PASSES * H], U8, "page1")
         w3_sc = slot("w3_sc", [P, PASSES * N], U8)
-        for tile in (tab2_sc, tab_sc):
-            nc.gpsimd.memset(tile[:].bitcast(I32), 0)
-        for tile in (w1_sc_raw, v1_sc_b, w1_sc_b, w3_sc):
+        nc.gpsimd.memset(tab2_sc[:].bitcast(I32), 0)
+        nc.vector.memset(rows_i32(tab_sc, QUAD, QUAD), 0)
+        nc.vector.memset(rows_i32(tab_sc, 2 * QUAD, 2 * QUAD), 0)
+        for tile in (v1_sc, w1_sc_raw, w3_sc):
             nc.vector.memset(tile[:].bitcast(I32), 0)
 
-        def load_words(name, src, tag=None):
+        def load_words(name, src, tag):
             words = slot(name, [P, T], I32, tag)
             nc.sync.dma_start(words[:], src.rearrange("p n i -> p (n i)").bitcast(I32))
             return words
 
-        def load_two_pass_scales(tile, src):
+        def load_scale_rows(tile, src):
             for q in range(QUADS):
-                nc.sync.dma_start(quad_rows(tile, q, 0, PASSES * ROWS),
-                                  src[:, ROWS * q : ROWS * (q + 1), :].bitcast(I32))
+                nc.sync.dma_start(
+                    rows_i32(tile, QUAD * q, ROWS).rearrange("r (a n) -> r a n", a=src.shape[0]),
+                    src[:, ROWS * q : ROWS * (q + 1), :].rearrange("a r n -> r a n").bitcast(I32))
 
         def load_w2(b):
-            raw = slot("w2_raw%d" % b, [P, PACK, K_PASS], F32, "resp%d" % (1 - b))
+            raw = slot("w2_raw%d" % b, [P, PACK, K_PASS], F32, "resp%d" % (2 - b))
             nc.sync.dma_start(raw[:], w2[:, K_PASS * b : K_PASS * (b + 1)].rearrange("(p j) c -> p j c", j=PACK))
             return raw
 
-        def load_gain(name, src, t):
-            gain = slot("%s_%d" % (name, t), [P, S], F32)
+        gains = {}
+
+        def load_gain(stream, t):
+            gain = slot("gain_%s%d" % (stream, t), [P, S], F32)
+            src = wg2 if stream == "had" else wg1
             rows = src.rearrange("(m t) j -> m t j", t=PACK)[:, t, :]
             for q in range(QUADS):
                 nc.sync.dma_start(gain[QUAD * q : QUAD * (q + 1), :], rows)
-            return gain
+            gains[(stream, t)] = gain
+
+        resp2 = {}
 
         def load_squared_resp(i):
             b, t = divmod(i, PACK)
@@ -97,208 +109,250 @@ def tile_list_shower_deposit_weave_kernel(
             for h in range(2):
                 cols = slice(HALF * h, HALF * (h + 1))
                 nc.scalar.activation(tile[:, cols], tile[:, cols], ACT.Square)
-            return tile
+            resp2[i] = tile
 
         idx2 = load_list("idx2", offs2)
-        for q in range(QUADS):
-            nc.sync.dma_start(quad_rows(tab2_sc, q, 0, ROWS), tab2_scales[0, ROWS * q : ROWS * (q + 1), :].bitcast(I32))
-        tab2_w = load_words("tab2_w", tab2_words[0])
+        load_scale_rows(tab2_sc, tab2_scales)
         idx1 = load_list("idx1", offs)
+        nc.sync.dma_start(rows_i32(tab_sc, 0, QUAD), tab_scales.rearrange("a g n -> g a n").bitcast(I32))
+        tab2_w = load_words("tab2_w", tab2_words[0], "planes1")
         w2_raw = [load_w2(0)]
-        load_two_pass_scales(tab_sc, tab_scales)
+        tab_w = [load_words("tab_w0", tab_words[0], "page2")]
+        idx4 = load_list("idx4", offs4)
+        load_gain("had", 0)
+        tab_w.append(load_words("tab_w1", tab_words[1], "page3"))
+        load_gain("had", 1)
         w1_raw = slot("w1_raw", [P, PASSES * 2 * H], U8)
         nc.sync.dma_start(w1_raw[:].bitcast(I32).rearrange("p (a n) -> p a n", a=PASSES),
                           w1_words.rearrange("a p n -> p a n").bitcast(I32))
-        load_two_pass_scales(w1_sc_raw, w1_scales)
-        w2_raw.append(load_w2(1))
-        tab_w = [load_words("tab_w0", tab_words[0], "page1")]
-        idx4 = load_list("idx4", offs4)
-        gains = {("had", 0): load_gain("wg2", wg2, 0)}
-        tab_w.append(load_words("tab_w1", tab_words[1], "page0"))
+        load_scale_rows(w1_sc_raw, w1_scales)
+        load_gain("had", 2)
         idx3 = load_list("idx3", offs3)
 
-        def gather(name, window, lst, dtype, tag=None):
-            picked = slot(name, [P, S], dtype, tag)
+        def gather(name, window, lst, dtype):
+            picked = slot(name, [P, S], dtype)
             nc.vector.tensor_copy(picked[:], window.indirect(lst[:]))
             return picked
 
-        v2_w = gather("v2_w", tab2_w[:].bitcast(U32), idx2, U32)
-        v2_sc = gather("v2_sc", tab2_sc[:], idx2, U8, "tab2_w")
-        v1_sc_a = gather("v1_sc_a", tab_sc[:], idx1, U8, "tab2_sc")
-
-        w2_codes = slot("w2_codes", [P, H], U32)
+        w2_codes = {}
         w2_sc = slot("w2_sc", [P, H], U8)
+        w2_bf = {}
 
-        def quantize_w2(b):
-            grouped = slot("w2_bf%d" % b, [P, K_PASS * PACK], BF16, "v1_w%d" % (1 - b))
-            nc.scalar.copy(grouped[:].rearrange("p (t m j) -> p m t j", t=PACK, j=PACK),
-                           w2_raw[b][:].rearrange("p j (m t) -> p m t j", t=PACK))
-            cols = slice(K_PASS * b, K_PASS * (b + 1))
-            nc.vector.quantize_mx(out=w2_codes[:, cols].bitcast(FP8X4), scales=w2_sc[:, cols], in_=grouped[:])
+        def round_w2(b, t0, t1, tag=None):
+            grouped = slot("w2_bf%d_%d" % (b, t0), [P, (t1 - t0) * K_PASS], BF16, tag)
+            nc.scalar.copy(grouped[:].rearrange("p (t m j) -> p m t j", m=P, j=PACK),
+                           w2_raw[b][:].rearrange("p j (m t) -> p m t j", t=PACK)[:, :, t0:t1, :])
+            w2_bf[(b, t0)] = grouped
+
+        def quantize_w2(b, t0, t1, tag=None):
+            codes = slot("w2_codes%d_%d" % (b, t0), [P, (t1 - t0) * P], U32, tag)
+            cols = slice(K_PASS * b + P * t0, K_PASS * b + P * t1)
+            nc.vector.quantize_mx(out=codes[:].bitcast(FP8X4), scales=w2_sc[:, cols], in_=w2_bf[(b, t0)][:])
+            for t in range(t0, t1):
+                w2_codes[PACK * b + t] = codes[:, P * (t - t0) : P * (t - t0 + 1)]
 
         def reorder_columns(dst, src):
             nc.vector.tensor_copy(dst.rearrange("p (g t m) -> p g t m", t=PACK, m=P),
                                   src.rearrange("p (g m t) -> p g t m", t=PACK, m=P))
 
-        def second_pass_scales(dst, src):
-            for q in range(QUADS):
-                nc.sync.dma_start(quad_rows(dst, q, 0, ROWS), quad_rows(src, q, ROWS, ROWS))
+        v2_sc = gather("v2_sc", tab2_sc[:], idx2, U8)
+        v1_sc_rows = gather("v1_sc_rows", tab_sc[:], idx1, U8)
+        v2_w = gather("v2_w", tab2_w[:].bitcast(U32), idx2, U32)
+        round_w2(0, 0, 1)
+        round_w2(0, 1, PACK)
+        quantize_w2(0, 0, 1)
+        v1_w = [gather("v1_w0", tab_w[0][:].bitcast(U32), idx1, U32)]
+        quantize_w2(0, 1, PACK)
+        v1_w.append(gather("v1_w1", tab_w[1][:].bitcast(U32), idx1, U32))
+        for q in range(QUADS):
+            nc.sync.dma_start(rows_i32(v1_sc, QUAD * q, ROWS), rows_i32(v1_sc_rows, PASSES * ROWS * q, PASSES * ROWS))
 
-        quantize_w2(0)
-        w1_sc_a = slot("w1_sc_a", [P, H], U8, "tab_sc")
-        reorder_columns(w1_sc_a[:], w1_sc_raw[:])
-        w1_codes = slot("w1_codes", [P, PASSES * 2 * H], U8, "w1_sc_raw")
-        reorder_columns(w1_codes[:].bitcast(U16), w1_raw[:].bitcast(U16))
-        quantize_w2(1)
-        v1_w = [gather("v1_w%d" % a, tab_w[a][:].bitcast(U32), idx1, U32) for a in range(PASSES)]
-        second_pass_scales(w1_sc_b, w1_sc_a)
-        second_pass_scales(v1_sc_b, v1_sc_a)
-        w1_sc = [w1_sc_a, w1_sc_b]
-        v1_sc = [v1_sc_a, v1_sc_b]
-
+        load_gain("pho", 0)
+        load_gain("had", 3)
         for t in range(1, PACK):
-            gains[("had", t)] = load_gain("wg2", wg2, t)
-            gains[("pho", t - 1)] = load_gain("wg1", wg1, t - 1)
-        gains[("pho", PACK - 1)] = load_gain("wg1", wg1, PACK - 1)
+            load_gain("pho", t)
         w3_codes = slot("w3_codes", [P, PASSES * N], I32)
         nc.sync.dma_start(w3_codes[:].rearrange("p (a n) -> p a n", a=PASSES),
                           w3_words.rearrange("a p n i -> p a (n i)").bitcast(I32))
-        for q in range(QUADS):
-            nc.sync.dma_start(quad_rows(w3_sc, q, 0, ROWS).rearrange("r (a n) -> r a n", a=PASSES),
-                              w3_scales[:, ROWS * q : ROWS * (q + 1), :].rearrange("a r n -> r a n").bitcast(I32))
+        load_scale_rows(w3_sc, w3_scales)
 
-        units = [("had", 0)]
-        for i in range(1, PAGES):
-            units += [("had", i), ("pho", i - 1)]
-        units.append(("pho", PAGES - 1))
+        units = [("had", i) for i in range(LAG)]
+        for i in range(LAG, PAGES):
+            units += [("had", i), ("pho", i - LAG)]
+        units += [("pho", i) for i in range(PAGES - LAG, PAGES)]
+        last_unit = len(units) - 1
 
+        w1 = {}
         feats = {}
-        raws = {}
+
+        def pieces(u):
+            if u == last_unit:
+                return [(0, LAST_CUT, "z_codes0"), (LAST_CUT, S, "feat%d" % (u % FEAT_SLOTS))]
+            if u == 0:
+                return [(0, S, "w1_codes")]
+            return [(0, S, "feat%d" % (u % FEAT_SLOTS))]
+
+        planes = {}
+        hosts = {}
+
+        def plane_tile(b):
+            if b not in planes:
+                planes[b] = slot("planes_%d" % b, [P, CHUNKS, PACK, CHUNK], BF16, "planes%d" % b)
+            return planes[b]
+
+        def staged(u, lo, hi):
+            stream, i = units[u]
+            if stream == "had" and i >= 1:
+                if u not in hosts:
+                    hosts[u] = slot("raw_%d" % u, [P, S], F32, "resp%d" % (abs(i - LAG) % RESP_SLOTS))
+                return hosts[u][:, lo:hi].rearrange("p (c n) -> p c n", n=P)
+            stream, i = units[u - AHEAD] if u >= AHEAD else ("had", 0)
+            if stream == "had":
+                return None
+            b, t = divmod(i, PACK)
+            return plane_tile(b)[:, lo // P : hi // P, t, :].bitcast(F32)
 
         def produce(u):
             stream, i = units[u]
             m0 = P * i
-            feat = slot("feat_%d" % u, [P, S], F32, "feat%d" % (u % FEAT_SLOTS))
-            host, half = divmod(u - 3, 2)
-            if host not in raws:
-                raws[host] = slot("raw_%d" % (host + 2), [P, 2 * S], F32, "resp%d" % (host % RESP_SLOTS))
-            raw = raws[host][:, S * half : S * (half + 1)]
+            feats[u] = [(lo, hi, slot("feat_%d_%d" % (u, lo), [P, hi - lo], F32, tag)) for lo, hi, tag in pieces(u)]
             for c in range(S // BANK):
                 cols = slice(BANK * c, BANK * (c + 1))
+                bank = banks[c]
                 if stream == "had":
-                    bank = banks[c]
-                    nc.tensor.matmul_mx(out=bank[:], lhsT=w2_codes[:, m0 : m0 + P].bitcast(FP8X4),
+                    nc.tensor.matmul_mx(out=bank[:], lhsT=w2_codes[i].bitcast(FP8X4),
                                         lhsT_scale=w2_sc[:, m0 : m0 + P],
                                         rhs=v2_w[:, cols].bitcast(FP8X4), rhs_scale=v2_sc[:, cols],
                                         start=True, stop=True)
-                    nc.scalar.activation(raw[:, cols], bank[:], ACT.Square)
                 else:
-                    bank = banks[2 + c]
                     for a in range(PASSES):
                         c0 = H * a + m0
-                        nc.tensor.matmul_mx(out=bank[:], lhsT=w1_codes[:, 2 * c0 : 2 * (c0 + P)].bitcast(FP4X4),
-                                            lhsT_scale=w1_sc[a][:, m0 : m0 + P],
-                                            rhs=v1_w[a][:, cols].bitcast(FP8X4), rhs_scale=v1_sc[a][:, cols],
+                        nc.tensor.matmul_mx(out=bank[:], lhsT=w1["codes"][:, 2 * c0 : 2 * (c0 + P)].bitcast(FP4X4),
+                                            lhsT_scale=w1["sc"][:, c0 : c0 + P],
+                                            rhs=v1_w[a][:, cols].bitcast(FP8X4),
+                                            rhs_scale=v1_sc[:, S * a + cols.start : S * a + cols.stop],
                                             start=(a == 0), stop=(a == PASSES - 1))
-                    nc.scalar.activation(raw[:, cols], bank[:], ACT.Relu)
-            nc.gpsimd.tensor_tensor(feat[:], raw, gains[(stream, i % PACK)][:], MULT)
-            feats[u] = feat
+                func = ACT.Square if stream == "had" else ACT.Relu
+                for lo, hi, feat in feats[u]:
+                    a0, a1 = max(lo, cols.start), min(hi, cols.stop)
+                    if a0 < a1:
+                        raw = staged(u, a0, a1)
+                        if raw is None:
+                            raw = feat[:, a0 - lo : a1 - lo].rearrange("p (c n) -> p c n", n=P)
+                        sums = bank[:, a0 - cols.start : a1 - cols.start]
+                        nc.scalar.activation(raw, sums.rearrange("p (c n) -> p c n", n=P), func)
+            gain = gains[(stream, i % PACK)]
+            for lo, hi, feat in feats[u]:
+                step = BANK if u == 0 else hi - lo
+                for a0 in range(lo, hi, step):
+                    part = feat[:, a0 - lo : a0 - lo + step].rearrange("p (c n) -> p c n", n=P)
+                    raw = staged(u, a0, a0 + step)
+                    nc.gpsimd.tensor_tensor(part, part if raw is None else raw,
+                                            gain[:, a0 : a0 + step].rearrange("p (c n) -> p c n", n=P), MULT)
 
         pages = {}
-        resp2 = {}
-        planes = {}
-        z_codes = {1: slot("z_codes1", [P, T2], U32)}
-        z_sc = slot("z_sc", [P, PASSES * T2], U8)
 
-        def scatter(u):
+        def scatter(u, piece):
             stream, i = units[u]
             if stream == "had":
                 pages[i] = slot("page_%d" % i, [P, T2], F32, "page%d" % (i % PAGE_SLOTS))
             lst = idx4 if stream == "had" else idx3
-            nc.vector.tensor_copy(pages[i][:].indirect(lst[:]), feats[u][:])
+            lo, hi, feat = feats[u][piece]
+            nc.vector.tensor_copy(pages[i][:].indirect(lst[:, lo // PER_COL : hi // PER_COL]), feat[:])
 
-        def weigh(engine, i, cols):
+        def weigh(engine, i, c0, c1):
             b, t = divmod(i, PACK)
-            engine.tensor_tensor(planes[b][:, t, cols], pages[i][:, cols], resp2[i][:, cols], MULT)
+            cols = slice(CHUNK * c0, CHUNK * c1)
+            engine.tensor_tensor(plane_tile(b)[:, c0:c1, t, :],
+                                 pages[i][:, cols].rearrange("p (c n) -> p c n", n=CHUNK),
+                                 resp2[i][:, cols].rearrange("p (c n) -> p c n", n=CHUNK), MULT)
 
-        def weave(copy, b, dst, cols):
-            copy(dst.rearrange("p (c i t) -> p c t i", t=PACK, i=4),
-                 planes[b][:, :, cols].rearrange("p t (c i) -> p c t i", i=4))
+        woven = {}
 
-        def quantize_z(b, src, cols):
-            at = slice(T2 * b + cols.start, T2 * b + cols.stop)
-            nc.vector.quantize_mx(out=z_codes[b][:, cols].bitcast(FP8X4), scales=z_sc[:, at], in_=src)
+        def weave(copy, b, c):
+            dst = woven[b][:, PACK * CHUNK * c : PACK * CHUNK * (c + 1)]
+            copy(dst.rearrange("p (n i t) -> p n t i", t=PACK, i=4),
+                 planes[b][:, c, :, :].rearrange("p t (n i) -> p n t i", i=4))
 
-        last = PAGES - 1
-        halves = [slice(HALF * h, HALF * (h + 1)) for h in range(2)]
-        woven_first = []
+        z_sc = slot("z_sc", [P, PASSES * T2], U8)
+        z_codes = {}
+
+        def quantize_z(b, c0, c1, tag=None):
+            codes = slot("z_codes%d_%d" % (b, c0), [P, CHUNK * (c1 - c0)], U32, tag)
+            nc.vector.quantize_mx(out=codes[:].bitcast(FP8X4),
+                                  scales=z_sc[:, T2 * b + CHUNK * c0 : T2 * b + CHUNK * c1],
+                                  in_=woven[b][:, PACK * CHUNK * c0 : PACK * CHUNK * c1])
+            for c in range(c0, c1):
+                z_codes[(b, c)] = codes[:, CHUNK * (c - c0) : CHUNK * (c - c0 + 1)]
+
         for u in range(AHEAD):
             produce(u)
-        for u in range(len(units)):
-            if u + AHEAD < len(units):
-                produce(u + AHEAD)
-            if u % 2 == 0:
-                resp2[u // 2] = load_squared_resp(u // 2)
-            scatter(u)
+        for u in range(last_unit):
             stream, i = units[u]
-            if stream == "pho" and i < last:
+            if u + AHEAD <= last_unit:
+                produce(u + AHEAD)
+            if stream == "had" and i >= LAG:
+                load_squared_resp(i - LAG)
+            scatter(u, 0)
+            if u == 0:
+                w1["codes"] = slot("w1_codes", [P, PASSES * 2 * H], U8)
+                reorder_columns(w1["codes"][:].bitcast(U16), w1_raw[:].bitcast(U16))
+                w1["sc"] = slot("w1_sc", [P, PASSES * H], U8, "w1_raw")
+                reorder_columns(w1["sc"][:], w1_sc_raw[:])
+            if u == 1:
+                w2_raw.append(load_w2(1))
+                round_w2(1, 0, PACK, "page2")
+                quantize_w2(1, 0, PACK)
+            if stream == "pho":
                 b, t = divmod(i, PACK)
-                if t == 0:
-                    planes[b] = slot("planes_%d" % b, [P, PACK, T2], BF16, "planes%d" % b)
-                for cols in halves:
-                    weigh(nc.gpsimd, i, cols)
+                for h in range(2):
+                    weigh(nc.gpsimd, i, CHUNKS // 2 * h, CHUNKS // 2 * (h + 1))
                 if t == PACK - 1:
-                    for h, cols in enumerate(halves):
-                        woven_first.append(slot("woven_0_%d" % h, [P, HALF * PACK], BF16, "woven%d" % h))
-                        weave(nc.scalar.copy, b, woven_first[h][:], cols)
-
-        woven_last = slot("woven_1", [P, T2 * PACK], BF16, "planes0")
-        stage = [slot("stage%d" % n, [P, T2], F32, tag) for n, tag in enumerate(("page0", "page2", "tab2_w", "resp2"))]
-        spans = [slice(lo, hi) for lo, hi in zip(EDGES, EDGES[1:])]
-
-        def part(c):
-            return woven_last[:, PACK * spans[c].start : PACK * spans[c].stop]
-
-        def sums(c, n):
-            return banks[4 * ((c + 1) % 2) + n][:, 0 : spans[c].stop - spans[c].start]
+                    woven[b] = slot("woven_%d" % b, [P, T2 * PACK], BF16)
+                    for c in range(CHUNKS):
+                        weave(nc.scalar.copy, b, c)
+                if PAGES - LAG <= i + RESP_SLOTS < PAGES:
+                    load_squared_resp(i + RESP_SLOTS)
 
         def accumulate(c, b):
-            lo, hi = spans[c].start, spans[c].stop
             for n in range(N // P):
                 w0 = N * b + P * n
-                nc.tensor.matmul_mx(out=sums(c, n),
+                bank = banks[2 * (c % OPEN) + n // 2]
+                nc.tensor.matmul_mx(out=bank[:, CHUNK * (n % 2) : CHUNK * (n % 2 + 1)],
                                     lhsT=w3_codes[:, w0 : w0 + P].bitcast(FP8X4), lhsT_scale=w3_sc[:, w0 : w0 + P],
-                                    rhs=z_codes[b][:, lo:hi].bitcast(FP8X4),
-                                    rhs_scale=z_sc[:, T2 * b + lo : T2 * b + hi],
-                                    start=(b == 0), stop=(b == PASSES - 1))
+                                    rhs=z_codes[(b, c)].bitcast(FP8X4),
+                                    rhs_scale=z_sc[:, T2 * b + CHUNK * c : T2 * b + CHUNK * (c + 1)],
+                                    start=(b == 0 and n % 2 == 0), stop=(b == PASSES - 1 and n % 2 == 1))
 
         def finish(c):
-            quantize_z(1, part(c), spans[c])
             accumulate(c, 1)
-            for n in range(N // P):
-                res = stage[n][:, spans[c]]
-                if c >= len(spans) - 2 and n % 2 == 1:
-                    nc.vector.tensor_copy(res, sums(c, n))
-                else:
-                    nc.scalar.copy(res, sums(c, n))
-                nc.sync.dma_start(out[P * n : P * (n + 1), spans[c]], res)
-            if c + 2 < len(spans):
-                accumulate(c + 2, 0)
+            stage = slot("stage_%d" % c, [P, 2, BANK], F32, "feat%d" % (c % FEAT_SLOTS))
+            for h in range(2):
+                copy = nc.vector.tensor_copy if c == CHUNKS - 1 and h == 1 else nc.scalar.copy
+                copy(stage[:, h, :], banks[2 * (c % OPEN) + h][:])
+                rows = out[2 * P * h : 2 * P * (h + 1), CHUNK * c : CHUNK * (c + 1)]
+                nc.sync.dma_start(rows.rearrange("(n p) c -> p n c", p=P),
+                                  stage[:, h, :].rearrange("p (n c) -> p n c", c=CHUNK))
 
-        z_codes[0] = slot("z_codes0", [P, T2], U32, "resp%d" % ((last - 1) % RESP_SLOTS))
-        weigh(nc.vector, last, spans[0])
-        weigh(nc.vector, last, spans[1])
-        weave(nc.vector.tensor_copy, 1, part(0), spans[0])
-        weave(nc.scalar.copy, 1, part(1), spans[1])
-        quantize_z(0, woven_first[0][:], halves[0])
-        accumulate(0, 0)
-        accumulate(1, 0)
-        weigh(nc.vector, last, spans[2])
-        quantize_z(0, woven_first[1][:], halves[1])
-        finish(0)
-        for c in range(2, len(spans)):
-            weave(nc.vector.tensor_copy, 1, part(c), spans[c])
-            if c + 1 < len(spans):
-                weigh(nc.vector, last, spans[c + 1])
-            finish(c - 1)
-        finish(len(spans) - 1)
+        last = PAGES - 1
+        scatter(last_unit, 0)
+        quantize_z(0, 0, OPEN, "z_codes0")
+        for c in range(OPEN):
+            accumulate(c, 0)
+        lo, hi, feat = feats[last_unit][1]
+        nc.vector.tensor_copy(pages[last][:].indirect(idx3[:, lo // PER_COL : hi // PER_COL]), feat[:])
+        woven[1] = slot("woven_1", [P, T2 * PACK], BF16, "planes0")
+        weigh(nc.vector, last, 0, 1)
+        weigh(nc.vector, last, 1, 2)
+        weave(nc.vector.tensor_copy, 1, 0)
+        weave(nc.scalar.copy, 1, 1)
+        for c in range(CHUNKS):
+            if c + 2 < CHUNKS:
+                weigh(nc.vector, last, c + 2, c + 3)
+            quantize_z(1, c, c + 1)
+            if c + 2 < CHUNKS:
+                weave(nc.vector.tensor_copy, 1, c + 2)
+            finish(c)
+            if c + OPEN < CHUNKS:
+                quantize_z(0, c + OPEN, c + OPEN + 1)
+                accumulate(c + OPEN, 0)

@@ -65,7 +65,7 @@ def tile_list_shower_deposit_weave_kernel(
         tab2_sc = slot("tab2_sc", [P, T], U8)
         tab_sc = slot("tab_sc", [P, T], U8)
         v1_sc = slot("v1_sc", [P, PASSES * S], U8)
-        w1_sc_raw = slot("w1_sc_raw", [P, PASSES * H], U8, "page1")
+        w1_sc_raw = slot("w1_sc_raw", [P, PASSES * H], U8)
         w3_sc = slot("w3_sc", [P, PASSES * N], U8)
         nc.gpsimd.memset(tab2_sc[:].bitcast(I32), 0)
         nc.vector.memset(rows_i32(tab_sc, QUAD, QUAD), 0)
@@ -136,20 +136,14 @@ def tile_list_shower_deposit_weave_kernel(
 
         w2_codes = {}
         w2_sc = slot("w2_sc", [P, H], U8)
-        w2_bf = {}
 
-        def round_w2(b, t0, t1, tag=None):
-            grouped = slot("w2_bf%d_%d" % (b, t0), [P, (t1 - t0) * K_PASS], BF16, tag)
+        def quantize_w2(b, rounded_tag, codes_tag=None):
+            grouped = slot("w2_bf%d" % b, [P, PACK * K_PASS], BF16, rounded_tag)
             nc.scalar.copy(grouped[:].rearrange("p (t m j) -> p m t j", m=P, j=PACK),
-                           w2_raw[b][:].rearrange("p j (m t) -> p m t j", t=PACK)[:, :, t0:t1, :])
-            w2_bf[(b, t0)] = grouped
-
-        def quantize_w2(b, t0, t1, tag=None):
-            codes = slot("w2_codes%d_%d" % (b, t0), [P, (t1 - t0) * P], U32, tag)
-            cols = slice(K_PASS * b + P * t0, K_PASS * b + P * t1)
-            nc.vector.quantize_mx(out=codes[:].bitcast(FP8X4), scales=w2_sc[:, cols], in_=w2_bf[(b, t0)][:])
-            for t in range(t0, t1):
-                w2_codes[PACK * b + t] = codes[:, P * (t - t0) : P * (t - t0 + 1)]
+                           w2_raw[b][:].rearrange("p j (m t) -> p m t j", t=PACK))
+            w2_codes[b] = slot("w2_codes%d" % b, [P, K_PASS], U32, codes_tag)
+            nc.vector.quantize_mx(out=w2_codes[b][:].bitcast(FP8X4),
+                                  scales=w2_sc[:, K_PASS * b : K_PASS * (b + 1)], in_=grouped[:])
 
         def reorder_columns(dst, src):
             nc.vector.tensor_copy(dst.rearrange("p (g t m) -> p g t m", t=PACK, m=P),
@@ -158,12 +152,8 @@ def tile_list_shower_deposit_weave_kernel(
         v2_sc = gather("v2_sc", tab2_sc[:], idx2, U8)
         v1_sc_rows = gather("v1_sc_rows", tab_sc[:], idx1, U8)
         v2_w = gather("v2_w", tab2_w[:].bitcast(U32), idx2, U32)
-        round_w2(0, 0, 1)
-        round_w2(0, 1, PACK)
-        quantize_w2(0, 0, 1)
-        v1_w = [gather("v1_w0", tab_w[0][:].bitcast(U32), idx1, U32)]
-        quantize_w2(0, 1, PACK)
-        v1_w.append(gather("v1_w1", tab_w[1][:].bitcast(U32), idx1, U32))
+        quantize_w2(0, "v1_w0")
+        v1_w = [gather("v1_w%d" % a, tab_w[a][:].bitcast(U32), idx1, U32) for a in range(PASSES)]
         for q in range(QUADS):
             nc.sync.dma_start(rows_i32(v1_sc, QUAD * q, ROWS), rows_i32(v1_sc_rows, PASSES * ROWS * q, PASSES * ROWS))
 
@@ -177,50 +167,57 @@ def tile_list_shower_deposit_weave_kernel(
         load_scale_rows(w3_sc, w3_scales)
 
         units = [("had", i) for i in range(LAG)]
-        for i in range(LAG, PAGES):
+        last = PAGES - 1
+        for i in range(LAG, last):
             units += [("had", i), ("pho", i - LAG)]
-        units += [("pho", i) for i in range(PAGES - LAG, PAGES)]
+        units += [("pho", i) for i in range(last - LAG, last)] + [("had", last), ("pho", last)]
         last_unit = len(units) - 1
 
         w1 = {}
         feats = {}
 
-        def pieces(u):
-            if u == last_unit:
-                return [(0, LAST_CUT, "z_codes0"), (LAST_CUT, S, "feat%d" % (u % FEAT_SLOTS))]
-            if u == 0:
-                return [(0, S, "w1_codes")]
-            return [(0, S, "feat%d" % (u % FEAT_SLOTS))]
-
         planes = {}
-        hosts = {}
 
-        def plane_tile(b):
-            if b not in planes:
-                planes[b] = slot("planes_%d" % b, [P, CHUNKS, PACK, CHUNK], BF16, "planes%d" % b)
-            return planes[b]
-
-        def staged(u, lo, hi):
-            stream, i = units[u]
-            if stream == "had" and i >= 1:
-                if u not in hosts:
-                    hosts[u] = slot("raw_%d" % u, [P, S], F32, "resp%d" % (abs(i - LAG) % RESP_SLOTS))
-                return hosts[u][:, lo:hi].rearrange("p (c n) -> p c n", n=P)
-            stream, i = units[u - AHEAD] if u >= AHEAD else ("had", 0)
-            if stream == "had":
-                return None
+        def plane(i):
             b, t = divmod(i, PACK)
-            return plane_tile(b)[:, lo // P : hi // P, t, :].bitcast(F32)
+            if b not in planes:
+                planes[b] = slot("planes_%d" % b, [P, PACK // (b + 1), T2], BF16, "planes%d" % b)
+            return planes[b][:, t, :]
+
+        first_hosts = {0: 1, 2: 0, 4: 1, 6: 2}
+
+        def staging(u):
+            if u in first_hosts:
+                return slot("raw_%d" % u, [P, S], F32, "resp%d" % first_hosts[u])[:]
+            if u == last_unit:
+                return slot("raw_%d" % u, [P, S], F32, "feat%d" % (u % FEAT_SLOTS))[:]
+            if u >= AHEAD and units[u - AHEAD][0] == "pho":
+                return plane(units[u - AHEAD][1]).bitcast(F32)
+            return None
+
+        raws = {}
+
+        def apply_gain(u, lo, hi, tag):
+            stream, i = units[u]
+            feat = slot("feat_%d_%d" % (u, lo), [P, hi - lo], F32, tag)
+            nc.gpsimd.tensor_tensor(feat[:], raws[u][:, lo:hi], gains[(stream, i % PACK)][:, lo:hi], MULT)
+            return feat
 
         def produce(u):
             stream, i = units[u]
             m0 = P * i
-            feats[u] = [(lo, hi, slot("feat_%d_%d" % (u, lo), [P, hi - lo], F32, tag)) for lo, hi, tag in pieces(u)]
+            raw = staging(u)
+            tag = "w1_codes" if u == 0 else "feat%d" % (u % FEAT_SLOTS)
+            if u != last_unit:
+                feats[u] = slot("feat_%d" % u, [P, S], F32, tag)
+            if raw is None:
+                raw = feats[u][:]
+            raws[u] = raw
             for c in range(S // BANK):
                 cols = slice(BANK * c, BANK * (c + 1))
                 bank = banks[c]
                 if stream == "had":
-                    nc.tensor.matmul_mx(out=bank[:], lhsT=w2_codes[i].bitcast(FP8X4),
+                    nc.tensor.matmul_mx(out=bank[:], lhsT=w2_codes[i // PACK][:, m0 % K_PASS : m0 % K_PASS + P].bitcast(FP8X4),
                                         lhsT_scale=w2_sc[:, m0 : m0 + P],
                                         rhs=v2_w[:, cols].bitcast(FP8X4), rhs_scale=v2_sc[:, cols],
                                         start=True, stop=True)
@@ -232,87 +229,91 @@ def tile_list_shower_deposit_weave_kernel(
                                             rhs=v1_w[a][:, cols].bitcast(FP8X4),
                                             rhs_scale=v1_sc[:, S * a + cols.start : S * a + cols.stop],
                                             start=(a == 0), stop=(a == PASSES - 1))
-                func = ACT.Square if stream == "had" else ACT.Relu
-                for lo, hi, feat in feats[u]:
-                    a0, a1 = max(lo, cols.start), min(hi, cols.stop)
-                    if a0 < a1:
-                        raw = staged(u, a0, a1)
-                        if raw is None:
-                            raw = feat[:, a0 - lo : a1 - lo].rearrange("p (c n) -> p c n", n=P)
-                        sums = bank[:, a0 - cols.start : a1 - cols.start]
-                        nc.scalar.activation(raw, sums.rearrange("p (c n) -> p c n", n=P), func)
+                nc.scalar.activation(raw[:, cols], bank[:], ACT.Square if stream == "had" else ACT.Relu)
+            if u == last_unit:
+                feats[u] = apply_gain(u, 0, LAST_CUT, "z_codes0")
+                return
             gain = gains[(stream, i % PACK)]
-            for lo, hi, feat in feats[u]:
-                step = BANK if u == 0 else hi - lo
-                for a0 in range(lo, hi, step):
-                    part = feat[:, a0 - lo : a0 - lo + step].rearrange("p (c n) -> p c n", n=P)
-                    raw = staged(u, a0, a0 + step)
-                    nc.gpsimd.tensor_tensor(part, part if raw is None else raw,
-                                            gain[:, a0 : a0 + step].rearrange("p (c n) -> p c n", n=P), MULT)
+            step = BANK if u == 0 else S
+            for lo in range(0, S, step):
+                nc.gpsimd.tensor_tensor(feats[u][:, lo : lo + step], raw[:, lo : lo + step], gain[:, lo : lo + step], MULT)
 
         pages = {}
 
-        def scatter(u, piece):
+        def scatter(u, feat, lo, hi):
             stream, i = units[u]
             if stream == "had":
                 pages[i] = slot("page_%d" % i, [P, T2], F32, "page%d" % (i % PAGE_SLOTS))
             lst = idx4 if stream == "had" else idx3
-            lo, hi, feat = feats[u][piece]
             nc.vector.tensor_copy(pages[i][:].indirect(lst[:, lo // PER_COL : hi // PER_COL]), feat[:])
 
+        pairs = slot("pairs", [P, CHUNKS, 2, 2 * CHUNK], BF16)
+
         def weigh(engine, i, c0, c1):
-            b, t = divmod(i, PACK)
             cols = slice(CHUNK * c0, CHUNK * c1)
-            engine.tensor_tensor(plane_tile(b)[:, c0:c1, t, :],
-                                 pages[i][:, cols].rearrange("p (c n) -> p c n", n=CHUNK),
-                                 resp2[i][:, cols].rearrange("p (c n) -> p c n", n=CHUNK), MULT)
+            if i < last - 1:
+                engine.tensor_tensor(plane(i)[:, cols], pages[i][:, cols], resp2[i][:, cols], MULT)
+            else:
+                half = pairs[:, c0:c1, 1, :].rearrange("p c (n e) -> p c n e", e=2)[:, :, :, i % 2]
+                engine.tensor_tensor(half, pages[i][:, cols].rearrange("p (c n) -> p c n", n=CHUNK),
+                                     resp2[i][:, cols].rearrange("p (c n) -> p c n", n=CHUNK), MULT)
 
         woven = {}
 
-        def weave(copy, b, c):
-            dst = woven[b][:, PACK * CHUNK * c : PACK * CHUNK * (c + 1)]
-            copy(dst.rearrange("p (n i t) -> p n t i", t=PACK, i=4),
-                 planes[b][:, c, :, :].rearrange("p t (n i) -> p n t i", i=4))
+        def weave_planes(c0, c1):
+            dst = woven[0][:, PACK * CHUNK * c0 : PACK * CHUNK * c1]
+            nc.scalar.copy(dst.rearrange("p (n i t) -> p n t i", t=PACK, i=4),
+                           planes[0][:, :, CHUNK * c0 : CHUNK * c1].rearrange("p t (n i) -> p n t i", i=4))
+
+        def pair_planes(c0, c1):
+            nc.scalar.copy(pairs[:, c0:c1, 0, :].rearrange("p c (n e) -> p c n e", e=2),
+                           planes[1][:, :, CHUNK * c0 : CHUNK * c1].rearrange("p e (c n) -> p c n e", n=CHUNK))
+
+        def weave_pairs(copy, word, c):
+            dst = woven[1][:, PACK * CHUNK * c : PACK * CHUNK * (c + 1)]
+            copy(dst.bitcast(word).rearrange("p (n h) -> p n h", h=2),
+                 pairs[:, c, :, :].bitcast(word).rearrange("p h n -> p n h"))
 
         z_sc = slot("z_sc", [P, PASSES * T2], U8)
         z_codes = {}
 
-        def quantize_z(b, c0, c1, tag=None):
-            codes = slot("z_codes%d_%d" % (b, c0), [P, CHUNK * (c1 - c0)], U32, tag)
-            nc.vector.quantize_mx(out=codes[:].bitcast(FP8X4),
+        def quantize_z(b, c0, c1, codes):
+            nc.vector.quantize_mx(out=codes.bitcast(FP8X4),
                                   scales=z_sc[:, T2 * b + CHUNK * c0 : T2 * b + CHUNK * c1],
                                   in_=woven[b][:, PACK * CHUNK * c0 : PACK * CHUNK * c1])
             for c in range(c0, c1):
                 z_codes[(b, c)] = codes[:, CHUNK * (c - c0) : CHUNK * (c - c0 + 1)]
 
-        for u in range(AHEAD):
-            produce(u)
+        produce(0)
+        w2_raw.append(load_w2(1))
+        produce(1)
         for u in range(last_unit):
             stream, i = units[u]
             if u + AHEAD <= last_unit:
                 produce(u + AHEAD)
-            if stream == "had" and i >= LAG:
-                load_squared_resp(i - LAG)
-            scatter(u, 0)
+            if u in first_hosts and u > 0:
+                load_squared_resp(first_hosts[u])
+            scatter(u, feats[u], 0, S)
             if u == 0:
                 w1["codes"] = slot("w1_codes", [P, PASSES * 2 * H], U8)
                 reorder_columns(w1["codes"][:].bitcast(U16), w1_raw[:].bitcast(U16))
                 w1["sc"] = slot("w1_sc", [P, PASSES * H], U8, "w1_raw")
                 reorder_columns(w1["sc"][:], w1_sc_raw[:])
-            if u == 1:
-                w2_raw.append(load_w2(1))
-                round_w2(1, 0, PACK, "page2")
-                quantize_w2(1, 0, PACK)
+                quantize_w2(1, "page1", "w1_sc_raw")
             if stream == "pho":
-                b, t = divmod(i, PACK)
                 for h in range(2):
-                    weigh(nc.gpsimd, i, CHUNKS // 2 * h, CHUNKS // 2 * (h + 1))
-                if t == PACK - 1:
-                    woven[b] = slot("woven_%d" % b, [P, T2 * PACK], BF16)
-                    for c in range(CHUNKS):
-                        weave(nc.scalar.copy, b, c)
-                if PAGES - LAG <= i + RESP_SLOTS < PAGES:
+                    weigh(nc.gpsimd, i, OPEN * h, OPEN * (h + 1))
+                if i == PACK - 1:
+                    woven[0] = slot("woven_0", [P, T2 * PACK], BF16)
+                    for c in range(0, CHUNKS, 2):
+                        weave_planes(c, c + 2)
+                if i == PACK + 1:
+                    for h in range(2):
+                        pair_planes(OPEN * h, OPEN * (h + 1))
+                if i + RESP_SLOTS < PAGES:
                     load_squared_resp(i + RESP_SLOTS)
+                if i == last - 1:
+                    last_feat = apply_gain(last_unit, LAST_CUT, S, "page%d" % (i % PAGE_SLOTS))
 
         def accumulate(c, b):
             for n in range(N // P):
@@ -334,25 +335,28 @@ def tile_list_shower_deposit_weave_kernel(
                 nc.sync.dma_start(rows.rearrange("(n p) c -> p n c", p=P),
                                   stage[:, h, :].rearrange("p (n c) -> p n c", c=CHUNK))
 
-        last = PAGES - 1
-        scatter(last_unit, 0)
-        quantize_z(0, 0, OPEN, "z_codes0")
+        scatter(last_unit, feats[last_unit], 0, LAST_CUT)
+        early = slot("z_codes0_early", [P, HALF], U32, "z_codes0")
+        quantize_z(0, 0, OPEN, early[:])
         for c in range(OPEN):
             accumulate(c, 0)
-        lo, hi, feat = feats[last_unit][1]
-        nc.vector.tensor_copy(pages[last][:].indirect(idx3[:, lo // PER_COL : hi // PER_COL]), feat[:])
+        scatter(last_unit, last_feat, LAST_CUT, S)
+        late = slot("z_codes0_late", [P, HALF], U32, "page%d" % ((last - 1) % PAGE_SLOTS))
+        second = slot("z_codes1", [P, T2], U32, "resp%d" % ((last - 1) % RESP_SLOTS))
         woven[1] = slot("woven_1", [P, T2 * PACK], BF16, "planes0")
         weigh(nc.vector, last, 0, 1)
         weigh(nc.vector, last, 1, 2)
-        weave(nc.vector.tensor_copy, 1, 0)
-        weave(nc.scalar.copy, 1, 1)
+        weave_pairs(nc.vector.tensor_copy, I32, 0)
+        weave_pairs(nc.scalar.copy, U32, 1)
         for c in range(CHUNKS):
             if c + 2 < CHUNKS:
                 weigh(nc.vector, last, c + 2, c + 3)
-            quantize_z(1, c, c + 1)
-            if c + 2 < CHUNKS:
-                weave(nc.vector.tensor_copy, 1, c + 2)
+            quantize_z(1, c, c + 1, second[:, CHUNK * c : CHUNK * (c + 1)])
+            if c == 0:
+                weave_pairs(nc.scalar.copy, U32, 2)
+            elif c + 2 < CHUNKS:
+                weave_pairs(nc.vector.tensor_copy, I32, c + 2)
             finish(c)
             if c + OPEN < CHUNKS:
-                quantize_z(0, c + OPEN, c + OPEN + 1)
+                quantize_z(0, c + OPEN, c + OPEN + 1, late[:, CHUNK * c : CHUNK * (c + 1)])
                 accumulate(c + OPEN, 0)

@@ -65,7 +65,7 @@ def tile_list_shower_deposit_weave_kernel(
         tab2_sc = slot("tab2_sc", [P, T], U8)
         tab_sc = slot("tab_sc", [P, T], U8)
         v1_sc = slot("v1_sc", [P, PASSES * S], U8)
-        w1_sc_raw = slot("w1_sc_raw", [P, PASSES * H], U8)
+        w1_sc_raw = slot("w1_sc_raw", [P, PASSES * H], U8, "page2")
         w3_sc = slot("w3_sc", [P, PASSES * N], U8)
         nc.gpsimd.memset(tab2_sc[:].bitcast(I32), 0)
         nc.vector.memset(rows_i32(tab_sc, QUAD, QUAD), 0)
@@ -85,7 +85,7 @@ def tile_list_shower_deposit_weave_kernel(
                     src[:, ROWS * q : ROWS * (q + 1), :].rearrange("a r n -> r a n").bitcast(I32))
 
         def load_w2(b):
-            raw = slot("w2_raw%d" % b, [P, PACK, K_PASS], F32, "resp%d" % (2 - b))
+            raw = slot("w2_raw%d" % b, [P, PACK, K_PASS], F32, "resp%d" % (2 - 2 * b))
             nc.sync.dma_start(raw[:], w2[:, K_PASS * b : K_PASS * (b + 1)].rearrange("(p j) c -> p j c", j=PACK))
             return raw
 
@@ -115,48 +115,54 @@ def tile_list_shower_deposit_weave_kernel(
         load_scale_rows(tab2_sc, tab2_scales)
         idx1 = load_list("idx1", offs)
         nc.sync.dma_start(rows_i32(tab_sc, 0, QUAD), tab_scales.rearrange("a g n -> g a n").bitcast(I32))
-        tab2_w = load_words("tab2_w", tab2_words[0], "planes1")
         w2_raw = [load_w2(0)]
-        tab_w = [load_words("tab_w0", tab_words[0], "page2")]
+        tab2_w = load_words("tab2_w", tab2_words[0], "planes1")
         idx4 = load_list("idx4", offs4)
         load_gain("had", 0)
-        tab_w.append(load_words("tab_w1", tab_words[1], "page3"))
+        tab_w = [load_words("tab_w0", tab_words[0], "resp1")]
         load_gain("had", 1)
+        tab_w.append(load_words("tab_w1", tab_words[1], "page1"))
+        load_gain("had", 2)
         w1_raw = slot("w1_raw", [P, PASSES * 2 * H], U8)
         nc.sync.dma_start(w1_raw[:].bitcast(I32).rearrange("p (a n) -> p a n", a=PASSES),
                           w1_words.rearrange("a p n -> p a n").bitcast(I32))
         load_scale_rows(w1_sc_raw, w1_scales)
-        load_gain("had", 2)
         idx3 = load_list("idx3", offs3)
+        w2_raw.append(load_w2(1))
 
-        def gather(name, window, lst, dtype):
-            picked = slot(name, [P, S], dtype)
-            nc.vector.tensor_copy(picked[:], window.indirect(lst[:]))
-            return picked
+        def gather(picked, window, lst, lo, hi):
+            nc.vector.tensor_copy(picked[:, lo:hi], window.indirect(lst[:, lo // PER_COL : hi // PER_COL]))
 
         w2_codes = {}
         w2_sc = slot("w2_sc", [P, H], U8)
 
-        def quantize_w2(b, rounded_tag, codes_tag=None):
-            grouped = slot("w2_bf%d" % b, [P, PACK * K_PASS], BF16, rounded_tag)
-            nc.scalar.copy(grouped[:].rearrange("p (t m j) -> p m t j", m=P, j=PACK),
+        w2_bf = {}
+
+        def round_w2(b, tag):
+            w2_bf[b] = slot("w2_bf%d" % b, [P, PACK * K_PASS], BF16, tag)
+            nc.scalar.copy(w2_bf[b][:].rearrange("p (t m j) -> p m t j", m=P, j=PACK),
                            w2_raw[b][:].rearrange("p j (m t) -> p m t j", t=PACK))
-            w2_codes[b] = slot("w2_codes%d" % b, [P, K_PASS], U32, codes_tag)
+
+        def quantize_w2(b):
+            w2_codes[b] = slot("w2_codes%d" % b, [P, K_PASS], U32)
             nc.vector.quantize_mx(out=w2_codes[b][:].bitcast(FP8X4),
-                                  scales=w2_sc[:, K_PASS * b : K_PASS * (b + 1)], in_=grouped[:])
+                                  scales=w2_sc[:, K_PASS * b : K_PASS * (b + 1)], in_=w2_bf[b][:])
 
         def reorder_columns(dst, src):
             nc.vector.tensor_copy(dst.rearrange("p (g t m) -> p g t m", t=PACK, m=P),
                                   src.rearrange("p (g m t) -> p g t m", t=PACK, m=P))
 
-        v2_sc = gather("v2_sc", tab2_sc[:], idx2, U8)
-        v1_sc_rows = gather("v1_sc_rows", tab_sc[:], idx1, U8)
-        v2_w = gather("v2_w", tab2_w[:].bitcast(U32), idx2, U32)
-        quantize_w2(0, "v1_w0")
-        v1_w = [gather("v1_w%d" % a, tab_w[a][:].bitcast(U32), idx1, U32) for a in range(PASSES)]
+        v2_sc = slot("v2_sc", [P, S], U8)
+        gather(v2_sc, tab2_sc[:], idx2, 0, S)
+        v1_sc_rows = slot("v1_sc_rows", [P, S], U8)
+        gather(v1_sc_rows, tab_sc[:], idx1, 0, S)
+        round_w2(0, "v2_w")
+        quantize_w2(0)
+        v2_w = slot("v2_w", [P, S], U32)
+        for lo in range(0, S, BANK):
+            gather(v2_w, tab2_w[:].bitcast(U32), idx2, lo, lo + BANK)
         for q in range(QUADS):
             nc.sync.dma_start(rows_i32(v1_sc, QUAD * q, ROWS), rows_i32(v1_sc_rows, PASSES * ROWS * q, PASSES * ROWS))
-
         load_gain("pho", 0)
         load_gain("had", 3)
         for t in range(1, PACK):
@@ -184,59 +190,69 @@ def tile_list_shower_deposit_weave_kernel(
                 planes[b] = slot("planes_%d" % b, [P, PACK // (b + 1), T2], BF16, "planes%d" % b)
             return planes[b][:, t, :]
 
-        first_hosts = {0: 1, 2: 0, 4: 1, 6: 2}
+        raw_hosts = {3: "resp0", 4: "resp1", 6: "resp0", 8: "resp1", 10: "resp2", 12: "resp0"}
+        feat_hosts = {1: "w1_codes", 2: "resp2", 3: "w2_codes1"}
 
         def staging(u):
-            if u in first_hosts:
-                return slot("raw_%d" % u, [P, S], F32, "resp%d" % first_hosts[u])[:]
-            if u == last_unit:
-                return slot("raw_%d" % u, [P, S], F32, "feat%d" % (u % FEAT_SLOTS))[:]
+            if u in raw_hosts:
+                return slot("raw_%d" % u, [P, S], F32, raw_hosts[u])[:]
             if u >= AHEAD and units[u - AHEAD][0] == "pho":
                 return plane(units[u - AHEAD][1]).bitcast(F32)
             return None
 
-        raws = {}
+        def hadron_sums(bank, i, cols):
+            m0 = P * i
+            nc.tensor.matmul_mx(out=bank[:], lhsT=w2_codes[i // PACK][:, m0 % K_PASS : m0 % K_PASS + P].bitcast(FP8X4),
+                                lhsT_scale=w2_sc[:, m0 : m0 + P],
+                                rhs=v2_w[:, cols].bitcast(FP8X4), rhs_scale=v2_sc[:, cols],
+                                start=True, stop=True)
 
-        def apply_gain(u, lo, hi, tag):
-            stream, i = units[u]
-            feat = slot("feat_%d_%d" % (u, lo), [P, hi - lo], F32, tag)
-            nc.gpsimd.tensor_tensor(feat[:], raws[u][:, lo:hi], gains[(stream, i % PACK)][:, lo:hi], MULT)
-            return feat
+        pairs = slot("pairs", [P, CHUNKS, 2, 2 * CHUNK], BF16)
+
+        def by_chunk(ap):
+            return ap.rearrange("p (c n) -> p c n", n=CHUNK)
+
+        def photon_sums(bank, i, cols):
+            for a in range(PASSES):
+                c0 = H * a + P * i
+                nc.tensor.matmul_mx(out=bank[:], lhsT=w1["codes"][:, 2 * c0 : 2 * (c0 + P)].bitcast(FP4X4),
+                                    lhsT_scale=w1["sc"][:, c0 : c0 + P],
+                                    rhs=w1["v"][:, a, cols].bitcast(FP8X4),
+                                    rhs_scale=v1_sc[:, S * a + cols.start : S * a + cols.stop],
+                                    start=(a == 0), stop=(a == PASSES - 1))
+
+        def produce_last():
+            raw = pairs[:, 0 : LAST_CUT // CHUNK, 1, :].bitcast(F32)
+            rest = slot("raw_rest", [P, S - LAST_CUT], F32)
+            for c in range(S // BANK):
+                photon_sums(banks[c], last, slice(BANK * c, BANK * (c + 1)))
+            nc.scalar.activation(raw[:, 0:2, :], by_chunk(banks[0][:]), ACT.Relu)
+            nc.scalar.activation(raw[:, 2, :], banks[1][:, 0:CHUNK], ACT.Relu)
+            nc.scalar.activation(rest[:], banks[1][:, CHUNK:BANK], ACT.Relu)
+            feats[last_unit] = slot("feat_last", [P, LAST_CUT], F32, "z_codes0")
+            nc.gpsimd.tensor_tensor(by_chunk(feats[last_unit][:]), raw,
+                                    by_chunk(gains[("pho", last % PACK)][:, 0:LAST_CUT]), MULT)
+            feats["rest"] = rest
 
         def produce(u):
             stream, i = units[u]
-            m0 = P * i
             raw = staging(u)
-            tag = "w1_codes" if u == 0 else "feat%d" % (u % FEAT_SLOTS)
-            if u != last_unit:
-                feats[u] = slot("feat_%d" % u, [P, S], F32, tag)
+            tag = feat_hosts.get(u, "feat%d" % (u % FEAT_SLOTS))
+            feats[u] = slot("feat_%d" % u, [P, S], F32, tag)
             if raw is None:
                 raw = feats[u][:]
-            raws[u] = raw
             for c in range(S // BANK):
                 cols = slice(BANK * c, BANK * (c + 1))
                 bank = banks[c]
                 if stream == "had":
-                    nc.tensor.matmul_mx(out=bank[:], lhsT=w2_codes[i // PACK][:, m0 % K_PASS : m0 % K_PASS + P].bitcast(FP8X4),
-                                        lhsT_scale=w2_sc[:, m0 : m0 + P],
-                                        rhs=v2_w[:, cols].bitcast(FP8X4), rhs_scale=v2_sc[:, cols],
-                                        start=True, stop=True)
+                    hadron_sums(bank, i, cols)
                 else:
-                    for a in range(PASSES):
-                        c0 = H * a + m0
-                        nc.tensor.matmul_mx(out=bank[:], lhsT=w1["codes"][:, 2 * c0 : 2 * (c0 + P)].bitcast(FP4X4),
-                                            lhsT_scale=w1["sc"][:, c0 : c0 + P],
-                                            rhs=v1_w[a][:, cols].bitcast(FP8X4),
-                                            rhs_scale=v1_sc[:, S * a + cols.start : S * a + cols.stop],
-                                            start=(a == 0), stop=(a == PASSES - 1))
+                    photon_sums(bank, i, cols)
                 nc.scalar.activation(raw[:, cols], bank[:], ACT.Square if stream == "had" else ACT.Relu)
-            if u == last_unit:
-                feats[u] = apply_gain(u, 0, LAST_CUT, "z_codes0")
-                return
-            gain = gains[(stream, i % PACK)]
-            step = BANK if u == 0 else S
+            step = BANK if u == LAG + 1 else S
             for lo in range(0, S, step):
-                nc.gpsimd.tensor_tensor(feats[u][:, lo : lo + step], raw[:, lo : lo + step], gain[:, lo : lo + step], MULT)
+                cols = slice(lo, lo + step)
+                nc.gpsimd.tensor_tensor(feats[u][:, cols], raw[:, cols], gains[(stream, i % PACK)][:, cols], MULT)
 
         pages = {}
 
@@ -246,8 +262,6 @@ def tile_list_shower_deposit_weave_kernel(
                 pages[i] = slot("page_%d" % i, [P, T2], F32, "page%d" % (i % PAGE_SLOTS))
             lst = idx4 if stream == "had" else idx3
             nc.vector.tensor_copy(pages[i][:].indirect(lst[:, lo // PER_COL : hi // PER_COL]), feat[:])
-
-        pairs = slot("pairs", [P, CHUNKS, 2, 2 * CHUNK], BF16)
 
         def weigh(engine, i, c0, c1):
             cols = slice(CHUNK * c0, CHUNK * c1)
@@ -284,36 +298,62 @@ def tile_list_shower_deposit_weave_kernel(
             for c in range(c0, c1):
                 z_codes[(b, c)] = codes[:, CHUNK * (c - c0) : CHUNK * (c - c0 + 1)]
 
-        produce(0)
-        w2_raw.append(load_w2(1))
+        first = []
+        for c, host in enumerate(("page3", "v1_w")):
+            cols = slice(BANK * c, BANK * (c + 1))
+            first.append(slot("raw_0_%d" % c, [P, BANK], F32, host))
+            hadron_sums(banks[c], 0, cols)
+            nc.scalar.activation(first[c][:], banks[c][:], ACT.Square)
         produce(1)
-        for u in range(last_unit):
+        produce(2)
+        pages[0] = slot("page_0", [P, T2], F32, "page0")
+        for c in range(S // BANK):
+            cols = slice(BANK * c, BANK * (c + 1))
+            nc.vector.tensor_tensor(pages[0][:].indirect(idx4[:, cols.start // PER_COL : cols.stop // PER_COL]),
+                                    first[c][:], gains[("had", 0)][:, cols], MULT)
+        w1["v"] = slot("v1_w", [P, PASSES, S], U32)
+        for a in range(PASSES):
+            gather(w1["v"][:, a, :], tab_w[a][:].bitcast(U32), idx1, 0, S)
+        round_w2(1, "page3")
+        scatter(1, feats[1], 0, S)
+        w1["codes"] = slot("w1_codes", [P, PASSES * 2 * H], U8)
+        reorder_columns(w1["codes"][:].bitcast(U16), w1_raw[:].bitcast(U16))
+        w1["sc"] = slot("w1_sc", [P, PASSES * H], U8, "w1_raw")
+        reorder_columns(w1["sc"][:], w1_sc_raw[:])
+        produce(3)
+        load_squared_resp(0)
+        for u in range(AHEAD, last_unit):
             stream, i = units[u]
-            if u + AHEAD <= last_unit:
+            if u == 4:
+                quantize_w2(1)
+            if u + AHEAD < last_unit - 1:
                 produce(u + AHEAD)
-            if u in first_hosts and u > 0:
-                load_squared_resp(first_hosts[u])
+            if u + AHEAD == last_unit - 2:
+                produce(last_unit - 1)
+            if u + AHEAD == last_unit - 1:
+                produce_last()
+            if u == 2:
+                load_squared_resp(1)
+            if u in (4, 6, 8, 10):
+                load_squared_resp(u // 2 + 1)
             scatter(u, feats[u], 0, S)
-            if u == 0:
-                w1["codes"] = slot("w1_codes", [P, PASSES * 2 * H], U8)
-                reorder_columns(w1["codes"][:].bitcast(U16), w1_raw[:].bitcast(U16))
-                w1["sc"] = slot("w1_sc", [P, PASSES * H], U8, "w1_raw")
-                reorder_columns(w1["sc"][:], w1_sc_raw[:])
-                quantize_w2(1, "page1", "w1_sc_raw")
+            if u == 2:
+                load_squared_resp(2)
             if stream == "pho":
                 for h in range(2):
                     weigh(nc.gpsimd, i, OPEN * h, OPEN * (h + 1))
-                if i == PACK - 1:
+                if i == PACK:
                     woven[0] = slot("woven_0", [P, T2 * PACK], BF16)
                     for c in range(0, CHUNKS, 2):
                         weave_planes(c, c + 2)
                 if i == PACK + 1:
                     for h in range(2):
                         pair_planes(OPEN * h, OPEN * (h + 1))
-                if i + RESP_SLOTS < PAGES:
-                    load_squared_resp(i + RESP_SLOTS)
+                if i + RESP_SLOTS == last:
+                    load_squared_resp(last)
                 if i == last - 1:
-                    last_feat = apply_gain(last_unit, LAST_CUT, S, "page%d" % (i % PAGE_SLOTS))
+                    last_feat = slot("feat_rest", [P, S - LAST_CUT], F32, "page%d" % (i % PAGE_SLOTS))
+                    nc.gpsimd.tensor_tensor(last_feat[:], feats["rest"][:], gains[("pho", last % PACK)][:, LAST_CUT:S], MULT)
 
         def accumulate(c, b):
             for n in range(N // P):

@@ -37,7 +37,7 @@ AHEAD = 2
 CHUNK = 256
 CHUNKS = T2 // CHUNK
 OPEN = BANKS // 2
-LAST_CUT = 768
+LAST_CUT = BANK
 
 
 def tile_list_shower_deposit_weave_kernel(
@@ -65,7 +65,7 @@ def tile_list_shower_deposit_weave_kernel(
         tab2_sc = slot("tab2_sc", [P, T], U8)
         tab_sc = slot("tab_sc", [P, T], U8)
         v1_sc = slot("v1_sc", [P, PASSES * S], U8)
-        w1_sc_raw = slot("w1_sc_raw", [P, PASSES * H], U8, "page2")
+        w1_sc_raw = slot("w1_sc_raw", [P, PASSES * H], U8)
         w3_sc = slot("w3_sc", [P, PASSES * N], U8)
         nc.gpsimd.memset(tab2_sc[:].bitcast(I32), 0)
         nc.vector.memset(rows_i32(tab_sc, QUAD, QUAD), 0)
@@ -116,7 +116,7 @@ def tile_list_shower_deposit_weave_kernel(
         idx1 = load_list("idx1", offs)
         nc.sync.dma_start(rows_i32(tab_sc, 0, QUAD), tab_scales.rearrange("a g n -> g a n").bitcast(I32))
         w2_raw = [load_w2(0)]
-        tab2_w = load_words("tab2_w", tab2_words[0], "planes1")
+        tab2_w = load_words("tab2_w", tab2_words[0], "woven_0")
         idx4 = load_list("idx4", offs4)
         load_gain("had", 0)
         tab_w = [load_words("tab_w0", tab_words[0], "resp1")]
@@ -148,9 +148,14 @@ def tile_list_shower_deposit_weave_kernel(
             nc.vector.quantize_mx(out=w2_codes[b][:].bitcast(FP8X4),
                                   scales=w2_sc[:, K_PASS * b : K_PASS * (b + 1)], in_=w2_bf[b][:])
 
-        def reorder_columns(dst, src):
-            nc.vector.tensor_copy(dst.rearrange("p (g t m) -> p g t m", t=PACK, m=P),
-                                  src.rearrange("p (g m t) -> p g t m", t=PACK, m=P))
+        w1_codes = slot("w1_codes", [P, PASSES * 2 * H], U8)
+        w1_sc = slot("w1_sc", [P, PASSES * H], U8)
+
+        def reorder_w1(t):
+            nc.gpsimd.tensor_copy(w1_codes[:].rearrange("p (g t m e) -> p g t m e", t=PACK, m=P, e=2)[:, :, t, :, :],
+                                  w1_raw[:].rearrange("p (g m t e) -> p g t m e", t=PACK, m=P, e=2)[:, :, t, :, :])
+            nc.gpsimd.tensor_copy(w1_sc[:].rearrange("p (g t m) -> p g t m", t=PACK, m=P)[:, :, t, :],
+                                  w1_sc_raw[:].rearrange("p (g m t) -> p g t m", t=PACK, m=P)[:, :, t, :])
 
         v2_sc = slot("v2_sc", [P, S], U8)
         gather(v2_sc, tab2_sc[:], idx2, 0, S)
@@ -182,20 +187,26 @@ def tile_list_shower_deposit_weave_kernel(
         w1 = {}
         feats = {}
 
-        planes = {}
+        planes = slot("planes", [P, PACK, T2], BF16)
+        pairs = slot("pairs", [P, CHUNKS, 2, 2 * CHUNK], BF16)
+
+        def by_chunk(ap, width=CHUNK):
+            return ap.rearrange("p (c n) -> p c n", n=width)
 
         def plane(i):
             b, t = divmod(i, PACK)
-            if b not in planes:
-                planes[b] = slot("planes_%d" % b, [P, PACK // (b + 1), T2], BF16, "planes%d" % b)
-            return planes[b][:, t, :]
+            if b == 0:
+                return by_chunk(planes[:, t, :])
+            if t < 2:
+                return pairs[:, :, 1, CHUNK * t : CHUNK * (t + 1)]
+            return pairs[:, :, 1, :].rearrange("p c (n e) -> p c n e", e=2)[:, :, :, t - 2]
 
         raw_hosts = {3: "resp0", 4: "resp1", 6: "resp0", 8: "resp1", 10: "resp2", 12: "resp0"}
-        feat_hosts = {1: "w1_codes", 2: "resp2", 3: "w2_codes1"}
+        feat_hosts = {2: "resp2", 3: "w2_codes1"}
 
         def staging(u):
             if u in raw_hosts:
-                return slot("raw_%d" % u, [P, S], F32, raw_hosts[u])[:]
+                return by_chunk(slot("raw_%d" % u, [P, S], F32, raw_hosts[u])[:], P)
             if u >= AHEAD and units[u - AHEAD][0] == "pho":
                 return plane(units[u - AHEAD][1]).bitcast(F32)
             return None
@@ -207,32 +218,24 @@ def tile_list_shower_deposit_weave_kernel(
                                 rhs=v2_w[:, cols].bitcast(FP8X4), rhs_scale=v2_sc[:, cols],
                                 start=True, stop=True)
 
-        pairs = slot("pairs", [P, CHUNKS, 2, 2 * CHUNK], BF16)
-
-        def by_chunk(ap):
-            return ap.rearrange("p (c n) -> p c n", n=CHUNK)
-
         def photon_sums(bank, i, cols):
             for a in range(PASSES):
                 c0 = H * a + P * i
-                nc.tensor.matmul_mx(out=bank[:], lhsT=w1["codes"][:, 2 * c0 : 2 * (c0 + P)].bitcast(FP4X4),
-                                    lhsT_scale=w1["sc"][:, c0 : c0 + P],
+                nc.tensor.matmul_mx(out=bank[:], lhsT=w1_codes[:, 2 * c0 : 2 * (c0 + P)].bitcast(FP4X4),
+                                    lhsT_scale=w1_sc[:, c0 : c0 + P],
                                     rhs=w1["v"][:, a, cols].bitcast(FP8X4),
                                     rhs_scale=v1_sc[:, S * a + cols.start : S * a + cols.stop],
                                     start=(a == 0), stop=(a == PASSES - 1))
 
         def produce_last():
-            raw = pairs[:, 0 : LAST_CUT // CHUNK, 1, :].bitcast(F32)
-            rest = slot("raw_rest", [P, S - LAST_CUT], F32)
+            raws = []
             for c in range(S // BANK):
                 photon_sums(banks[c], last, slice(BANK * c, BANK * (c + 1)))
-            nc.scalar.activation(raw[:, 0:2, :], by_chunk(banks[0][:]), ACT.Relu)
-            nc.scalar.activation(raw[:, 2, :], banks[1][:, 0:CHUNK], ACT.Relu)
-            nc.scalar.activation(rest[:], banks[1][:, CHUNK:BANK], ACT.Relu)
-            feats[last_unit] = slot("feat_last", [P, LAST_CUT], F32, "z_codes0")
-            nc.gpsimd.tensor_tensor(by_chunk(feats[last_unit][:]), raw,
-                                    by_chunk(gains[("pho", last % PACK)][:, 0:LAST_CUT]), MULT)
-            feats["rest"] = rest
+                raws.append(slot("raw_last%d" % c, [P, BANK], F32))
+                nc.scalar.activation(raws[c][:], banks[c][:], ACT.Relu)
+            feats[last_unit] = slot("feat_last", [P, BANK], F32, "z_codes0")
+            nc.gpsimd.tensor_tensor(feats[last_unit][:], raws[0][:], gains[("pho", last % PACK)][:, 0:BANK], MULT)
+            feats["rest"] = raws[1]
 
         def produce(u):
             stream, i = units[u]
@@ -240,7 +243,7 @@ def tile_list_shower_deposit_weave_kernel(
             tag = feat_hosts.get(u, "feat%d" % (u % FEAT_SLOTS))
             feats[u] = slot("feat_%d" % u, [P, S], F32, tag)
             if raw is None:
-                raw = feats[u][:]
+                raw = by_chunk(feats[u][:], P)
             for c in range(S // BANK):
                 cols = slice(BANK * c, BANK * (c + 1))
                 bank = banks[c]
@@ -248,11 +251,12 @@ def tile_list_shower_deposit_weave_kernel(
                     hadron_sums(bank, i, cols)
                 else:
                     photon_sums(bank, i, cols)
-                nc.scalar.activation(raw[:, cols], bank[:], ACT.Square if stream == "had" else ACT.Relu)
+                nc.scalar.activation(raw[:, 4 * c : 4 * (c + 1), :], by_chunk(bank[:], P), ACT.Square if stream == "had" else ACT.Relu)
             step = BANK if u == LAG + 1 else S
             for lo in range(0, S, step):
                 cols = slice(lo, lo + step)
-                nc.gpsimd.tensor_tensor(feats[u][:, cols], raw[:, cols], gains[(stream, i % PACK)][:, cols], MULT)
+                nc.gpsimd.tensor_tensor(by_chunk(feats[u][:, cols], P), raw[:, lo // P : (lo + step) // P, :],
+                                        by_chunk(gains[(stream, i % PACK)][:, cols], P), MULT)
 
         pages = {}
 
@@ -265,23 +269,18 @@ def tile_list_shower_deposit_weave_kernel(
 
         def weigh(engine, i, c0, c1):
             cols = slice(CHUNK * c0, CHUNK * c1)
-            if i < last - 1:
-                engine.tensor_tensor(plane(i)[:, cols], pages[i][:, cols], resp2[i][:, cols], MULT)
-            else:
-                half = pairs[:, c0:c1, 1, :].rearrange("p c (n e) -> p c n e", e=2)[:, :, :, i % 2]
-                engine.tensor_tensor(half, pages[i][:, cols].rearrange("p (c n) -> p c n", n=CHUNK),
-                                     resp2[i][:, cols].rearrange("p (c n) -> p c n", n=CHUNK), MULT)
+            engine.tensor_tensor(plane(i)[:, c0:c1, :], by_chunk(pages[i][:, cols]), by_chunk(resp2[i][:, cols]), MULT)
 
         woven = {}
 
         def weave_planes(c0, c1):
             dst = woven[0][:, PACK * CHUNK * c0 : PACK * CHUNK * c1]
             nc.scalar.copy(dst.rearrange("p (n i t) -> p n t i", t=PACK, i=4),
-                           planes[0][:, :, CHUNK * c0 : CHUNK * c1].rearrange("p t (n i) -> p n t i", i=4))
+                           planes[:, :, CHUNK * c0 : CHUNK * c1].rearrange("p t (n i) -> p n t i", i=4))
 
         def pair_planes(c0, c1):
             nc.scalar.copy(pairs[:, c0:c1, 0, :].rearrange("p c (n e) -> p c n e", e=2),
-                           planes[1][:, :, CHUNK * c0 : CHUNK * c1].rearrange("p e (c n) -> p c n e", n=CHUNK))
+                           pairs[:, c0:c1, 1, :].rearrange("p c (e n) -> p c n e", e=2))
 
         def weave_pairs(copy, word, c):
             dst = woven[1][:, PACK * CHUNK * c : PACK * CHUNK * (c + 1)]
@@ -316,16 +315,15 @@ def tile_list_shower_deposit_weave_kernel(
             gather(w1["v"][:, a, :], tab_w[a][:].bitcast(U32), idx1, 0, S)
         round_w2(1, "page3")
         scatter(1, feats[1], 0, S)
-        w1["codes"] = slot("w1_codes", [P, PASSES * 2 * H], U8)
-        reorder_columns(w1["codes"][:].bitcast(U16), w1_raw[:].bitcast(U16))
-        w1["sc"] = slot("w1_sc", [P, PASSES * H], U8, "w1_raw")
-        reorder_columns(w1["sc"][:], w1_sc_raw[:])
+        reorder_w1(0)
         produce(3)
         load_squared_resp(0)
         for u in range(AHEAD, last_unit):
             stream, i = units[u]
             if u == 4:
                 quantize_w2(1)
+            if u in (3, 5, 7):
+                reorder_w1(u // 2)
             if u + AHEAD < last_unit - 1:
                 produce(u + AHEAD)
             if u + AHEAD == last_unit - 2:
@@ -383,7 +381,7 @@ def tile_list_shower_deposit_weave_kernel(
         scatter(last_unit, last_feat, LAST_CUT, S)
         late = slot("z_codes0_late", [P, HALF], U32, "page%d" % ((last - 1) % PAGE_SLOTS))
         second = slot("z_codes1", [P, T2], U32, "resp%d" % ((last - 1) % RESP_SLOTS))
-        woven[1] = slot("woven_1", [P, T2 * PACK], BF16, "planes0")
+        woven[1] = slot("woven_1", [P, T2 * PACK], BF16, "planes")
         weigh(nc.vector, last, 0, 1)
         weigh(nc.vector, last, 1, 2)
         weave_pairs(nc.vector.tensor_copy, I32, 0)
@@ -399,4 +397,5 @@ def tile_list_shower_deposit_weave_kernel(
             finish(c)
             if c + OPEN < CHUNKS:
                 quantize_z(0, c + OPEN, c + OPEN + 1, late[:, CHUNK * c : CHUNK * (c + 1)])
-                accumulate(c + OPEN, 0)
+            if OPEN <= c + OPEN - 1 < CHUNKS:
+                accumulate(c + OPEN - 1, 0)

@@ -37,6 +37,8 @@ AHEAD = 2
 CHUNK = 256
 CHUNKS = T2 // CHUNK
 OPEN = BANKS // 2
+EDGES = [0, CHUNK // 2] + list(range(CHUNK, T2, CHUNK)) + [T2 - CHUNK // 2, T2]
+SCALAR_WEAVES = (2, 3)
 LAST_CUT = BANK
 
 
@@ -67,7 +69,7 @@ def tile_list_shower_deposit_weave_kernel(
         v1_sc = slot("v1_sc", [P, PASSES * S], U8)
         w1_sc_raw = slot("w1_sc_raw", [P, PASSES * H], U8)
         w3_sc = slot("w3_sc", [P, PASSES * N], U8)
-        nc.gpsimd.memset(tab2_sc[:].bitcast(I32), 0)
+        nc.vector.memset(tab2_sc[:].bitcast(I32), 0)
         nc.vector.memset(rows_i32(tab_sc, QUAD, QUAD), 0)
         nc.vector.memset(rows_i32(tab_sc, 2 * QUAD, 2 * QUAD), 0)
         for tile in (v1_sc, w1_sc_raw, w3_sc):
@@ -91,12 +93,13 @@ def tile_list_shower_deposit_weave_kernel(
 
         gains = {}
 
-        def load_gain(stream, t):
+        def load_gain(stream, t, step=S):
             gain = slot("gain_%s%d" % (stream, t), [P, S], F32)
             src = wg2 if stream == "had" else wg1
             rows = src.rearrange("(m t) j -> m t j", t=PACK)[:, t, :]
-            for q in range(QUADS):
-                nc.sync.dma_start(gain[QUAD * q : QUAD * (q + 1), :], rows)
+            for lo in range(0, S, step):
+                for q in range(QUADS):
+                    nc.sync.dma_start(gain[QUAD * q : QUAD * (q + 1), lo : lo + step], rows[:, lo : lo + step])
             gains[(stream, t)] = gain
 
         resp2 = {}
@@ -111,17 +114,17 @@ def tile_list_shower_deposit_weave_kernel(
                 nc.scalar.activation(tile[:, cols], tile[:, cols], ACT.Square)
             resp2[i] = tile
 
-        idx2 = load_list("idx2", offs2)
-        load_scale_rows(tab2_sc, tab2_scales)
         idx1 = load_list("idx1", offs)
         nc.sync.dma_start(rows_i32(tab_sc, 0, QUAD), tab_scales.rearrange("a g n -> g a n").bitcast(I32))
-        w2_raw = [load_w2(0)]
+        idx2 = load_list("idx2", offs2)
         tab2_w = load_words("tab2_w", tab2_words[0], "woven_0")
+        load_scale_rows(tab2_sc, tab2_scales)
+        w2_raw = [load_w2(0)]
         idx4 = load_list("idx4", offs4)
-        load_gain("had", 0)
-        tab_w = [load_words("tab_w0", tab_words[0], "resp1")]
+        load_gain("had", 0, BANK)
+        tab_w = [load_words("tab_w0", tab_words[0], "page1")]
         load_gain("had", 1)
-        tab_w.append(load_words("tab_w1", tab_words[1], "page1"))
+        tab_w.append(load_words("tab_w1", tab_words[1], "resp1"))
         load_gain("had", 2)
         w1_raw = slot("w1_raw", [P, PASSES * 2 * H], U8)
         nc.sync.dma_start(w1_raw[:].bitcast(I32).rearrange("p (a n) -> p a n", a=PASSES),
@@ -131,22 +134,23 @@ def tile_list_shower_deposit_weave_kernel(
         w2_raw.append(load_w2(1))
 
         def gather(picked, window, lst, lo, hi):
-            nc.vector.tensor_copy(picked[:, lo:hi], window.indirect(lst[:, lo // PER_COL : hi // PER_COL]))
+            nc.vector.tensor_copy(picked, window.indirect(lst[:, lo // PER_COL : hi // PER_COL]))
 
         w2_codes = {}
         w2_sc = slot("w2_sc", [P, H], U8)
 
         w2_bf = {}
 
-        def round_w2(b, tag):
-            w2_bf[b] = slot("w2_bf%d" % b, [P, PACK * K_PASS], BF16, tag)
-            nc.scalar.copy(w2_bf[b][:].rearrange("p (t m j) -> p m t j", m=P, j=PACK),
-                           w2_raw[b][:].rearrange("p j (m t) -> p m t j", t=PACK))
+        def round_w2(copy, b, t0, t1, tag):
+            w2_bf[(b, t0)] = slot("w2_bf%d_%d" % (b, t0), [P, (t1 - t0) * K_PASS], BF16, tag)
+            copy(w2_bf[(b, t0)][:].rearrange("p (t m j) -> p m t j", m=P, j=PACK),
+                 w2_raw[b][:].rearrange("p j (m t) -> p m t j", t=PACK)[:, :, t0:t1, :])
 
-        def quantize_w2(b):
-            w2_codes[b] = slot("w2_codes%d" % b, [P, K_PASS], U32)
-            nc.vector.quantize_mx(out=w2_codes[b][:].bitcast(FP8X4),
-                                  scales=w2_sc[:, K_PASS * b : K_PASS * (b + 1)], in_=w2_bf[b][:])
+        def quantize_w2(b, t0, t1):
+            if b not in w2_codes:
+                w2_codes[b] = slot("w2_codes%d" % b, [P, K_PASS], U32)
+            nc.vector.quantize_mx(out=w2_codes[b][:, P * t0 : P * t1].bitcast(FP8X4),
+                                  scales=w2_sc[:, K_PASS * b + P * t0 : K_PASS * b + P * t1], in_=w2_bf[(b, t0)][:])
 
         w1_codes = slot("w1_codes", [P, PASSES * 2 * H], U8)
         w1_sc = slot("w1_sc", [P, PASSES * H], U8)
@@ -157,15 +161,18 @@ def tile_list_shower_deposit_weave_kernel(
             nc.gpsimd.tensor_copy(w1_sc[:].rearrange("p (g t m) -> p g t m", t=PACK, m=P)[:, :, t, :],
                                   w1_sc_raw[:].rearrange("p (g m t) -> p g t m", t=PACK, m=P)[:, :, t, :])
 
-        v2_sc = slot("v2_sc", [P, S], U8)
-        gather(v2_sc, tab2_sc[:], idx2, 0, S)
         v1_sc_rows = slot("v1_sc_rows", [P, S], U8)
-        gather(v1_sc_rows, tab_sc[:], idx1, 0, S)
-        round_w2(0, "v2_w")
-        quantize_w2(0)
+        gather(v1_sc_rows[:], tab_sc[:], idx1, 0, S)
         v2_w = slot("v2_w", [P, S], U32)
-        for lo in range(0, S, BANK):
-            gather(v2_w, tab2_w[:].bitcast(U32), idx2, lo, lo + BANK)
+        gather(v2_w[:], tab2_w[:].bitcast(U32), idx2, 0, S)
+        v2_sc = [slot("v2_sc0", [P, BANK], U8)]
+        gather(v2_sc[0][:], tab2_sc[:], idx2, 0, BANK)
+        round_w2(nc.gpsimd.tensor_copy, 0, 0, 1, "v2_sc1")
+        round_w2(nc.scalar.copy, 0, 1, PACK, "page0")
+        quantize_w2(0, 0, 1)
+        v2_sc.append(slot("v2_sc1", [P, BANK], U8))
+        gather(v2_sc[1][:], tab2_sc[:], idx2, BANK, S)
+        quantize_w2(0, 1, PACK)
         for q in range(QUADS):
             nc.sync.dma_start(rows_i32(v1_sc, QUAD * q, ROWS), rows_i32(v1_sc_rows, PASSES * ROWS * q, PASSES * ROWS))
         load_gain("pho", 0)
@@ -215,7 +222,7 @@ def tile_list_shower_deposit_weave_kernel(
             m0 = P * i
             nc.tensor.matmul_mx(out=bank[:], lhsT=w2_codes[i // PACK][:, m0 % K_PASS : m0 % K_PASS + P].bitcast(FP8X4),
                                 lhsT_scale=w2_sc[:, m0 : m0 + P],
-                                rhs=v2_w[:, cols].bitcast(FP8X4), rhs_scale=v2_sc[:, cols],
+                                rhs=v2_w[:, cols].bitcast(FP8X4), rhs_scale=v2_sc[cols.start // BANK][:],
                                 start=True, stop=True)
 
         def photon_sums(bank, i, cols):
@@ -282,20 +289,8 @@ def tile_list_shower_deposit_weave_kernel(
             nc.scalar.copy(pairs[:, c0:c1, 0, :].rearrange("p c (n e) -> p c n e", e=2),
                            pairs[:, c0:c1, 1, :].rearrange("p c (e n) -> p c n e", e=2))
 
-        def weave_pairs(copy, word, c):
-            dst = woven[1][:, PACK * CHUNK * c : PACK * CHUNK * (c + 1)]
-            copy(dst.bitcast(word).rearrange("p (n h) -> p n h", h=2),
-                 pairs[:, c, :, :].bitcast(word).rearrange("p h n -> p n h"))
-
         z_sc = slot("z_sc", [P, PASSES * T2], U8)
         z_codes = {}
-
-        def quantize_z(b, c0, c1, codes):
-            nc.vector.quantize_mx(out=codes.bitcast(FP8X4),
-                                  scales=z_sc[:, T2 * b + CHUNK * c0 : T2 * b + CHUNK * c1],
-                                  in_=woven[b][:, PACK * CHUNK * c0 : PACK * CHUNK * c1])
-            for c in range(c0, c1):
-                z_codes[(b, c)] = codes[:, CHUNK * (c - c0) : CHUNK * (c - c0 + 1)]
 
         first = []
         for c, host in enumerate(("page3", "v1_w")):
@@ -313,7 +308,7 @@ def tile_list_shower_deposit_weave_kernel(
         w1["v"] = slot("v1_w", [P, PASSES, S], U32)
         for a in range(PASSES):
             gather(w1["v"][:, a, :], tab_w[a][:].bitcast(U32), idx1, 0, S)
-        round_w2(1, "page3")
+        round_w2(nc.scalar.copy, 1, 0, PACK, "page3")
         scatter(1, feats[1], 0, S)
         reorder_w1(0)
         produce(3)
@@ -321,7 +316,7 @@ def tile_list_shower_deposit_weave_kernel(
         for u in range(AHEAD, last_unit):
             stream, i = units[u]
             if u == 4:
-                quantize_w2(1)
+                quantize_w2(1, 0, PACK)
             if u in (3, 5, 7):
                 reorder_w1(u // 2)
             if u + AHEAD < last_unit - 1:
@@ -353,49 +348,80 @@ def tile_list_shower_deposit_weave_kernel(
                     last_feat = slot("feat_rest", [P, S - LAST_CUT], F32, "page%d" % (i % PAGE_SLOTS))
                     nc.gpsimd.tensor_tensor(last_feat[:], feats["rest"][:], gains[("pho", last % PACK)][:, LAST_CUT:S], MULT)
 
+        spans = [slice(lo, hi) for lo, hi in zip(EDGES, EDGES[1:])]
+        early_spans = EDGES.index(HALF)
+
+        def sums(c, n):
+            width = spans[c].stop - spans[c].start
+            bank, col = divmod((N // P) * (spans[c].start % HALF) + n * width, BANK)
+            return banks[bank], col, width
+
         def accumulate(c, b):
+            lo, hi = spans[c].start, spans[c].stop
             for n in range(N // P):
                 w0 = N * b + P * n
-                bank = banks[2 * (c % OPEN) + n // 2]
-                nc.tensor.matmul_mx(out=bank[:, CHUNK * (n % 2) : CHUNK * (n % 2 + 1)],
+                bank, col, width = sums(c, n)
+                nc.tensor.matmul_mx(out=bank[:, col : col + width],
                                     lhsT=w3_codes[:, w0 : w0 + P].bitcast(FP8X4), lhsT_scale=w3_sc[:, w0 : w0 + P],
-                                    rhs=z_codes[(b, c)].bitcast(FP8X4),
-                                    rhs_scale=z_sc[:, T2 * b + CHUNK * c : T2 * b + CHUNK * (c + 1)],
-                                    start=(b == 0 and n % 2 == 0), stop=(b == PASSES - 1 and n % 2 == 1))
+                                    rhs=z_codes[(b, lo // HALF)][:, lo % HALF : lo % HALF + width].bitcast(FP8X4),
+                                    rhs_scale=z_sc[:, T2 * b + lo : T2 * b + hi],
+                                    start=(b == 0 and col == 0), stop=(b == PASSES - 1 and col + width == BANK))
 
         def finish(c):
             accumulate(c, 1)
-            stage = slot("stage_%d" % c, [P, 2, BANK], F32, "feat%d" % (c % FEAT_SLOTS))
-            for h in range(2):
-                copy = nc.vector.tensor_copy if c == CHUNKS - 1 and h == 1 else nc.scalar.copy
-                copy(stage[:, h, :], banks[2 * (c % OPEN) + h][:])
-                rows = out[2 * P * h : 2 * P * (h + 1), CHUNK * c : CHUNK * (c + 1)]
-                nc.sync.dma_start(rows.rearrange("(n p) c -> p n c", p=P),
-                                  stage[:, h, :].rearrange("p (n c) -> p n c", c=CHUNK))
+            width = spans[c].stop - spans[c].start
+            stage = slot("stage_%d" % c, [P, (N // P) * width], F32, "feat%d" % (c % FEAT_SLOTS))
+            per_bank = BANK // width
+            for h in range((N // P) // per_bank):
+                copy = nc.vector.tensor_copy if c == len(spans) - 1 else nc.scalar.copy
+                part = stage[:, BANK * h : BANK * (h + 1)]
+                copy(part, sums(c, per_bank * h)[0][:])
+                rows = out[per_bank * P * h : per_bank * P * (h + 1), spans[c]]
+                nc.sync.dma_start(rows.rearrange("(n p) c -> p n c", p=P), by_chunk(part, width))
+
+        def quantize_z(b, cols):
+            codes = z_codes[(b, cols.start // HALF)][:, cols.start % HALF : (cols.stop - 1) % HALF + 1]
+            nc.vector.quantize_mx(out=codes.bitcast(FP8X4), scales=z_sc[:, T2 * b + cols.start : T2 * b + cols.stop],
+                                  in_=woven[b][:, PACK * cols.start : PACK * cols.stop])
+
+        def weigh_last(c):
+            chunk, lo = divmod(spans[c].start, CHUNK)
+            width = spans[c].stop - spans[c].start
+            nc.vector.tensor_tensor(plane(last)[:, chunk, lo : lo + width], pages[last][:, spans[c]],
+                                    resp2[last][:, spans[c]], MULT)
+
+        def weave_pairs(c):
+            chunk, lo = divmod(spans[c].start, CHUNK)
+            width = spans[c].stop - spans[c].start
+            copy, word = (nc.scalar.copy, U32) if c in SCALAR_WEAVES else (nc.vector.tensor_copy, I32)
+            dst = woven[1][:, PACK * spans[c].start : PACK * spans[c].stop]
+            copy(dst.bitcast(word).rearrange("p (n h) -> p n h", h=2),
+                 pairs[:, chunk, :, :].bitcast(word)[:, :, lo : lo + width].rearrange("p h n -> p n h"))
 
         scatter(last_unit, feats[last_unit], 0, LAST_CUT)
-        early = slot("z_codes0_early", [P, HALF], U32, "z_codes0")
-        quantize_z(0, 0, OPEN, early[:])
-        for c in range(OPEN):
+        z_codes[(0, 0)] = slot("z_codes0_early", [P, HALF], U32, "z_codes0")
+        quantize_z(0, slice(0, HALF))
+        for c in range(early_spans):
             accumulate(c, 0)
         scatter(last_unit, last_feat, LAST_CUT, S)
-        late = slot("z_codes0_late", [P, HALF], U32, "page%d" % ((last - 1) % PAGE_SLOTS))
-        second = slot("z_codes1", [P, T2], U32, "resp%d" % ((last - 1) % RESP_SLOTS))
+        z_codes[(0, 1)] = slot("z_codes0_late", [P, HALF], U32, "page%d" % ((last - 1) % PAGE_SLOTS))
+        second = slot("z_codes1", [P, 2, HALF], U32, "resp%d" % ((last - 1) % RESP_SLOTS))
+        z_codes[(1, 0)], z_codes[(1, 1)] = second[:, 0, :], second[:, 1, :]
         woven[1] = slot("woven_1", [P, T2 * PACK], BF16, "planes")
-        weigh(nc.vector, last, 0, 1)
-        weigh(nc.vector, last, 1, 2)
-        weave_pairs(nc.vector.tensor_copy, I32, 0)
-        weave_pairs(nc.scalar.copy, U32, 1)
-        for c in range(CHUNKS):
-            if c + 2 < CHUNKS:
-                weigh(nc.vector, last, c + 2, c + 3)
-            quantize_z(1, c, c + 1, second[:, CHUNK * c : CHUNK * (c + 1)])
-            if c == 0:
-                weave_pairs(nc.scalar.copy, U32, 2)
-            elif c + 2 < CHUNKS:
-                weave_pairs(nc.vector.tensor_copy, I32, c + 2)
+        weigh_last(0)
+        weigh_last(1)
+        weave_pairs(0)
+        weave_pairs(1)
+        opened = early_spans
+        for c in range(len(spans)):
+            if c + 2 < len(spans):
+                weigh_last(c + 2)
+            quantize_z(1, spans[c])
+            if c + 2 < len(spans):
+                weave_pairs(c + 2)
             finish(c)
-            if c + OPEN < CHUNKS:
-                quantize_z(0, c + OPEN, c + OPEN + 1, late[:, CHUNK * c : CHUNK * (c + 1)])
-            if OPEN <= c + OPEN - 1 < CHUNKS:
-                accumulate(c + OPEN - 1, 0)
+            if 1 <= c <= OPEN:
+                quantize_z(0, slice(HALF + CHUNK * (c - 1), HALF + CHUNK * c))
+            while opened < len(spans) and c >= 1 and spans[opened].stop - HALF <= spans[c - 1].stop:
+                accumulate(opened, 0)
+                opened += 1

@@ -64,7 +64,7 @@ def tile_list_shower_deposit_weave_kernel(
 
         banks = [ps.tile([P, BANK], F32, name="bank%d" % j, tag="bank%d" % j) for j in range(BANKS)]
 
-        tab2_sc = slot("tab2_sc", [P, T], U8)
+        tab2_sc = slot("tab2_sc", [P, T], U8, "page3")
         tab_sc = slot("tab_sc", [P, T], U8)
         v1_sc = slot("v1_sc", [P, PASSES * S], U8)
         w1_sc_raw = slot("w1_sc_raw", [P, PASSES * H], U8)
@@ -122,9 +122,9 @@ def tile_list_shower_deposit_weave_kernel(
         w2_raw = [load_w2(0)]
         idx4 = load_list("idx4", offs4)
         load_gain("had", 0, BANK)
-        tab_w = [load_words("tab_w0", tab_words[0], "page1")]
+        tab_w = [load_words("tab_w0", tab_words[0], "resp1")]
         load_gain("had", 1)
-        tab_w.append(load_words("tab_w1", tab_words[1], "resp1"))
+        tab_w.append(load_words("tab_w1", tab_words[1], "page1"))
         load_gain("had", 2)
         w1_raw = slot("w1_raw", [P, PASSES * 2 * H], U8)
         nc.sync.dma_start(w1_raw[:].bitcast(I32).rearrange("p (a n) -> p a n", a=PASSES),
@@ -293,21 +293,25 @@ def tile_list_shower_deposit_weave_kernel(
         z_codes = {}
 
         first = []
-        for c, host in enumerate(("page3", "v1_w")):
+        for c, host in enumerate(("v1_w", "raw_1_1")):
             cols = slice(BANK * c, BANK * (c + 1))
             first.append(slot("raw_0_%d" % c, [P, BANK], F32, host))
             hadron_sums(banks[c], 0, cols)
             nc.scalar.activation(first[c][:], banks[c][:], ACT.Square)
-        produce(1)
-        produce(2)
         pages[0] = slot("page_0", [P, T2], F32, "page0")
+        feats[1] = slot("feat_1", [P, S], F32, "feat1")
         for c in range(S // BANK):
             cols = slice(BANK * c, BANK * (c + 1))
             nc.vector.tensor_tensor(pages[0][:].indirect(idx4[:, cols.start // PER_COL : cols.stop // PER_COL]),
                                     first[c][:], gains[("had", 0)][:, cols], MULT)
-        w1["v"] = slot("v1_w", [P, PASSES, S], U32)
-        for a in range(PASSES):
-            gather(w1["v"][:, a, :], tab_w[a][:].bitcast(U32), idx1, 0, S)
+            if c == 0:
+                w1["v"] = slot("v1_w", [P, PASSES, S], U32)
+            gather(w1["v"][:, c, :], tab_w[c][:].bitcast(U32), idx1, 0, S)
+            second_raw = slot("raw_1_%d" % c, [P, BANK], F32)
+            hadron_sums(banks[c], 1, cols)
+            nc.scalar.activation(second_raw[:], banks[c][:], ACT.Square)
+            nc.gpsimd.tensor_tensor(feats[1][:, cols], second_raw[:], gains[("had", 1)][:, cols], MULT)
+        produce(2)
         round_w2(nc.scalar.copy, 1, 0, PACK, "page3")
         scatter(1, feats[1], 0, S)
         reorder_w1(0)

@@ -39,7 +39,8 @@ CHUNKS = T2 // CHUNK
 OPEN = BANKS // 2
 EDGES = [0, CHUNK // 2] + list(range(CHUNK, T2, CHUNK)) + [T2 - CHUNK // 2, T2]
 SCALAR_WEAVES = (2, 3)
-LAST_CUT = BANK
+LAST_CUT = 3 * CHUNK
+EARLY = BANK
 
 
 def tile_list_shower_deposit_weave_kernel(
@@ -235,14 +236,14 @@ def tile_list_shower_deposit_weave_kernel(
                                     start=(a == 0), stop=(a == PASSES - 1))
 
         def produce_last():
-            raws = []
+            raw = slot("raw_last", [P, S], F32)
             for c in range(S // BANK):
-                photon_sums(banks[c], last, slice(BANK * c, BANK * (c + 1)))
-                raws.append(slot("raw_last%d" % c, [P, BANK], F32))
-                nc.scalar.activation(raws[c][:], banks[c][:], ACT.Relu)
-            feats[last_unit] = slot("feat_last", [P, BANK], F32, "z_codes0")
-            nc.gpsimd.tensor_tensor(feats[last_unit][:], raws[0][:], gains[("pho", last % PACK)][:, 0:BANK], MULT)
-            feats["rest"] = raws[1]
+                cols = slice(BANK * c, BANK * (c + 1))
+                photon_sums(banks[c], last, cols)
+                nc.scalar.activation(raw[:, cols], banks[c][:], ACT.Relu)
+            feats[last_unit] = slot("feat_last", [P, LAST_CUT], F32, "z_codes0")
+            nc.gpsimd.tensor_tensor(feats[last_unit][:], raw[:, 0:LAST_CUT], gains[("pho", last % PACK)][:, 0:LAST_CUT], MULT)
+            feats["rest"] = raw[:, LAST_CUT:S]
 
         def produce(u):
             stream, i = units[u]
@@ -350,10 +351,17 @@ def tile_list_shower_deposit_weave_kernel(
                     load_squared_resp(last)
                 if i == last - 1:
                     last_feat = slot("feat_rest", [P, S - LAST_CUT], F32, "page%d" % (i % PAGE_SLOTS))
-                    nc.gpsimd.tensor_tensor(last_feat[:], feats["rest"][:], gains[("pho", last % PACK)][:, LAST_CUT:S], MULT)
+                    nc.gpsimd.tensor_tensor(last_feat[:], feats["rest"], gains[("pho", last % PACK)][:, LAST_CUT:S], MULT)
 
         spans = [slice(lo, hi) for lo, hi in zip(EDGES, EDGES[1:])]
-        early_spans = EDGES.index(HALF)
+        early_spans = EDGES.index(EARLY)
+
+        def codes(b, cols):
+            if b == 0 and cols.start < EARLY:
+                return z_codes["early"][:, cols]
+            if b == 0:
+                return z_codes["late"][:, cols.start - EARLY : cols.stop - EARLY]
+            return z_codes["second"][:, cols]
 
         def sums(c, n):
             width = spans[c].stop - spans[c].start
@@ -367,7 +375,7 @@ def tile_list_shower_deposit_weave_kernel(
                 bank, col, width = sums(c, n)
                 nc.tensor.matmul_mx(out=bank[:, col : col + width],
                                     lhsT=w3_codes[:, w0 : w0 + P].bitcast(FP8X4), lhsT_scale=w3_sc[:, w0 : w0 + P],
-                                    rhs=z_codes[(b, lo // HALF)][:, lo % HALF : lo % HALF + width].bitcast(FP8X4),
+                                    rhs=codes(b, spans[c]).bitcast(FP8X4),
                                     rhs_scale=z_sc[:, T2 * b + lo : T2 * b + hi],
                                     start=(b == 0 and col == 0), stop=(b == PASSES - 1 and col + width == BANK))
 
@@ -384,8 +392,7 @@ def tile_list_shower_deposit_weave_kernel(
                 nc.sync.dma_start(rows.rearrange("(n p) c -> p n c", p=P), by_chunk(part, width))
 
         def quantize_z(b, cols):
-            codes = z_codes[(b, cols.start // HALF)][:, cols.start % HALF : (cols.stop - 1) % HALF + 1]
-            nc.vector.quantize_mx(out=codes.bitcast(FP8X4), scales=z_sc[:, T2 * b + cols.start : T2 * b + cols.stop],
+            nc.vector.quantize_mx(out=codes(b, cols).bitcast(FP8X4), scales=z_sc[:, T2 * b + cols.start : T2 * b + cols.stop],
                                   in_=woven[b][:, PACK * cols.start : PACK * cols.stop])
 
         def weigh_last(c):
@@ -403,14 +410,13 @@ def tile_list_shower_deposit_weave_kernel(
                  pairs[:, chunk, :, :].bitcast(word)[:, :, lo : lo + width].rearrange("p h n -> p n h"))
 
         scatter(last_unit, feats[last_unit], 0, LAST_CUT)
-        z_codes[(0, 0)] = slot("z_codes0_early", [P, HALF], U32, "z_codes0")
-        quantize_z(0, slice(0, HALF))
+        z_codes["early"] = slot("z_codes0_early", [P, EARLY], U32, "z_codes0")
+        quantize_z(0, slice(0, EARLY))
         for c in range(early_spans):
             accumulate(c, 0)
         scatter(last_unit, last_feat, LAST_CUT, S)
-        z_codes[(0, 1)] = slot("z_codes0_late", [P, HALF], U32, "page%d" % ((last - 1) % PAGE_SLOTS))
-        second = slot("z_codes1", [P, 2, HALF], U32, "resp%d" % ((last - 1) % RESP_SLOTS))
-        z_codes[(1, 0)], z_codes[(1, 1)] = second[:, 0, :], second[:, 1, :]
+        z_codes["late"] = slot("z_codes0_late", [P, T2 - EARLY], U32, "page%d" % ((last - 1) % PAGE_SLOTS))
+        z_codes["second"] = slot("z_codes1", [P, T2], U32, "resp%d" % ((last - 1) % RESP_SLOTS))
         woven[1] = slot("woven_1", [P, T2 * PACK], BF16, "planes")
         weigh_last(0)
         weigh_last(1)
@@ -424,8 +430,9 @@ def tile_list_shower_deposit_weave_kernel(
             if c + 2 < len(spans):
                 weave_pairs(c + 2)
             finish(c)
-            if 1 <= c <= OPEN:
-                quantize_z(0, slice(HALF + CHUNK * (c - 1), HALF + CHUNK * c))
-            while opened < len(spans) and c >= 1 and spans[opened].stop - HALF <= spans[c - 1].stop:
+            if EARLY + CHUNK * c < T2:
+                quantize_z(0, slice(EARLY + CHUNK * c, EARLY + CHUNK * (c + 1)))
+            while (opened < len(spans) and spans[opened].stop <= EARLY + CHUNK * (c + 1)
+                   and spans[opened].stop - HALF <= spans[c].start):
                 accumulate(opened, 0)
                 opened += 1

@@ -38,7 +38,7 @@ CHUNK = 256
 CHUNKS = T2 // CHUNK
 OPEN = BANKS // 2
 EDGES = [0, CHUNK // 2] + list(range(CHUNK, T2, CHUNK)) + [T2 - CHUNK // 2, T2]
-SCALAR_WEAVES = (2, 3)
+SCALAR_WEAVES = (1, 2, 3, 4)
 LAST_CUT = 3 * CHUNK
 EARLY = BANK
 
@@ -74,7 +74,7 @@ def tile_list_shower_deposit_weave_kernel(
         nc.vector.memset(rows_i32(tab_sc, QUAD, QUAD), 0)
         nc.vector.memset(rows_i32(tab_sc, 2 * QUAD, 2 * QUAD), 0)
         for tile in (v1_sc, w1_sc_raw, w3_sc):
-            nc.vector.memset(tile[:].bitcast(I32), 0)
+            nc.gpsimd.memset(tile[:].bitcast(I32), 0)
 
         def load_words(name, src, tag):
             words = slot(name, [P, T], I32, tag)

@@ -94,14 +94,13 @@ def tile_list_shower_deposit_weave_kernel(
 
         gains = {}
 
-        def load_gain(stream, t, step=S):
-            gain = slot("gain_%s%d" % (stream, t), [P, S], F32)
+        def load_gain(stream, t, lo=0, hi=S):
+            if (stream, t) not in gains:
+                gains[(stream, t)] = slot("gain_%s%d" % (stream, t), [P, S], F32)
             src = wg2 if stream == "had" else wg1
             rows = src.rearrange("(m t) j -> m t j", t=PACK)[:, t, :]
-            for lo in range(0, S, step):
-                for q in range(QUADS):
-                    nc.sync.dma_start(gain[QUAD * q : QUAD * (q + 1), lo : lo + step], rows[:, lo : lo + step])
-            gains[(stream, t)] = gain
+            for q in range(QUADS):
+                nc.sync.dma_start(gains[(stream, t)][QUAD * q : QUAD * (q + 1), lo:hi], rows[:, lo:hi])
 
         resp2 = {}
 
@@ -118,14 +117,16 @@ def tile_list_shower_deposit_weave_kernel(
         idx1 = load_list("idx1", offs)
         nc.sync.dma_start(rows_i32(tab_sc, 0, QUAD), tab_scales.rearrange("a g n -> g a n").bitcast(I32))
         idx2 = load_list("idx2", offs2)
-        tab2_w = load_words("tab2_w", tab2_words[0], "woven_0")
         load_scale_rows(tab2_sc, tab2_scales)
         w2_raw = [load_w2(0)]
+        tab2_w = load_words("tab2_w", tab2_words[0], "woven_0")
         idx4 = load_list("idx4", offs4)
-        load_gain("had", 0, BANK)
+        load_gain("had", 0, 0, BANK)
         tab_w = [load_words("tab_w0", tab_words[0], "resp1")]
-        load_gain("had", 1)
+        load_gain("had", 1, 0, BANK)
+        load_gain("had", 0, BANK, S)
         tab_w.append(load_words("tab_w1", tab_words[1], "page1"))
+        load_gain("had", 1, BANK, S)
         load_gain("had", 2)
         w1_raw = slot("w1_raw", [P, PASSES * 2 * H], U8)
         nc.sync.dma_start(w1_raw[:].bitcast(I32).rearrange("p (a n) -> p a n", a=PASSES),
@@ -164,15 +165,14 @@ def tile_list_shower_deposit_weave_kernel(
 
         v1_sc_rows = slot("v1_sc_rows", [P, S], U8)
         gather(v1_sc_rows[:], tab_sc[:], idx1, 0, S)
-        v2_w = slot("v2_w", [P, S], U32)
-        gather(v2_w[:], tab2_w[:].bitcast(U32), idx2, 0, S)
-        v2_sc = [slot("v2_sc0", [P, BANK], U8)]
-        gather(v2_sc[0][:], tab2_sc[:], idx2, 0, BANK)
-        round_w2(nc.gpsimd.tensor_copy, 0, 0, 1, "v2_sc1")
+        v2_sc = slot("v2_sc", [P, S], U8)
+        gather(v2_sc[:], tab2_sc[:], idx2, 0, S)
+        round_w2(nc.gpsimd.tensor_copy, 0, 0, 1, "v2_w")
         round_w2(nc.scalar.copy, 0, 1, PACK, "page0")
         quantize_w2(0, 0, 1)
-        v2_sc.append(slot("v2_sc1", [P, BANK], U8))
-        gather(v2_sc[1][:], tab2_sc[:], idx2, BANK, S)
+        v2_w = slot("v2_w", [P, S], U32)
+        for lo in range(0, S, BANK):
+            gather(v2_w[:, lo : lo + BANK], tab2_w[:].bitcast(U32), idx2, lo, lo + BANK)
         quantize_w2(0, 1, PACK)
         for q in range(QUADS):
             nc.sync.dma_start(rows_i32(v1_sc, QUAD * q, ROWS), rows_i32(v1_sc_rows, PASSES * ROWS * q, PASSES * ROWS))
@@ -223,7 +223,7 @@ def tile_list_shower_deposit_weave_kernel(
             m0 = P * i
             nc.tensor.matmul_mx(out=bank[:], lhsT=w2_codes[i // PACK][:, m0 % K_PASS : m0 % K_PASS + P].bitcast(FP8X4),
                                 lhsT_scale=w2_sc[:, m0 : m0 + P],
-                                rhs=v2_w[:, cols].bitcast(FP8X4), rhs_scale=v2_sc[cols.start // BANK][:],
+                                rhs=v2_w[:, cols].bitcast(FP8X4), rhs_scale=v2_sc[:, cols],
                                 start=True, stop=True)
 
         def photon_sums(bank, i, cols):

@@ -36,7 +36,6 @@ FEAT_SLOTS = 6
 AHEAD = 2
 CHUNK = 256
 CHUNKS = T2 // CHUNK
-OPEN = BANKS // 2
 EDGES = [0, CHUNK // 2] + list(range(CHUNK, T2, CHUNK)) + [T2 - CHUNK // 2, T2]
 SCALAR_WEAVES = (1, 2, 3, 4)
 LAST_CUT = 3 * CHUNK
@@ -63,6 +62,9 @@ def tile_list_shower_deposit_weave_kernel(
         def rows_i32(tile, first, count):
             return tile[first : first + count, :].bitcast(I32)
 
+        def split(ap, width):
+            return ap.rearrange("p (c n) -> p c n", n=width)
+
         banks = [ps.tile([P, BANK], F32, name="bank%d" % j, tag="bank%d" % j) for j in range(BANKS)]
 
         tab2_sc = slot("tab2_sc", [P, T], U8, "page3")
@@ -87,8 +89,8 @@ def tile_list_shower_deposit_weave_kernel(
                     rows_i32(tile, QUAD * q, ROWS).rearrange("r (a n) -> r a n", a=src.shape[0]),
                     src[:, ROWS * q : ROWS * (q + 1), :].rearrange("a r n -> r a n").bitcast(I32))
 
-        def load_w2(b):
-            raw = slot("w2_raw%d" % b, [P, PACK, K_PASS], F32, "resp%d" % (2 - 2 * b))
+        def load_w2(b, tag):
+            raw = slot("w2_raw%d" % b, [P, PACK, K_PASS], F32, tag)
             nc.sync.dma_start(raw[:], w2[:, K_PASS * b : K_PASS * (b + 1)].rearrange("(p j) c -> p j c", j=PACK))
             return raw
 
@@ -117,9 +119,9 @@ def tile_list_shower_deposit_weave_kernel(
         idx1 = load_list("idx1", offs)
         nc.sync.dma_start(rows_i32(tab_sc, 0, QUAD), tab_scales.rearrange("a g n -> g a n").bitcast(I32))
         idx2 = load_list("idx2", offs2)
-        load_scale_rows(tab2_sc, tab2_scales)
-        w2_raw = [load_w2(0)]
         tab2_w = load_words("tab2_w", tab2_words[0], "woven_0")
+        load_scale_rows(tab2_sc, tab2_scales)
+        w2_raw = [load_w2(0, "resp2")]
         idx4 = load_list("idx4", offs4)
         load_gain("had", 0, 0, BANK)
         tab_w = [load_words("tab_w0", tab_words[0], "resp1")]
@@ -133,14 +135,16 @@ def tile_list_shower_deposit_weave_kernel(
                           w1_words.rearrange("a p n -> p a n").bitcast(I32))
         load_scale_rows(w1_sc_raw, w1_scales)
         idx3 = load_list("idx3", offs3)
-        w2_raw.append(load_w2(1))
+        w2_raw.append(load_w2(1, "resp0"))
+
+        def entries(lst, lo, hi):
+            return lst[:, lo // PER_COL : hi // PER_COL]
 
         def gather(picked, window, lst, lo, hi):
-            nc.vector.tensor_copy(picked, window.indirect(lst[:, lo // PER_COL : hi // PER_COL]))
+            nc.vector.tensor_copy(picked, window.indirect(entries(lst, lo, hi)))
 
         w2_codes = {}
         w2_sc = slot("w2_sc", [P, H], U8)
-
         w2_bf = {}
 
         def round_w2(copy, b, t0, t1, tag):
@@ -165,17 +169,19 @@ def tile_list_shower_deposit_weave_kernel(
 
         v1_sc_rows = slot("v1_sc_rows", [P, S], U8)
         gather(v1_sc_rows[:], tab_sc[:], idx1, 0, S)
-        v2_sc = slot("v2_sc", [P, S], U8)
-        gather(v2_sc[:], tab2_sc[:], idx2, 0, S)
-        round_w2(nc.gpsimd.tensor_copy, 0, 0, 1, "v2_w")
+        v2_w = slot("v2_w", [P, S], U32)
+        gather(v2_w[:], tab2_w[:].bitcast(U32), idx2, 0, S)
+        v2_sc = [slot("v2_sc0", [P, BANK], U8)]
+        gather(v2_sc[0][:], tab2_sc[:], idx2, 0, BANK)
+        round_w2(nc.gpsimd.tensor_copy, 0, 0, 1, "v2_sc1")
         round_w2(nc.scalar.copy, 0, 1, PACK, "page0")
         quantize_w2(0, 0, 1)
-        v2_w = slot("v2_w", [P, S], U32)
-        for lo in range(0, S, BANK):
-            gather(v2_w[:, lo : lo + BANK], tab2_w[:].bitcast(U32), idx2, lo, lo + BANK)
+        v2_sc.append(slot("v2_sc1", [P, BANK], U8))
+        gather(v2_sc[1][:], tab2_sc[:], idx2, BANK, S)
         quantize_w2(0, 1, PACK)
         for q in range(QUADS):
             nc.sync.dma_start(rows_i32(v1_sc, QUAD * q, ROWS), rows_i32(v1_sc_rows, PASSES * ROWS * q, PASSES * ROWS))
+
         load_gain("pho", 0)
         load_gain("had", 3)
         for t in range(1, PACK):
@@ -185,45 +191,40 @@ def tile_list_shower_deposit_weave_kernel(
                           w3_words.rearrange("a p n i -> p a (n i)").bitcast(I32))
         load_scale_rows(w3_sc, w3_scales)
 
-        units = [("had", i) for i in range(LAG)]
         last = PAGES - 1
+        units = [("had", i) for i in range(LAG)]
         for i in range(LAG, last):
             units += [("had", i), ("pho", i - LAG)]
         units += [("pho", i) for i in range(last - LAG, last)] + [("had", last), ("pho", last)]
         last_unit = len(units) - 1
-
-        w1 = {}
-        feats = {}
+        first_photon = units.index(("pho", 0))
 
         planes = slot("planes", [P, PACK, T2], BF16)
         pairs = slot("pairs", [P, CHUNKS, 2, 2 * CHUNK], BF16)
 
-        def by_chunk(ap, width=CHUNK):
-            return ap.rearrange("p (c n) -> p c n", n=width)
-
         def plane(i):
             b, t = divmod(i, PACK)
             if b == 0:
-                return by_chunk(planes[:, t, :])
+                return split(planes[:, t, :], CHUNK)
             if t < 2:
                 return pairs[:, :, 1, CHUNK * t : CHUNK * (t + 1)]
             return pairs[:, :, 1, :].rearrange("p c (n e) -> p c n e", e=2)[:, :, :, t - 2]
 
-        raw_hosts = {3: "resp0", 4: "resp1", 6: "resp0", 8: "resp1", 10: "resp2", 12: "resp0"}
-        feat_hosts = {2: "resp2", 3: "w2_codes1"}
+        after_page = {u + 3: i for u, (stream, i) in enumerate(units) if stream == "pho" and i < PACK}
+        raw_hosts = {u: "resp%d" % (i % RESP_SLOTS) for u, i in after_page.items()}
+        raw_hosts.update({first_photon: "resp0", first_photon + 1: "resp1"})
+        feat_hosts = {first_photon - 1: "resp2", first_photon: "w2_codes1"}
 
         def staging(u):
             if u in raw_hosts:
-                return by_chunk(slot("raw_%d" % u, [P, S], F32, raw_hosts[u])[:], P)
-            if u >= AHEAD and units[u - AHEAD][0] == "pho":
-                return plane(units[u - AHEAD][1]).bitcast(F32)
-            return None
+                return split(slot("raw_%d" % u, [P, S], F32, raw_hosts[u])[:], P)
+            return plane(units[u - AHEAD][1]).bitcast(F32)
 
         def hadron_sums(bank, i, cols):
             m0 = P * i
             nc.tensor.matmul_mx(out=bank[:], lhsT=w2_codes[i // PACK][:, m0 % K_PASS : m0 % K_PASS + P].bitcast(FP8X4),
                                 lhsT_scale=w2_sc[:, m0 : m0 + P],
-                                rhs=v2_w[:, cols].bitcast(FP8X4), rhs_scale=v2_sc[:, cols],
+                                rhs=v2_w[:, cols].bitcast(FP8X4), rhs_scale=v2_sc[cols.start // BANK][:],
                                 start=True, stop=True)
 
         def photon_sums(bank, i, cols):
@@ -231,40 +232,40 @@ def tile_list_shower_deposit_weave_kernel(
                 c0 = H * a + P * i
                 nc.tensor.matmul_mx(out=bank[:], lhsT=w1_codes[:, 2 * c0 : 2 * (c0 + P)].bitcast(FP4X4),
                                     lhsT_scale=w1_sc[:, c0 : c0 + P],
-                                    rhs=w1["v"][:, a, cols].bitcast(FP8X4),
+                                    rhs=v1_w[:, a, cols].bitcast(FP8X4),
                                     rhs_scale=v1_sc[:, S * a + cols.start : S * a + cols.stop],
                                     start=(a == 0), stop=(a == PASSES - 1))
 
-        def produce_last():
-            raw = slot("raw_last", [P, S], F32)
-            for c in range(S // BANK):
-                cols = slice(BANK * c, BANK * (c + 1))
-                photon_sums(banks[c], last, cols)
-                nc.scalar.activation(raw[:, cols], banks[c][:], ACT.Relu)
-            feats[last_unit] = slot("feat_last", [P, LAST_CUT], F32, "z_codes0")
-            nc.gpsimd.tensor_tensor(feats[last_unit][:], raw[:, 0:LAST_CUT], gains[("pho", last % PACK)][:, 0:LAST_CUT], MULT)
-            feats["rest"] = raw[:, LAST_CUT:S]
+        halves = [slice(0, BANK), slice(BANK, S)]
+        feats = {}
 
         def produce(u):
             stream, i = units[u]
-            raw = staging(u)
-            tag = feat_hosts.get(u, "feat%d" % (u % FEAT_SLOTS))
-            feats[u] = slot("feat_%d" % u, [P, S], F32, tag)
-            if raw is None:
-                raw = by_chunk(feats[u][:], P)
-            for c in range(S // BANK):
-                cols = slice(BANK * c, BANK * (c + 1))
-                bank = banks[c]
+            in_place = u < first_photon
+            raw = None if in_place else staging(u)
+            feats[u] = slot("feat_%d" % u, [P, S], F32, feat_hosts.get(u, "feat%d" % (u % FEAT_SLOTS)))
+            if in_place:
+                raw = split(feats[u][:], P)
+            for bank, cols in zip(banks, halves):
                 if stream == "had":
                     hadron_sums(bank, i, cols)
                 else:
                     photon_sums(bank, i, cols)
-                nc.scalar.activation(raw[:, 4 * c : 4 * (c + 1), :], by_chunk(bank[:], P), ACT.Square if stream == "had" else ACT.Relu)
-            step = BANK if u == LAG + 1 else S
-            for lo in range(0, S, step):
-                cols = slice(lo, lo + step)
-                nc.gpsimd.tensor_tensor(by_chunk(feats[u][:, cols], P), raw[:, lo // P : (lo + step) // P, :],
-                                        by_chunk(gains[(stream, i % PACK)][:, cols], P), MULT)
+                nc.scalar.activation(raw[:, cols.start // P : cols.stop // P, :], split(bank[:], P),
+                                     ACT.Square if stream == "had" else ACT.Relu)
+            for cols in halves if u == first_photon else [slice(0, S)]:
+                nc.gpsimd.tensor_tensor(split(feats[u][:, cols], P), raw[:, cols.start // P : cols.stop // P, :],
+                                        split(gains[(stream, i % PACK)][:, cols], P), MULT)
+
+        def produce_last():
+            raw = slot("raw_last", [P, S], F32)
+            for bank, cols in zip(banks, halves):
+                photon_sums(bank, last, cols)
+                nc.scalar.activation(raw[:, cols], bank[:], ACT.Relu)
+            feats[last_unit] = slot("feat_last", [P, LAST_CUT], F32, "z_codes0")
+            nc.gpsimd.tensor_tensor(feats[last_unit][:], raw[:, 0:LAST_CUT],
+                                    gains[("pho", last % PACK)][:, 0:LAST_CUT], MULT)
+            return raw[:, LAST_CUT:S]
 
         pages = {}
 
@@ -273,41 +274,46 @@ def tile_list_shower_deposit_weave_kernel(
             if stream == "had":
                 pages[i] = slot("page_%d" % i, [P, T2], F32, "page%d" % (i % PAGE_SLOTS))
             lst = idx4 if stream == "had" else idx3
-            nc.vector.tensor_copy(pages[i][:].indirect(lst[:, lo // PER_COL : hi // PER_COL]), feat[:])
+            nc.vector.tensor_copy(pages[i][:].indirect(entries(lst, lo, hi)), feat[:])
 
-        def weigh(engine, i, c0, c1):
-            cols = slice(CHUNK * c0, CHUNK * c1)
-            engine.tensor_tensor(plane(i)[:, c0:c1, :], by_chunk(pages[i][:, cols]), by_chunk(resp2[i][:, cols]), MULT)
+        half_chunks = [slice(0, CHUNKS // 2), slice(CHUNKS // 2, CHUNKS)]
+
+        def weigh(i):
+            for chunks in half_chunks:
+                cols = slice(CHUNK * chunks.start, CHUNK * chunks.stop)
+                nc.gpsimd.tensor_tensor(plane(i)[:, chunks, :], split(pages[i][:, cols], CHUNK),
+                                        split(resp2[i][:, cols], CHUNK), MULT)
 
         woven = {}
 
-        def weave_planes(c0, c1):
-            dst = woven[0][:, PACK * CHUNK * c0 : PACK * CHUNK * c1]
-            nc.scalar.copy(dst.rearrange("p (n i t) -> p n t i", t=PACK, i=4),
-                           planes[:, :, CHUNK * c0 : CHUNK * c1].rearrange("p t (n i) -> p n t i", i=4))
+        def weave_first_pass():
+            woven[0] = slot("woven_0", [P, T2 * PACK], BF16)
+            for lo in range(0, T2, BANK):
+                nc.scalar.copy(
+                    woven[0][:, PACK * lo : PACK * (lo + BANK)].rearrange("p (n i t) -> p n t i", t=PACK, i=4),
+                    planes[:, :, lo : lo + BANK].rearrange("p t (n i) -> p n t i", i=4))
 
-        def pair_planes(c0, c1):
-            nc.scalar.copy(pairs[:, c0:c1, 0, :].rearrange("p c (n e) -> p c n e", e=2),
-                           pairs[:, c0:c1, 1, :].rearrange("p c (e n) -> p c n e", e=2))
+        def pair_planes():
+            for chunks in half_chunks:
+                nc.scalar.copy(pairs[:, chunks, 0, :].rearrange("p c (n e) -> p c n e", e=2),
+                               pairs[:, chunks, 1, :].rearrange("p c (e n) -> p c n e", e=2))
 
         z_sc = slot("z_sc", [P, PASSES * T2], U8)
         z_codes = {}
 
-        first = []
+        first_raw = []
         for c, host in enumerate(("v1_w", "raw_1_1")):
-            cols = slice(BANK * c, BANK * (c + 1))
-            first.append(slot("raw_0_%d" % c, [P, BANK], F32, host))
-            hadron_sums(banks[c], 0, cols)
-            nc.scalar.activation(first[c][:], banks[c][:], ACT.Square)
+            first_raw.append(slot("raw_0_%d" % c, [P, BANK], F32, host))
+            hadron_sums(banks[c], 0, halves[c])
+            nc.scalar.activation(first_raw[c][:], banks[c][:], ACT.Square)
         pages[0] = slot("page_0", [P, T2], F32, "page0")
         feats[1] = slot("feat_1", [P, S], F32, "feat1")
-        for c in range(S // BANK):
-            cols = slice(BANK * c, BANK * (c + 1))
-            nc.vector.tensor_tensor(pages[0][:].indirect(idx4[:, cols.start // PER_COL : cols.stop // PER_COL]),
-                                    first[c][:], gains[("had", 0)][:, cols], MULT)
+        for c, cols in enumerate(halves):
+            nc.vector.tensor_tensor(pages[0][:].indirect(entries(idx4, cols.start, cols.stop)),
+                                    first_raw[c][:], gains[("had", 0)][:, cols], MULT)
             if c == 0:
-                w1["v"] = slot("v1_w", [P, PASSES, S], U32)
-            gather(w1["v"][:, c, :], tab_w[c][:].bitcast(U32), idx1, 0, S)
+                v1_w = slot("v1_w", [P, PASSES, S], U32)
+            gather(v1_w[:, c, :], tab_w[c][:].bitcast(U32), idx1, 0, S)
             second_raw = slot("raw_1_%d" % c, [P, BANK], F32)
             hadron_sums(banks[c], 1, cols)
             nc.scalar.activation(second_raw[:], banks[c][:], ACT.Square)
@@ -316,45 +322,42 @@ def tile_list_shower_deposit_weave_kernel(
         round_w2(nc.scalar.copy, 1, 0, PACK, "page3")
         scatter(1, feats[1], 0, S)
         reorder_w1(0)
-        produce(3)
+        produce(first_photon)
         load_squared_resp(0)
+
         for u in range(AHEAD, last_unit):
             stream, i = units[u]
-            if u == 4:
+            ahead = u + AHEAD
+            if u == first_photon + 1:
                 quantize_w2(1, 0, PACK)
-            if u in (3, 5, 7):
-                reorder_w1(u // 2)
-            if u + AHEAD < last_unit - 1:
-                produce(u + AHEAD)
-            if u + AHEAD == last_unit - 2:
+            if stream == "pho" and i + 1 < PACK:
+                reorder_w1(i + 1)
+            if ahead < last_unit - 1:
+                produce(ahead)
+            if ahead == last_unit - 2:
                 produce(last_unit - 1)
-            if u + AHEAD == last_unit - 1:
-                produce_last()
-            if u == 2:
+            if ahead == last_unit - 1:
+                rest_raw = produce_last()
+            if ahead == first_photon + 1:
                 load_squared_resp(1)
-            if u in (4, 6, 8, 10):
-                load_squared_resp(u // 2 + 1)
+            if ahead in after_page:
+                load_squared_resp(after_page[ahead] + RESP_SLOTS)
             scatter(u, feats[u], 0, S)
-            if u == 2:
+            if u == first_photon - 1:
                 load_squared_resp(2)
             if stream == "pho":
-                for h in range(2):
-                    weigh(nc.gpsimd, i, OPEN * h, OPEN * (h + 1))
+                weigh(i)
                 if i == PACK:
-                    woven[0] = slot("woven_0", [P, T2 * PACK], BF16)
-                    for c in range(0, CHUNKS, 2):
-                        weave_planes(c, c + 2)
+                    weave_first_pass()
                 if i == PACK + 1:
-                    for h in range(2):
-                        pair_planes(OPEN * h, OPEN * (h + 1))
+                    pair_planes()
                 if i + RESP_SLOTS == last:
                     load_squared_resp(last)
                 if i == last - 1:
-                    last_feat = slot("feat_rest", [P, S - LAST_CUT], F32, "page%d" % (i % PAGE_SLOTS))
-                    nc.gpsimd.tensor_tensor(last_feat[:], feats["rest"], gains[("pho", last % PACK)][:, LAST_CUT:S], MULT)
+                    rest = slot("feat_rest", [P, S - LAST_CUT], F32, "page%d" % (i % PAGE_SLOTS))
+                    nc.gpsimd.tensor_tensor(rest[:], rest_raw, gains[("pho", last % PACK)][:, LAST_CUT:S], MULT)
 
         spans = [slice(lo, hi) for lo, hi in zip(EDGES, EDGES[1:])]
-        early_spans = EDGES.index(EARLY)
 
         def codes(b, cols):
             if b == 0 and cols.start < EARLY:
@@ -389,10 +392,11 @@ def tile_list_shower_deposit_weave_kernel(
                 part = stage[:, BANK * h : BANK * (h + 1)]
                 copy(part, sums(c, per_bank * h)[0][:])
                 rows = out[per_bank * P * h : per_bank * P * (h + 1), spans[c]]
-                nc.sync.dma_start(rows.rearrange("(n p) c -> p n c", p=P), by_chunk(part, width))
+                nc.sync.dma_start(rows.rearrange("(n p) c -> p n c", p=P), split(part, width))
 
         def quantize_z(b, cols):
-            nc.vector.quantize_mx(out=codes(b, cols).bitcast(FP8X4), scales=z_sc[:, T2 * b + cols.start : T2 * b + cols.stop],
+            nc.vector.quantize_mx(out=codes(b, cols).bitcast(FP8X4),
+                                  scales=z_sc[:, T2 * b + cols.start : T2 * b + cols.stop],
                                   in_=woven[b][:, PACK * cols.start : PACK * cols.stop])
 
         def weigh_last(c):
@@ -412,9 +416,10 @@ def tile_list_shower_deposit_weave_kernel(
         scatter(last_unit, feats[last_unit], 0, LAST_CUT)
         z_codes["early"] = slot("z_codes0_early", [P, EARLY], U32, "z_codes0")
         quantize_z(0, slice(0, EARLY))
-        for c in range(early_spans):
+        opened = EDGES.index(EARLY)
+        for c in range(opened):
             accumulate(c, 0)
-        scatter(last_unit, last_feat, LAST_CUT, S)
+        scatter(last_unit, rest, LAST_CUT, S)
         z_codes["late"] = slot("z_codes0_late", [P, T2 - EARLY], U32, "page%d" % ((last - 1) % PAGE_SLOTS))
         z_codes["second"] = slot("z_codes1", [P, T2], U32, "resp%d" % ((last - 1) % RESP_SLOTS))
         woven[1] = slot("woven_1", [P, T2 * PACK], BF16, "planes")
@@ -422,7 +427,6 @@ def tile_list_shower_deposit_weave_kernel(
         weigh_last(1)
         weave_pairs(0)
         weave_pairs(1)
-        opened = early_spans
         for c in range(len(spans)):
             if c + 2 < len(spans):
                 weigh_last(c + 2)
@@ -430,9 +434,10 @@ def tile_list_shower_deposit_weave_kernel(
             if c + 2 < len(spans):
                 weave_pairs(c + 2)
             finish(c)
-            if EARLY + CHUNK * c < T2:
-                quantize_z(0, slice(EARLY + CHUNK * c, EARLY + CHUNK * (c + 1)))
-            while (opened < len(spans) and spans[opened].stop <= EARLY + CHUNK * (c + 1)
+            quantised = EARLY + CHUNK * (c + 1)
+            if quantised <= T2:
+                quantize_z(0, slice(quantised - CHUNK, quantised))
+            while (opened < len(spans) and spans[opened].stop <= quantised
                    and spans[opened].stop - HALF <= spans[c].start):
                 accumulate(opened, 0)
                 opened += 1

@@ -15,6 +15,7 @@ FP8X4 = mybir.dt.float8_e4m3fn_x4
 FP4X4 = mybir.dt.float4_e2m1fn_x4
 ACT = mybir.ActivationFunctionType
 MULT = mybir.AluOpType.mult
+ADD = mybir.AluOpType.add
 
 P = 128
 PACK = 4
@@ -152,6 +153,9 @@ def tile_list_shower_deposit_weave_kernel(
             copy(w2_bf[(b, t0)][:].rearrange("p (t m j) -> p m t j", m=P, j=PACK),
                  w2_raw[b][:].rearrange("p j (m t) -> p m t j", t=PACK)[:, :, t0:t1, :])
 
+        def gpsimd_round(rounded, values):
+            nc.gpsimd.tensor_scalar(rounded, values, 1.0, 0.0, MULT, ADD)
+
         def quantize_w2(b, t0, t1):
             if b not in w2_codes:
                 w2_codes[b] = slot("w2_codes%d" % b, [P, K_PASS], U32)
@@ -162,8 +166,8 @@ def tile_list_shower_deposit_weave_kernel(
         w1_sc = slot("w1_sc", [P, PASSES * H], U8)
 
         def reorder_w1(t):
-            nc.gpsimd.tensor_copy(w1_codes[:].rearrange("p (g t m e) -> p g t m e", t=PACK, m=P, e=2)[:, :, t, :, :],
-                                  w1_raw[:].rearrange("p (g m t e) -> p g t m e", t=PACK, m=P, e=2)[:, :, t, :, :])
+            nc.gpsimd.tensor_copy(w1_codes[:].bitcast(U16).rearrange("p (g t m) -> p g t m", t=PACK, m=P)[:, :, t, :],
+                                  w1_raw[:].bitcast(U16).rearrange("p (g m t) -> p g t m", t=PACK, m=P)[:, :, t, :])
             nc.gpsimd.tensor_copy(w1_sc[:].rearrange("p (g t m) -> p g t m", t=PACK, m=P)[:, :, t, :],
                                   w1_sc_raw[:].rearrange("p (g m t) -> p g t m", t=PACK, m=P)[:, :, t, :])
 
@@ -173,7 +177,7 @@ def tile_list_shower_deposit_weave_kernel(
         gather(v2_w[:], tab2_w[:].bitcast(U32), idx2, 0, S)
         v2_sc = [slot("v2_sc0", [P, BANK], U8)]
         gather(v2_sc[0][:], tab2_sc[:], idx2, 0, BANK)
-        round_w2(nc.gpsimd.tensor_copy, 0, 0, 1, "v2_sc1")
+        round_w2(gpsimd_round, 0, 0, 1, "v2_sc1")
         round_w2(nc.scalar.copy, 0, 1, PACK, "page0")
         quantize_w2(0, 0, 1)
         v2_sc.append(slot("v2_sc1", [P, BANK], U8))

@@ -37,8 +37,7 @@ FEAT_SLOTS = 6
 AHEAD = 2
 CHUNK = 256
 CHUNKS = T2 // CHUNK
-EDGES = [0, CHUNK // 2] + list(range(CHUNK, T2, CHUNK)) + [T2 - CHUNK // 2, T2]
-SCALAR_WEAVES = (1, 2, 3, 4)
+EDGES = [0, CHUNK, BANK, 2 * BANK, 3 * BANK, T2]
 LAST_CUT = 3 * CHUNK
 EARLY = BANK
 
@@ -386,16 +385,25 @@ def tile_list_shower_deposit_weave_kernel(
                                     rhs_scale=z_sc[:, T2 * b + lo : T2 * b + hi],
                                     start=(b == 0 and col == 0), stop=(b == PASSES - 1 and col + width == BANK))
 
+        stages = []
+
         def finish(c):
             accumulate(c, 1)
             width = spans[c].stop - spans[c].start
-            stage = slot("stage_%d" % c, [P, (N // P) * width], F32, "feat%d" % (c % FEAT_SLOTS))
-            per_bank = BANK // width
-            for h in range((N // P) // per_bank):
-                copy = nc.vector.tensor_copy if c == len(spans) - 1 else nc.scalar.copy
-                part = stage[:, BANK * h : BANK * (h + 1)]
-                copy(part, sums(c, per_bank * h)[0][:])
-                rows = out[per_bank * P * h : per_bank * P * (h + 1), spans[c]]
+            for n in range(N // P):
+                bank, col, width = sums(c, n)
+                if n % 2 == 0:
+                    stages.append(slot("stage_%d_%d" % (c, n), [P, 2 * width], F32, "feat%d" % (len(stages) % FEAT_SLOTS)))
+                if width == BANK or (c == 0 and n < 2):
+                    count = 1
+                elif n % 2 == 0:
+                    count = 2
+                else:
+                    continue
+                part = stages[-1][:, width * (n % 2) : width * (n % 2 + count)]
+                copy = nc.vector.tensor_copy if c == len(spans) - 1 and n % 2 == 1 else nc.scalar.copy
+                copy(part, bank[:, col : col + count * width])
+                rows = out[P * n : P * (n + count), spans[c]]
                 nc.sync.dma_start(rows.rearrange("(n p) c -> p n c", p=P), split(part, width))
 
         def quantize_z(b, cols):
@@ -403,45 +411,52 @@ def tile_list_shower_deposit_weave_kernel(
                                   scales=z_sc[:, T2 * b + cols.start : T2 * b + cols.stop],
                                   in_=woven[b][:, PACK * cols.start : PACK * cols.stop])
 
-        def weigh_last(c):
-            chunk, lo = divmod(spans[c].start, CHUNK)
-            width = spans[c].stop - spans[c].start
-            nc.vector.tensor_tensor(plane(last)[:, chunk, lo : lo + width], pages[last][:, spans[c]],
-                                    resp2[last][:, spans[c]], MULT)
+        def weigh_last(k0, k1):
+            cols = slice(CHUNK * k0, CHUNK * k1)
+            nc.vector.tensor_tensor(plane(last)[:, k0:k1, :], split(pages[last][:, cols], CHUNK),
+                                    split(resp2[last][:, cols], CHUNK), MULT)
 
-        def weave_pairs(c):
-            chunk, lo = divmod(spans[c].start, CHUNK)
-            width = spans[c].stop - spans[c].start
-            copy, word = (nc.scalar.copy, U32) if c in SCALAR_WEAVES else (nc.vector.tensor_copy, I32)
-            dst = woven[1][:, PACK * spans[c].start : PACK * spans[c].stop]
-            copy(dst.bitcast(word).rearrange("p (n h) -> p n h", h=2),
-                 pairs[:, chunk, :, :].bitcast(word)[:, :, lo : lo + width].rearrange("p h n -> p n h"))
+        def weave_pairs(k0, k1, copy, word):
+            dst = woven[1][:, PACK * CHUNK * k0 : PACK * CHUNK * k1]
+            copy(dst.bitcast(word).rearrange("p (k n h) -> p k n h", h=2, n=CHUNK),
+                 pairs[:, k0:k1, :, :].bitcast(word).rearrange("p k h n -> p k n h"))
 
         scatter(last_unit, feats[last_unit], 0, LAST_CUT)
         z_codes["early"] = slot("z_codes0_early", [P, EARLY], U32, "z_codes0")
         quantize_z(0, slice(0, EARLY))
-        opened = EDGES.index(EARLY)
-        for c in range(opened):
-            accumulate(c, 0)
+        accumulate(0, 0)
+        accumulate(1, 0)
         scatter(last_unit, rest, LAST_CUT, S)
         z_codes["late"] = slot("z_codes0_late", [P, T2 - EARLY], U32, "page%d" % ((last - 1) % PAGE_SLOTS))
         z_codes["second"] = slot("z_codes1", [P, T2], U32, "resp%d" % ((last - 1) % RESP_SLOTS))
         woven[1] = slot("woven_1", [P, T2 * PACK], BF16, "planes")
-        weigh_last(0)
-        weigh_last(1)
-        weave_pairs(0)
-        weave_pairs(1)
-        for c in range(len(spans)):
-            if c + 2 < len(spans):
-                weigh_last(c + 2)
-            quantize_z(1, spans[c])
-            if c + 2 < len(spans):
-                weave_pairs(c + 2)
-            finish(c)
-            quantised = EARLY + CHUNK * (c + 1)
-            if quantised <= T2:
-                quantize_z(0, slice(quantised - CHUNK, quantised))
-            while (opened < len(spans) and spans[opened].stop <= quantised
-                   and spans[opened].stop - HALF <= spans[c].start):
-                accumulate(opened, 0)
-                opened += 1
+        on_vector = (nc.vector.tensor_copy, I32)
+        on_scalar = (nc.scalar.copy, U32)
+        weigh_last(0, 1)
+        weigh_last(1, 2)
+        weave_pairs(0, 1, *on_vector)
+        weave_pairs(1, 2, *on_scalar)
+        weigh_last(2, 3)
+        weave_pairs(2, 3, *on_scalar)
+        quantize_z(1, spans[0])
+        finish(0)
+        weigh_last(3, 4)
+        quantize_z(1, spans[1])
+        finish(1)
+        weave_pairs(3, 4, *on_vector)
+        quantize_z(0, spans[2])
+        accumulate(2, 0)
+        quantize_z(1, spans[2])
+        finish(2)
+        weigh_last(4, 6)
+        quantize_z(0, spans[3])
+        accumulate(3, 0)
+        weave_pairs(4, 6, *on_vector)
+        weigh_last(6, 8)
+        quantize_z(1, spans[3])
+        finish(3)
+        weave_pairs(6, 8, *on_vector)
+        quantize_z(0, spans[4])
+        accumulate(4, 0)
+        quantize_z(1, spans[4])
+        finish(4)

@@ -37,7 +37,7 @@ FEAT_SLOTS = 6
 AHEAD = 2
 CHUNK = 256
 CHUNKS = T2 // CHUNK
-EDGES = [0, CHUNK, BANK, 2 * BANK, 3 * BANK, T2]
+EDGES = [0, CHUNK, BANK, 2 * BANK, 3 * BANK, T2 - CHUNK, T2]
 LAST_CUT = 3 * CHUNK
 EARLY = BANK
 
@@ -401,7 +401,7 @@ def tile_list_shower_deposit_weave_kernel(
                 else:
                     continue
                 part = stages[-1][:, width * (n % 2) : width * (n % 2 + count)]
-                copy = nc.vector.tensor_copy if c == len(spans) - 1 and n % 2 == 1 else nc.scalar.copy
+                copy = nc.vector.tensor_copy if c == len(spans) - 1 and n == 0 else nc.scalar.copy
                 copy(part, bank[:, col : col + count * width])
                 rows = out[P * n : P * (n + count), spans[c]]
                 nc.sync.dma_start(rows.rearrange("(n p) c -> p n c", p=P), split(part, width))
@@ -452,11 +452,16 @@ def tile_list_shower_deposit_weave_kernel(
         quantize_z(0, spans[3])
         accumulate(3, 0)
         weave_pairs(4, 6, *on_vector)
-        weigh_last(6, 8)
+        weigh_last(6, 7)
         quantize_z(1, spans[3])
         finish(3)
-        weave_pairs(6, 8, *on_vector)
-        quantize_z(0, spans[4])
+        weave_pairs(6, 7, *on_vector)
+        quantize_z(0, slice(spans[4].start, T2))
         accumulate(4, 0)
+        accumulate(5, 0)
+        weigh_last(7, 8)
         quantize_z(1, spans[4])
         finish(4)
+        weave_pairs(7, 8, *on_vector)
+        quantize_z(1, spans[5])
+        finish(5)

@@ -29,6 +29,7 @@ PASSES = 2
 PAGES = H // P
 HALF = T2 // 2
 PER_COL = 16
+RUN = 4
 
 LAG = 2
 PAGE_SLOTS = LAG + 2
@@ -38,8 +39,6 @@ AHEAD = 2
 CHUNK = 256
 CHUNKS = T2 // CHUNK
 EDGES = [0, CHUNK, BANK, 2 * BANK, 3 * BANK, T2 - CHUNK, T2]
-LAST_CUT = 3 * CHUNK
-EARLY = BANK
 
 
 def tile_list_shower_deposit_weave_kernel(
@@ -106,15 +105,15 @@ def tile_list_shower_deposit_weave_kernel(
 
         resp2 = {}
 
-        def load_squared_resp(i):
+        def load_squared_resp(i, host=None):
             b, t = divmod(i, PACK)
             tile = slot("resp_%d" % i, [P, T2], F32, "resp%d" % (i % RESP_SLOTS))
             rows = resp[K_PASS * b : K_PASS * (b + 1), :].rearrange("(p t) n -> p t n", t=PACK)[:, t, :]
             nc.sync.dma_start(tile[:], rows)
+            resp2[i] = slot("resp2_%d" % i, [P, T2], F32, host) if host else tile
             for h in range(2):
                 cols = slice(HALF * h, HALF * (h + 1))
-                nc.scalar.activation(tile[:, cols], tile[:, cols], ACT.Square)
-            resp2[i] = tile
+                nc.scalar.activation(resp2[i][:, cols], tile[:, cols], ACT.Square)
 
         idx1 = load_list("idx1", offs)
         nc.sync.dma_start(rows_i32(tab_sc, 0, QUAD), tab_scales.rearrange("a g n -> g a n").bitcast(I32))
@@ -265,10 +264,8 @@ def tile_list_shower_deposit_weave_kernel(
             for bank, cols in zip(banks, halves):
                 photon_sums(bank, last, cols)
                 nc.scalar.activation(raw[:, cols], bank[:], ACT.Relu)
-            feats[last_unit] = slot("feat_last", [P, LAST_CUT], F32, "z_codes0")
-            nc.gpsimd.tensor_tensor(feats[last_unit][:], raw[:, 0:LAST_CUT],
-                                    gains[("pho", last % PACK)][:, 0:LAST_CUT], MULT)
-            return raw[:, LAST_CUT:S]
+            feats[last_unit] = slot("feat_last", [P, S], F32, "last_unit")
+            nc.gpsimd.tensor_tensor(feats[last_unit][:], raw[:], gains[("pho", last % PACK)][:], MULT)
 
         pages = {}
 
@@ -287,22 +284,19 @@ def tile_list_shower_deposit_weave_kernel(
                 nc.gpsimd.tensor_tensor(plane(i)[:, chunks, :], split(pages[i][:, cols], CHUNK),
                                         split(resp2[i][:, cols], CHUNK), MULT)
 
-        woven = {}
-
         def weave_first_pass():
-            woven[0] = slot("woven_0", [P, T2 * PACK], BF16)
+            woven = slot("woven_0", [P, T2 * PACK], BF16)
             for lo in range(0, T2, BANK):
                 nc.scalar.copy(
-                    woven[0][:, PACK * lo : PACK * (lo + BANK)].rearrange("p (n i t) -> p n t i", t=PACK, i=4),
-                    planes[:, :, lo : lo + BANK].rearrange("p t (n i) -> p n t i", i=4))
+                    woven[:, PACK * lo : PACK * (lo + BANK)].rearrange("p (n e t) -> p n t e", t=PACK, e=RUN),
+                    planes[:, :, lo : lo + BANK].rearrange("p t (n e) -> p n t e", e=RUN))
+            return woven
 
         def pair_planes():
             for chunks in half_chunks:
                 nc.scalar.copy(pairs[:, chunks, 0, :].rearrange("p c (n e) -> p c n e", e=2),
                                pairs[:, chunks, 1, :].rearrange("p c (e n) -> p c n e", e=2))
 
-        z_sc = slot("z_sc", [P, PASSES * T2], U8)
-        z_codes = {}
 
         first_raw = []
         for c, host in enumerate(("v1_w", "raw_1_1")):
@@ -340,7 +334,7 @@ def tile_list_shower_deposit_weave_kernel(
             if ahead == last_unit - 2:
                 produce(last_unit - 1)
             if ahead == last_unit - 1:
-                rest_raw = produce_last()
+                produce_last()
             if ahead == first_photon + 1:
                 load_squared_resp(1)
             if ahead in after_page:
@@ -351,23 +345,32 @@ def tile_list_shower_deposit_weave_kernel(
             if stream == "pho":
                 weigh(i)
                 if i == PACK:
-                    weave_first_pass()
+                    woven_first = weave_first_pass()
                 if i == PACK + 1:
                     pair_planes()
-                if i + RESP_SLOTS == last:
-                    load_squared_resp(last)
                 if i == last - 1:
-                    rest = slot("feat_rest", [P, S - LAST_CUT], F32, "page%d" % (i % PAGE_SLOTS))
-                    nc.gpsimd.tensor_tensor(rest[:], rest_raw, gains[("pho", last % PACK)][:, LAST_CUT:S], MULT)
+                    load_squared_resp(last, "page%d" % (i % PAGE_SLOTS))
 
         spans = [slice(lo, hi) for lo, hi in zip(EDGES, EDGES[1:])]
 
+        woven_hosts = ["planes", "page0", "page1", "resp2"]
+        first_hosts = ["last_unit"] + woven_hosts[:-1]
+        woven_quarters = [slot("woven_1_%d" % j, [P, PACK * BANK], BF16, host) for j, host in enumerate(woven_hosts)]
+        first_codes = []
+        second_codes = slot("z_codes1", [P, T2], U32, "resp%d" % ((last - 1) % RESP_SLOTS))
+        z_sc = [slot("z_sc%d" % b, [P, T2], U8) for b in range(PASSES)]
+
         def codes(b, cols):
-            if b == 0 and cols.start < EARLY:
-                return z_codes["early"][:, cols]
+            if b == 1:
+                return second_codes[:, cols]
+            j, first = divmod(cols.start, BANK)
+            return first_codes[j][:, first : first + cols.stop - cols.start]
+
+        def woven_cols(b, cols):
             if b == 0:
-                return z_codes["late"][:, cols.start - EARLY : cols.stop - EARLY]
-            return z_codes["second"][:, cols]
+                return woven_first[:, PACK * cols.start : PACK * cols.stop]
+            j, first = divmod(cols.start, BANK)
+            return woven_quarters[j][:, PACK * first : PACK * (first + cols.stop - cols.start)]
 
         def sums(c, n):
             width = spans[c].stop - spans[c].start
@@ -375,21 +378,18 @@ def tile_list_shower_deposit_weave_kernel(
             return banks[bank], col, width
 
         def accumulate(c, b):
-            lo, hi = spans[c].start, spans[c].stop
             for n in range(N // P):
                 w0 = N * b + P * n
                 bank, col, width = sums(c, n)
                 nc.tensor.matmul_mx(out=bank[:, col : col + width],
                                     lhsT=w3_codes[:, w0 : w0 + P].bitcast(FP8X4), lhsT_scale=w3_sc[:, w0 : w0 + P],
-                                    rhs=codes(b, spans[c]).bitcast(FP8X4),
-                                    rhs_scale=z_sc[:, T2 * b + lo : T2 * b + hi],
+                                    rhs=codes(b, spans[c]).bitcast(FP8X4), rhs_scale=z_sc[b][:, spans[c]],
                                     start=(b == 0 and col == 0), stop=(b == PASSES - 1 and col + width == BANK))
 
         stages = []
 
         def finish(c):
             accumulate(c, 1)
-            width = spans[c].stop - spans[c].start
             for n in range(N // P):
                 bank, col, width = sums(c, n)
                 if n % 2 == 0:
@@ -407,9 +407,15 @@ def tile_list_shower_deposit_weave_kernel(
                 nc.sync.dma_start(rows.rearrange("(n p) c -> p n c", p=P), split(part, width))
 
         def quantize_z(b, cols):
-            nc.vector.quantize_mx(out=codes(b, cols).bitcast(FP8X4),
-                                  scales=z_sc[:, T2 * b + cols.start : T2 * b + cols.stop],
-                                  in_=woven[b][:, PACK * cols.start : PACK * cols.stop])
+            nc.vector.quantize_mx(out=codes(b, cols).bitcast(FP8X4), scales=z_sc[b][:, cols], in_=woven_cols(b, cols))
+
+        def open_quarter(j):
+            cols = slice(BANK * j, BANK * (j + 1))
+            first_codes.append(slot("z_codes0_%d" % j, [P, BANK], U32, first_hosts[j]))
+            quantize_z(0, cols)
+            for c, span in enumerate(spans):
+                if span.start // BANK == j:
+                    accumulate(c, 0)
 
         def weigh_last(k0, k1):
             cols = slice(CHUNK * k0, CHUNK * k1)
@@ -417,19 +423,12 @@ def tile_list_shower_deposit_weave_kernel(
                                     split(resp2[last][:, cols], CHUNK), MULT)
 
         def weave_pairs(k0, k1, copy, word):
-            dst = woven[1][:, PACK * CHUNK * k0 : PACK * CHUNK * k1]
+            dst = woven_cols(1, slice(CHUNK * k0, CHUNK * k1))
             copy(dst.bitcast(word).rearrange("p (k n h) -> p k n h", h=2, n=CHUNK),
                  pairs[:, k0:k1, :, :].bitcast(word).rearrange("p k h n -> p k n h"))
 
-        scatter(last_unit, feats[last_unit], 0, LAST_CUT)
-        z_codes["early"] = slot("z_codes0_early", [P, EARLY], U32, "z_codes0")
-        quantize_z(0, slice(0, EARLY))
-        accumulate(0, 0)
-        accumulate(1, 0)
-        scatter(last_unit, rest, LAST_CUT, S)
-        z_codes["late"] = slot("z_codes0_late", [P, T2 - EARLY], U32, "page%d" % ((last - 1) % PAGE_SLOTS))
-        z_codes["second"] = slot("z_codes1", [P, T2], U32, "resp%d" % ((last - 1) % RESP_SLOTS))
-        woven[1] = slot("woven_1", [P, T2 * PACK], BF16, "planes")
+        scatter(last_unit, feats[last_unit], 0, S)
+        open_quarter(0)
         on_vector = (nc.vector.tensor_copy, I32)
         on_scalar = (nc.scalar.copy, U32)
         weigh_last(0, 1)
@@ -444,21 +443,17 @@ def tile_list_shower_deposit_weave_kernel(
         quantize_z(1, spans[1])
         finish(1)
         weave_pairs(3, 4, *on_vector)
-        quantize_z(0, spans[2])
-        accumulate(2, 0)
+        open_quarter(1)
         quantize_z(1, spans[2])
         finish(2)
         weigh_last(4, 6)
-        quantize_z(0, spans[3])
-        accumulate(3, 0)
+        open_quarter(2)
         weave_pairs(4, 6, *on_vector)
         weigh_last(6, 7)
         quantize_z(1, spans[3])
         finish(3)
         weave_pairs(6, 7, *on_vector)
-        quantize_z(0, slice(spans[4].start, T2))
-        accumulate(4, 0)
-        accumulate(5, 0)
+        open_quarter(3)
         weigh_last(7, 8)
         quantize_z(1, spans[4])
         finish(4)

@@ -387,6 +387,7 @@ def tile_list_shower_deposit_weave_kernel(
                                     start=(b == 0 and col == 0), stop=(b == PASSES - 1 and col + width == BANK))
 
         stages = []
+        vector_banks = [(len(spans) - 2, 2), (len(spans) - 1, 0)]
 
         def finish(c):
             accumulate(c, 1)
@@ -401,7 +402,7 @@ def tile_list_shower_deposit_weave_kernel(
                 else:
                     continue
                 part = stages[-1][:, width * (n % 2) : width * (n % 2 + count)]
-                copy = nc.vector.tensor_copy if c == len(spans) - 1 and n == 0 else nc.scalar.copy
+                copy = nc.vector.tensor_copy if (c, n) in vector_banks else nc.scalar.copy
                 copy(part, bank[:, col : col + count * width])
                 rows = out[P * n : P * (n + count), spans[c]]
                 nc.sync.dma_start(rows.rearrange("(n p) c -> p n c", p=P), split(part, width))
@@ -409,13 +410,13 @@ def tile_list_shower_deposit_weave_kernel(
         def quantize_z(b, cols):
             nc.vector.quantize_mx(out=codes(b, cols).bitcast(FP8X4), scales=z_sc[b][:, cols], in_=woven_cols(b, cols))
 
-        def open_quarter(j):
-            cols = slice(BANK * j, BANK * (j + 1))
-            first_codes.append(slot("z_codes0_%d" % j, [P, BANK], U32, first_hosts[j]))
-            quantize_z(0, cols)
-            for c, span in enumerate(spans):
-                if span.start // BANK == j:
-                    accumulate(c, 0)
+        def open_spans(c0, c1):
+            j, first = divmod(spans[c0].start, BANK)
+            if first == 0:
+                first_codes.append(slot("z_codes0_%d" % j, [P, BANK], U32, first_hosts[j]))
+            quantize_z(0, slice(spans[c0].start, spans[c1 - 1].stop))
+            for c in range(c0, c1):
+                accumulate(c, 0)
 
         def weigh_last(k0, k1):
             cols = slice(CHUNK * k0, CHUNK * k1)
@@ -428,7 +429,7 @@ def tile_list_shower_deposit_weave_kernel(
                  pairs[:, k0:k1, :, :].bitcast(word).rearrange("p k h n -> p k n h"))
 
         scatter(last_unit, feats[last_unit], 0, S)
-        open_quarter(0)
+        open_spans(0, 1)
         on_vector = (nc.vector.tensor_copy, I32)
         on_scalar = (nc.scalar.copy, U32)
         weigh_last(0, 1)
@@ -439,24 +440,25 @@ def tile_list_shower_deposit_weave_kernel(
         weave_pairs(2, 3, *on_scalar)
         quantize_z(1, spans[0])
         finish(0)
+        open_spans(1, 2)
         weigh_last(3, 4)
         quantize_z(1, spans[1])
         finish(1)
         weave_pairs(3, 4, *on_vector)
-        open_quarter(1)
+        open_spans(2, 3)
         quantize_z(1, spans[2])
         finish(2)
         weigh_last(4, 6)
-        open_quarter(2)
+        open_spans(3, 4)
         weave_pairs(4, 6, *on_vector)
         weigh_last(6, 7)
         quantize_z(1, spans[3])
         finish(3)
         weave_pairs(6, 7, *on_vector)
-        open_quarter(3)
+        open_spans(4, 6)
         weigh_last(7, 8)
         quantize_z(1, spans[4])
-        finish(4)
         weave_pairs(7, 8, *on_vector)
         quantize_z(1, spans[5])
+        finish(4)
         finish(5)

@@ -15,7 +15,6 @@ FP8X4 = mybir.dt.float8_e4m3fn_x4
 FP4X4 = mybir.dt.float4_e2m1fn_x4
 ACT = mybir.ActivationFunctionType
 MULT = mybir.AluOpType.mult
-ADD = mybir.AluOpType.add
 
 P = 128
 PACK = 4
@@ -36,6 +35,9 @@ PAGE_SLOTS = LAG + 2
 RESP_SLOTS = 3
 FEAT_SLOTS = 6
 AHEAD = 2
+FIRST = 256
+ARRIVAL = P - QUAD
+QUAD_ORDER = (0, 2, 1, 3)
 CHUNK = 256
 CHUNKS = T2 // CHUNK
 EDGES = [0, CHUNK, BANK, 2 * BANK, 3 * BANK, T2 - CHUNK, T2]
@@ -66,27 +68,42 @@ def tile_list_shower_deposit_weave_kernel(
 
         banks = [ps.tile([P, BANK], F32, name="bank%d" % j, tag="bank%d" % j) for j in range(BANKS)]
 
-        tab2_sc = slot("tab2_sc", [P, T], U8, "page3")
         tab_sc = slot("tab_sc", [P, T], U8)
-        v1_sc = slot("v1_sc", [P, PASSES * S], U8)
+        tab2_sc = slot("tab2_sc", [P, T], U8, "v1_w")
         w1_sc_raw = slot("w1_sc_raw", [P, PASSES * H], U8)
+        v1_sc = slot("v1_sc", [P, PASSES * S], U8)
+        v2_sc = slot("v2_sc", [P, S], U8)
         w3_sc = slot("w3_sc", [P, PASSES * N], U8)
-        nc.vector.memset(tab2_sc[:].bitcast(I32), 0)
-        nc.vector.memset(rows_i32(tab_sc, QUAD, QUAD), 0)
-        nc.vector.memset(rows_i32(tab_sc, 2 * QUAD, 2 * QUAD), 0)
-        for tile in (v1_sc, w1_sc_raw, w3_sc):
+        for tile in (tab_sc, tab2_sc):
+            nc.vector.memset(rows_i32(tile, 0, ARRIVAL), 0)
+        for tile in (w1_sc_raw, v1_sc):
             nc.gpsimd.memset(tile[:].bitcast(I32), 0)
+
+        def load_arrival_rows(tile, src):
+            nc.sync.dma_start(rows_i32(tile, ARRIVAL, QUAD), src.rearrange("a g n -> g a n").bitcast(I32))
+
+        def place_rows(queue, placed, arrived, passes):
+            for q in range(QUADS):
+                first = ARRIVAL + PASSES * ROWS * q
+                queue.dma_start(rows_i32(placed, QUAD * q, ROWS),
+                                arrived[first : first + PASSES * ROWS : PASSES // passes, :].bitcast(I32))
 
         def load_words(name, src, tag):
             words = slot(name, [P, T], I32, tag)
             nc.sync.dma_start(words[:], src.rearrange("p n i -> p (n i)").bitcast(I32))
             return words
 
-        def load_scale_rows(tile, src):
+        def load_scale_rows(queue, tile, src):
             for q in range(QUADS):
-                nc.sync.dma_start(
+                queue.dma_start(
                     rows_i32(tile, QUAD * q, ROWS).rearrange("r (a n) -> r a n", a=src.shape[0]),
                     src[:, ROWS * q : ROWS * (q + 1), :].rearrange("a r n -> r a n").bitcast(I32))
+
+        def load_w1(b):
+            raw = slot("w1_raw%d" % b, [P, PASSES * 2 * K_PASS], U8)
+            nc.sync.dma_start(raw[:].bitcast(I32).rearrange("p (a n) -> p a n", a=PASSES),
+                              w1_words[:, :, 2 * K_PASS * b : 2 * K_PASS * (b + 1)].rearrange("a p n -> p a n").bitcast(I32))
+            return raw
 
         def load_w2(b, tag):
             raw = slot("w2_raw%d" % b, [P, PACK, K_PASS], F32, tag)
@@ -100,7 +117,7 @@ def tile_list_shower_deposit_weave_kernel(
                 gains[(stream, t)] = slot("gain_%s%d" % (stream, t), [P, S], F32)
             src = wg2 if stream == "had" else wg1
             rows = src.rearrange("(m t) j -> m t j", t=PACK)[:, t, :]
-            for q in range(QUADS):
+            for q in QUAD_ORDER:
                 nc.sync.dma_start(gains[(stream, t)][QUAD * q : QUAD * (q + 1), lo:hi], rows[:, lo:hi])
 
         resp2 = {}
@@ -115,91 +132,73 @@ def tile_list_shower_deposit_weave_kernel(
                 cols = slice(HALF * h, HALF * (h + 1))
                 nc.scalar.activation(resp2[i][:, cols], tile[:, cols], ACT.Square)
 
-        idx1 = load_list("idx1", offs)
-        nc.sync.dma_start(rows_i32(tab_sc, 0, QUAD), tab_scales.rearrange("a g n -> g a n").bitcast(I32))
-        idx2 = load_list("idx2", offs2)
-        tab2_w = load_words("tab2_w", tab2_words[0], "woven_0")
-        load_scale_rows(tab2_sc, tab2_scales)
-        w2_raw = [load_w2(0, "resp2")]
-        idx4 = load_list("idx4", offs4)
-        load_gain("had", 0, 0, BANK)
-        tab_w = [load_words("tab_w0", tab_words[0], "resp1")]
-        load_gain("had", 1, 0, BANK)
-        load_gain("had", 0, BANK, S)
-        tab_w.append(load_words("tab_w1", tab_words[1], "page1"))
-        load_gain("had", 1, BANK, S)
-        load_gain("had", 2)
-        w1_raw = slot("w1_raw", [P, PASSES * 2 * H], U8)
-        nc.sync.dma_start(w1_raw[:].bitcast(I32).rearrange("p (a n) -> p a n", a=PASSES),
-                          w1_words.rearrange("a p n -> p a n").bitcast(I32))
-        load_scale_rows(w1_sc_raw, w1_scales)
-        idx3 = load_list("idx3", offs3)
-        w2_raw.append(load_w2(1, "resp0"))
-
         def entries(lst, lo, hi):
             return lst[:, lo // PER_COL : hi // PER_COL]
 
         def gather(picked, window, lst, lo, hi):
             nc.vector.tensor_copy(picked, window.indirect(entries(lst, lo, hi)))
 
-        w2_codes = {}
-        w2_sc = slot("w2_sc", [P, H], U8)
-        w2_bf = {}
-
-        def round_w2(copy, b, t0, t1, tag):
-            w2_bf[(b, t0)] = slot("w2_bf%d_%d" % (b, t0), [P, (t1 - t0) * K_PASS], BF16, tag)
-            copy(w2_bf[(b, t0)][:].rearrange("p (t m j) -> p m t j", m=P, j=PACK),
-                 w2_raw[b][:].rearrange("p j (m t) -> p m t j", t=PACK)[:, :, t0:t1, :])
-
-        def gpsimd_round(rounded, values):
-            nc.gpsimd.tensor_scalar(rounded, values, 1.0, 0.0, MULT, ADD)
-
-        def quantize_w2(b, t0, t1):
-            if b not in w2_codes:
-                w2_codes[b] = slot("w2_codes%d" % b, [P, K_PASS], U32)
-            nc.vector.quantize_mx(out=w2_codes[b][:, P * t0 : P * t1].bitcast(FP8X4),
-                                  scales=w2_sc[:, K_PASS * b + P * t0 : K_PASS * b + P * t1], in_=w2_bf[(b, t0)][:])
-
-        w1_codes = slot("w1_codes", [P, PASSES * 2 * H], U8)
-        w1_sc = slot("w1_sc", [P, PASSES * H], U8)
-
-        def reorder_w1(t):
-            nc.gpsimd.tensor_copy(w1_codes[:].bitcast(U16).rearrange("p (g t m) -> p g t m", t=PACK, m=P)[:, :, t, :],
-                                  w1_raw[:].bitcast(U16).rearrange("p (g m t) -> p g t m", t=PACK, m=P)[:, :, t, :])
-            nc.gpsimd.tensor_copy(w1_sc[:].rearrange("p (g t m) -> p g t m", t=PACK, m=P)[:, :, t, :],
-                                  w1_sc_raw[:].rearrange("p (g m t) -> p g t m", t=PACK, m=P)[:, :, t, :])
-
+        idx1 = load_list("idx1", offs)
+        load_arrival_rows(tab_sc, tab_scales)
+        idx2 = load_list("idx2", offs2)
+        load_arrival_rows(tab2_sc, tab2_scales.broadcast_to([PASSES, QUADS * ROWS, T]))
+        tab_w = [load_words("tab_w0", tab_words[0], "resp2"), load_words("tab_w1", tab_words[1], "page1")]
+        w1_raw = [load_w1(0)]
+        load_gain("pho", 0, 0, FIRST)
+        tab2_w = load_words("tab2_w", tab2_words[0], "page3")
+        load_scale_rows(nc.gpsimd, w1_sc_raw, w1_scales)
+        for tile in (v2_sc, w3_sc):
+            nc.gpsimd.memset(tile[:].bitcast(I32), 0)
         v1_sc_rows = slot("v1_sc_rows", [P, S], U8)
         gather(v1_sc_rows[:], tab_sc[:], idx1, 0, S)
-        v2_w = slot("v2_w", [P, S], U32)
-        gather(v2_w[:], tab2_w[:].bitcast(U32), idx2, 0, S)
-        v2_sc = [slot("v2_sc0", [P, BANK], U8)]
-        gather(v2_sc[0][:], tab2_sc[:], idx2, 0, BANK)
-        round_w2(gpsimd_round, 0, 0, 1, "v2_sc1")
-        round_w2(nc.scalar.copy, 0, 1, PACK, "page0")
-        quantize_w2(0, 0, 1)
-        v2_sc.append(slot("v2_sc1", [P, BANK], U8))
-        gather(v2_sc[1][:], tab2_sc[:], idx2, BANK, S)
-        quantize_w2(0, 1, PACK)
-        for q in range(QUADS):
-            nc.sync.dma_start(rows_i32(v1_sc, QUAD * q, ROWS), rows_i32(v1_sc_rows, PASSES * ROWS * q, PASSES * ROWS))
-
-        load_gain("pho", 0)
-        load_gain("had", 3)
+        place_rows(nc.scalar, v1_sc, v1_sc_rows, PASSES)
+        idx3 = load_list("idx3", offs3)
+        load_gain("pho", 1, 0, BANK)
+        load_gain("pho", 0, FIRST, S)
+        load_gain("pho", 1, BANK, S)
+        w2_raw = [load_w2(0, "resp0")]
+        w1_raw.append(load_w1(1))
+        load_gain("pho", 2)
+        w2_raw.append(load_w2(1, "resp1"))
+        idx4 = load_list("idx4", offs4)
+        load_gain("had", 0)
+        load_gain("pho", 3)
         for t in range(1, PACK):
-            load_gain("pho", t)
+            load_gain("had", t)
         w3_codes = slot("w3_codes", [P, PASSES * N], I32)
         nc.sync.dma_start(w3_codes[:].rearrange("p (a n) -> p a n", a=PASSES),
                           w3_words.rearrange("a p n i -> p a (n i)").bitcast(I32))
-        load_scale_rows(w3_sc, w3_scales)
+        load_scale_rows(nc.sync, w3_sc, w3_scales)
+
+        w1_parts = {}
+
+        def reorder_w1(b, t0, t1):
+            words = slot("w1_words%d_%d" % (b, t0), [P, (t1 - t0) * PASSES * 2 * P], U8)
+            nc.gpsimd.tensor_copy(words[:].bitcast(U16).rearrange("p (t a m) -> p t a m", a=PASSES, m=P),
+                                  w1_raw[b][:].bitcast(U16).rearrange("p (a m t) -> p t a m", t=PACK, m=P)[:, t0:t1, :, :])
+            scales = slot("w1_sc%d_%d" % (b, t0), [P, (t1 - t0) * PASSES * P], U8, "w1_raw%d" % b if t1 == PACK else None)
+            nc.gpsimd.tensor_copy(scales[:].rearrange("p (t a m) -> p t a m", a=PASSES, m=P),
+                                  w1_sc_raw[:].rearrange("p (a b m t) -> p b t a m", a=PASSES, t=PACK, m=P)[:, b, t0:t1, :, :])
+            for t in range(t0, t1):
+                w1_parts[PACK * b + t] = (words, scales, PASSES * P * (t - t0))
+
+        v2_sc_rows = slot("v2_sc_rows", [P, S], U8)
+        gather(v2_sc_rows[:], tab2_sc[:], idx2, 0, S)
+        v1_w = slot("v1_w", [P, PASSES, S], U32)
+        gather(v1_w[:, 0, :], tab_w[0][:].bitcast(U32), idx1, 0, S)
+        gather(v1_w[:, 1, :], tab_w[1][:].bitcast(U32), idx1, 0, S)
+        v2_w = slot("v2_w", [P, S], U32)
+        gather(v2_w[:], tab2_w[:].bitcast(U32), idx2, 0, S)
+        reorder_w1(0, 0, LAG)
+        reorder_w1(0, LAG, PACK)
 
         last = PAGES - 1
-        units = [("had", i) for i in range(LAG)]
+        units = [("pho", i) for i in range(LAG)]
         for i in range(LAG, last):
-            units += [("had", i), ("pho", i - LAG)]
-        units += [("pho", i) for i in range(last - LAG, last)] + [("had", last), ("pho", last)]
+            units += [("pho", i), ("had", i - LAG)]
+        units += [("had", i) for i in range(last - LAG, last)] + [("pho", last), ("had", last)]
         last_unit = len(units) - 1
-        first_photon = units.index(("pho", 0))
+        first_hadron = units.index(("had", 0))
 
         planes = slot("planes", [P, PACK, T2], BF16)
         pairs = slot("pairs", [P, CHUNKS, 2, 2 * CHUNK], BF16)
@@ -212,28 +211,27 @@ def tile_list_shower_deposit_weave_kernel(
                 return pairs[:, :, 1, CHUNK * t : CHUNK * (t + 1)]
             return pairs[:, :, 1, :].rearrange("p c (n e) -> p c n e", e=2)[:, :, :, t - 2]
 
-        after_page = {u + 3: i for u, (stream, i) in enumerate(units) if stream == "pho" and i < PACK}
+        after_page = {u + 3: i for u, (stream, i) in enumerate(units) if stream == "had" and i < PACK}
         raw_hosts = {u: "resp%d" % (i % RESP_SLOTS) for u, i in after_page.items()}
-        raw_hosts.update({first_photon: "resp0", first_photon + 1: "resp1"})
-        feat_hosts = {first_photon - 1: "resp2", first_photon: "w2_codes1"}
+        raw_hosts.update({first_hadron: "resp0", first_hadron + 1: "resp1"})
+        feat_hosts = {0: "w1_words1_0", 1: "w2_codes", first_hadron - 1: "resp2"}
 
         def staging(u):
             if u in raw_hosts:
                 return split(slot("raw_%d" % u, [P, S], F32, raw_hosts[u])[:], P)
             return plane(units[u - AHEAD][1]).bitcast(F32)
 
-        def hadron_sums(bank, i, cols):
+        def hadron_sums(sums, i, cols):
             m0 = P * i
-            nc.tensor.matmul_mx(out=bank[:], lhsT=w2_codes[i // PACK][:, m0 % K_PASS : m0 % K_PASS + P].bitcast(FP8X4),
-                                lhsT_scale=w2_sc[:, m0 : m0 + P],
-                                rhs=v2_w[:, cols].bitcast(FP8X4), rhs_scale=v2_sc[cols.start // BANK][:],
-                                start=True, stop=True)
+            nc.tensor.matmul_mx(out=sums, lhsT=w2_codes[:, m0 : m0 + P].bitcast(FP8X4), lhsT_scale=w2_sc[:, m0 : m0 + P],
+                                rhs=v2_w[:, cols].bitcast(FP8X4), rhs_scale=v2_sc[:, cols], start=True, stop=True)
 
-        def photon_sums(bank, i, cols):
+        def photon_sums(sums, i, cols):
+            words, scales, first = w1_parts[i]
             for a in range(PASSES):
-                c0 = H * a + P * i
-                nc.tensor.matmul_mx(out=bank[:], lhsT=w1_codes[:, 2 * c0 : 2 * (c0 + P)].bitcast(FP4X4),
-                                    lhsT_scale=w1_sc[:, c0 : c0 + P],
+                c0 = first + P * a
+                nc.tensor.matmul_mx(out=sums, lhsT=words[:, 2 * c0 : 2 * (c0 + P)].bitcast(FP4X4),
+                                    lhsT_scale=scales[:, c0 : c0 + P],
                                     rhs=v1_w[:, a, cols].bitcast(FP8X4),
                                     rhs_scale=v1_sc[:, S * a + cols.start : S * a + cols.stop],
                                     start=(a == 0), stop=(a == PASSES - 1))
@@ -243,38 +241,35 @@ def tile_list_shower_deposit_weave_kernel(
 
         def produce(u):
             stream, i = units[u]
-            in_place = u < first_photon
+            in_place = u < first_hadron
             raw = None if in_place else staging(u)
             feats[u] = slot("feat_%d" % u, [P, S], F32, feat_hosts.get(u, "feat%d" % (u % FEAT_SLOTS)))
             if in_place:
                 raw = split(feats[u][:], P)
             for bank, cols in zip(banks, halves):
                 if stream == "had":
-                    hadron_sums(bank, i, cols)
+                    hadron_sums(bank[:], i, cols)
                 else:
-                    photon_sums(bank, i, cols)
+                    photon_sums(bank[:], i, cols)
                 nc.scalar.activation(raw[:, cols.start // P : cols.stop // P, :], split(bank[:], P),
                                      ACT.Square if stream == "had" else ACT.Relu)
-            for cols in halves if u == first_photon else [slice(0, S)]:
-                nc.gpsimd.tensor_tensor(split(feats[u][:, cols], P), raw[:, cols.start // P : cols.stop // P, :],
-                                        split(gains[(stream, i % PACK)][:, cols], P), MULT)
+            nc.gpsimd.tensor_tensor(split(feats[u][:], P), raw, split(gains[(stream, i % PACK)][:], P), MULT)
 
         def produce_last():
             raw = slot("raw_last", [P, S], F32)
             for bank, cols in zip(banks, halves):
-                photon_sums(bank, last, cols)
-                nc.scalar.activation(raw[:, cols], bank[:], ACT.Relu)
+                hadron_sums(bank[:], last, cols)
+                nc.scalar.activation(raw[:, cols], bank[:], ACT.Square)
             feats[last_unit] = slot("feat_last", [P, S], F32, "last_unit")
-            nc.gpsimd.tensor_tensor(feats[last_unit][:], raw[:], gains[("pho", last % PACK)][:], MULT)
+            nc.gpsimd.tensor_tensor(feats[last_unit][:], raw[:], gains[("had", last % PACK)][:], MULT)
 
         pages = {}
 
-        def scatter(u, feat, lo, hi):
+        def scatter(u):
             stream, i = units[u]
-            if stream == "had":
+            if stream == "pho":
                 pages[i] = slot("page_%d" % i, [P, T2], F32, "page%d" % (i % PAGE_SLOTS))
-            lst = idx4 if stream == "had" else idx3
-            nc.vector.tensor_copy(pages[i][:].indirect(entries(lst, lo, hi)), feat[:])
+            nc.vector.tensor_copy(pages[i][:].indirect((idx4 if stream == "had" else idx3)[:]), feats[u][:])
 
         half_chunks = [slice(0, CHUNKS // 2), slice(CHUNKS // 2, CHUNKS)]
 
@@ -297,52 +292,51 @@ def tile_list_shower_deposit_weave_kernel(
                 nc.scalar.copy(pairs[:, chunks, 0, :].rearrange("p c (n e) -> p c n e", e=2),
                                pairs[:, chunks, 1, :].rearrange("p c (e n) -> p c n e", e=2))
 
-
-        first_raw = []
-        for c, host in enumerate(("v1_w", "raw_1_1")):
-            first_raw.append(slot("raw_0_%d" % c, [P, BANK], F32, host))
-            hadron_sums(banks[c], 0, halves[c])
-            nc.scalar.activation(first_raw[c][:], banks[c][:], ACT.Square)
-        pages[0] = slot("page_0", [P, T2], F32, "page0")
-        feats[1] = slot("feat_1", [P, S], F32, "feat1")
-        for c, cols in enumerate(halves):
-            nc.vector.tensor_tensor(pages[0][:].indirect(entries(idx4, cols.start, cols.stop)),
-                                    first_raw[c][:], gains[("had", 0)][:, cols], MULT)
-            if c == 0:
-                v1_w = slot("v1_w", [P, PASSES, S], U32)
-            gather(v1_w[:, c, :], tab_w[c][:].bitcast(U32), idx1, 0, S)
-            second_raw = slot("raw_1_%d" % c, [P, BANK], F32)
-            hadron_sums(banks[c], 1, cols)
-            nc.scalar.activation(second_raw[:], banks[c][:], ACT.Square)
-            nc.gpsimd.tensor_tensor(feats[1][:, cols], second_raw[:], gains[("had", 1)][:, cols], MULT)
+        for i in range(LAG):
+            feats[i] = slot("feat_%d" % i, [P, S], F32, feat_hosts.get(i, "feat%d" % i))
+        opening = [(0, 0, FIRST), (1, 0, BANK), (0, FIRST, S), (1, BANK, S)]
+        turn = 0
+        for i, lo, hi in opening:
+            for first in range(lo, hi, BANK):
+                cols = slice(first, min(first + BANK, hi))
+                sums = banks[turn % 2][:, 0 : cols.stop - cols.start]
+                turn += 1
+                photon_sums(sums, i, cols)
+                nc.scalar.activation(feats[i][:, cols], sums, ACT.Relu)
+            nc.gpsimd.tensor_tensor(feats[i][:, lo:hi], feats[i][:, lo:hi], gains[("pho", i)][:, lo:hi], MULT)
+            if lo == 0:
+                pages[i] = slot("page_%d" % i, [P, T2], F32, "page%d" % i)
+            nc.vector.tensor_copy(pages[i][:].indirect(entries(idx3, lo, hi)), feats[i][:, lo:hi])
         produce(2)
-        round_w2(nc.scalar.copy, 1, 0, PACK, "page3")
-        scatter(1, feats[1], 0, S)
-        reorder_w1(0)
-        produce(first_photon)
+        reorder_w1(1, 0, PACK)
+        w2_bf = slot("w2_bf", [P, PASSES, PACK * K_PASS], BF16, "page2")
+        for b in range(PASSES):
+            nc.scalar.copy(w2_bf[:, b, :].rearrange("p (t m j) -> p m t j", m=P, j=PACK),
+                           w2_raw[b][:].rearrange("p j (m t) -> p m t j", t=PACK))
+        place_rows(nc.sync, v2_sc, v2_sc_rows, 1)
+        w2_codes = slot("w2_codes", [P, H], U32)
+        w2_sc = slot("w2_sc", [P, H], U8)
+        nc.vector.quantize_mx(out=w2_codes[:].bitcast(FP8X4), scales=w2_sc[:], in_=w2_bf[:].rearrange("p b n -> p (b n)"))
+        produce(first_hadron)
         load_squared_resp(0)
 
         for u in range(AHEAD, last_unit):
             stream, i = units[u]
             ahead = u + AHEAD
-            if u == first_photon + 1:
-                quantize_w2(1, 0, PACK)
-            if stream == "pho" and i + 1 < PACK:
-                reorder_w1(i + 1)
             if ahead < last_unit - 1:
                 produce(ahead)
             if ahead == last_unit - 2:
                 produce(last_unit - 1)
             if ahead == last_unit - 1:
                 produce_last()
-            if ahead == first_photon + 1:
+            if ahead == first_hadron + 1:
                 load_squared_resp(1)
             if ahead in after_page:
                 load_squared_resp(after_page[ahead] + RESP_SLOTS)
-            scatter(u, feats[u], 0, S)
-            if u == first_photon - 1:
+            scatter(u)
+            if u == first_hadron - 1:
                 load_squared_resp(2)
-            if stream == "pho":
+            if stream == "had":
                 weigh(i)
                 if i == PACK:
                     woven_first = weave_first_pass()
@@ -428,7 +422,7 @@ def tile_list_shower_deposit_weave_kernel(
             copy(dst.bitcast(word).rearrange("p (k n h) -> p k n h", h=2, n=CHUNK),
                  pairs[:, k0:k1, :, :].bitcast(word).rearrange("p k h n -> p k n h"))
 
-        scatter(last_unit, feats[last_unit], 0, S)
+        scatter(last_unit)
         open_spans(0, 1)
         on_vector = (nc.vector.tensor_copy, I32)
         on_scalar = (nc.scalar.copy, U32)

@@ -142,27 +142,30 @@ def tile_list_shower_deposit_weave_kernel(
         load_arrival_rows(tab_sc, tab_scales)
         idx2 = load_list("idx2", offs2)
         load_arrival_rows(tab2_sc, tab2_scales.broadcast_to([PASSES, QUADS * ROWS, T]))
+        idx3 = load_list("idx3", offs3)
         tab_w = [load_words("tab_w0", tab_words[0], "resp2"), load_words("tab_w1", tab_words[1], "page1")]
         w1_raw = [load_w1(0)]
         load_gain("pho", 0, 0, FIRST)
+        load_gain("pho", 1, 0, BANK)
         tab2_w = load_words("tab2_w", tab2_words[0], "page3")
         load_scale_rows(nc.gpsimd, w1_sc_raw, w1_scales)
         for tile in (v2_sc, w3_sc):
             nc.gpsimd.memset(tile[:].bitcast(I32), 0)
         v1_sc_rows = slot("v1_sc_rows", [P, S], U8)
         gather(v1_sc_rows[:], tab_sc[:], idx1, 0, S)
-        place_rows(nc.scalar, v1_sc, v1_sc_rows, PASSES)
-        idx3 = load_list("idx3", offs3)
-        load_gain("pho", 1, 0, BANK)
+        place_rows(nc.gpsimd, v1_sc, v1_sc_rows, PASSES)
         load_gain("pho", 0, FIRST, S)
         load_gain("pho", 1, BANK, S)
         w2_raw = [load_w2(0, "resp0")]
-        w1_raw.append(load_w1(1))
+        v2_sc_rows = slot("v2_sc_rows", [P, S], U8)
+        gather(v2_sc_rows[:], tab2_sc[:], idx2, 0, S)
+        place_rows(nc.sync, v2_sc, v2_sc_rows, 1)
         load_gain("pho", 2)
-        w2_raw.append(load_w2(1, "resp1"))
         idx4 = load_list("idx4", offs4)
         load_gain("had", 0)
         load_gain("pho", 3)
+        w1_raw.append(load_w1(1))
+        w2_raw.append(load_w2(1, "woven_0"))
         for t in range(1, PACK):
             load_gain("had", t)
         w3_codes = slot("w3_codes", [P, PASSES * N], I32)
@@ -182,15 +185,11 @@ def tile_list_shower_deposit_weave_kernel(
             for t in range(t0, t1):
                 w1_parts[PACK * b + t] = (words, scales, PASSES * P * (t - t0))
 
-        v2_sc_rows = slot("v2_sc_rows", [P, S], U8)
-        gather(v2_sc_rows[:], tab2_sc[:], idx2, 0, S)
         v1_w = slot("v1_w", [P, PASSES, S], U32)
         gather(v1_w[:, 0, :], tab_w[0][:].bitcast(U32), idx1, 0, S)
-        gather(v1_w[:, 1, :], tab_w[1][:].bitcast(U32), idx1, 0, S)
-        v2_w = slot("v2_w", [P, S], U32)
-        gather(v2_w[:], tab2_w[:].bitcast(U32), idx2, 0, S)
+        gather(v1_w[:, 1, 0:FIRST], tab_w[1][:].bitcast(U32), idx1, 0, FIRST)
+        gather(v1_w[:, 1, FIRST:S], tab_w[1][:].bitcast(U32), idx1, FIRST, S)
         reorder_w1(0, 0, LAG)
-        reorder_w1(0, LAG, PACK)
 
         last = PAGES - 1
         units = [("pho", i) for i in range(LAG)]
@@ -214,7 +213,7 @@ def tile_list_shower_deposit_weave_kernel(
         after_page = {u + 3: i for u, (stream, i) in enumerate(units) if stream == "had" and i < PACK}
         raw_hosts = {u: "resp%d" % (i % RESP_SLOTS) for u, i in after_page.items()}
         raw_hosts.update({first_hadron: "resp0", first_hadron + 1: "resp1"})
-        feat_hosts = {0: "w1_words1_0", 1: "w2_codes", first_hadron - 1: "resp2"}
+        feat_hosts = {0: "w1_words1_0", 1: "w2_codes0", first_hadron - 1: "resp2", first_hadron: "w2_codes1"}
 
         def staging(u):
             if u in raw_hosts:
@@ -223,7 +222,7 @@ def tile_list_shower_deposit_weave_kernel(
 
         def hadron_sums(sums, i, cols):
             m0 = P * i
-            nc.tensor.matmul_mx(out=sums, lhsT=w2_codes[:, m0 : m0 + P].bitcast(FP8X4), lhsT_scale=w2_sc[:, m0 : m0 + P],
+            nc.tensor.matmul_mx(out=sums, lhsT=w2_codes[i // PACK][:, m0 % K_PASS : m0 % K_PASS + P].bitcast(FP8X4), lhsT_scale=w2_sc[:, m0 : m0 + P],
                                 rhs=v2_w[:, cols].bitcast(FP8X4), rhs_scale=v2_sc[:, cols], start=True, stop=True)
 
         def photon_sums(sums, i, cols):
@@ -292,37 +291,59 @@ def tile_list_shower_deposit_weave_kernel(
                 nc.scalar.copy(pairs[:, chunks, 0, :].rearrange("p c (n e) -> p c n e", e=2),
                                pairs[:, chunks, 1, :].rearrange("p c (e n) -> p c n e", e=2))
 
-        for i in range(LAG):
-            feats[i] = slot("feat_%d" % i, [P, S], F32, feat_hosts.get(i, "feat%d" % i))
-        opening = [(0, 0, FIRST), (1, 0, BANK), (0, FIRST, S), (1, BANK, S)]
-        turn = 0
-        for i, lo, hi in opening:
+        w2_bf = {}
+        w2_codes = {}
+        w2_sc = slot("w2_sc", [P, H], U8)
+
+        def round_w2(b, host):
+            w2_bf[b] = slot("w2_bf%d" % b, [P, PACK * K_PASS], BF16, host)
+            nc.scalar.copy(w2_bf[b][:].rearrange("p (t m j) -> p m t j", m=P, j=PACK),
+                           w2_raw[b][:].rearrange("p j (m t) -> p m t j", t=PACK))
+
+        def quantize_w2(b):
+            w2_codes[b] = slot("w2_codes%d" % b, [P, K_PASS], U32)
+            nc.vector.quantize_mx(out=w2_codes[b][:].bitcast(FP8X4), scales=w2_sc[:, K_PASS * b : K_PASS * (b + 1)],
+                                  in_=w2_bf[b][:])
+
+        turns = []
+
+        def raw_features(raw, i, lo, hi):
             for first in range(lo, hi, BANK):
                 cols = slice(first, min(first + BANK, hi))
-                sums = banks[turn % 2][:, 0 : cols.stop - cols.start]
-                turn += 1
+                sums = banks[len(turns) % 2][:, 0 : cols.stop - cols.start]
+                turns.append(cols)
                 photon_sums(sums, i, cols)
-                nc.scalar.activation(feats[i][:, cols], sums, ACT.Relu)
-            nc.gpsimd.tensor_tensor(feats[i][:, lo:hi], feats[i][:, lo:hi], gains[("pho", i)][:, lo:hi], MULT)
-            if lo == 0:
-                pages[i] = slot("page_%d" % i, [P, T2], F32, "page%d" % i)
-            nc.vector.tensor_copy(pages[i][:].indirect(entries(idx3, lo, hi)), feats[i][:, lo:hi])
+                nc.scalar.activation(raw[:, cols.start - lo : cols.stop - lo], sums, ACT.Relu)
+
+        cuts = [FIRST, BANK]
+        for i, host in enumerate(("raw_0", "v2_w")):
+            raw = slot("raw_%d" % i, [P, cuts[i]], F32, host)
+            raw_features(raw, i, 0, cuts[i])
+            pages[i] = slot("page_%d" % i, [P, T2], F32, "page%d" % i)
+            nc.vector.tensor_tensor(pages[i][:].indirect(entries(idx3, 0, cuts[i])),
+                                    raw[:], gains[("pho", i)][:, 0 : cuts[i]], MULT)
+        v2_w = slot("v2_w", [P, S], U32)
+        gather(v2_w[:], tab2_w[:].bitcast(U32), idx2, 0, S)
+        for i, host in enumerate(("w1_words0_2", "raw_0")):
+            raw = slot("rest_%d" % i, [P, S - cuts[i]], F32, host)
+            raw_features(raw, i, cuts[i], S)
+            feats[i] = slot("feat_%d" % i, [P, S - cuts[i]], F32, feat_hosts[i])
+            nc.gpsimd.tensor_tensor(feats[i][:], raw[:], gains[("pho", i)][:, cuts[i] : S], MULT)
+            nc.vector.tensor_copy(pages[i][:].indirect(entries(idx3, cuts[i], S)), feats[i][:])
+        reorder_w1(0, LAG, PACK)
         produce(2)
         reorder_w1(1, 0, PACK)
-        w2_bf = slot("w2_bf", [P, PASSES, PACK * K_PASS], BF16, "page2")
-        for b in range(PASSES):
-            nc.scalar.copy(w2_bf[:, b, :].rearrange("p (t m j) -> p m t j", m=P, j=PACK),
-                           w2_raw[b][:].rearrange("p j (m t) -> p m t j", t=PACK))
-        place_rows(nc.sync, v2_sc, v2_sc_rows, 1)
-        w2_codes = slot("w2_codes", [P, H], U32)
-        w2_sc = slot("w2_sc", [P, H], U8)
-        nc.vector.quantize_mx(out=w2_codes[:].bitcast(FP8X4), scales=w2_sc[:], in_=w2_bf[:].rearrange("p b n -> p (b n)"))
+        round_w2(0, "page2")
+        quantize_w2(0)
         produce(first_hadron)
+        round_w2(1, "page3")
         load_squared_resp(0)
 
         for u in range(AHEAD, last_unit):
             stream, i = units[u]
             ahead = u + AHEAD
+            if u == first_hadron + 1:
+                quantize_w2(1)
             if ahead < last_unit - 1:
                 produce(ahead)
             if ahead == last_unit - 2:

@@ -76,8 +76,8 @@ def tile_list_shower_deposit_weave_kernel(
         w3_sc = slot("w3_sc", [P, PASSES * N], U8)
         for tile in (tab_sc, tab2_sc):
             nc.vector.memset(rows_i32(tile, 0, ARRIVAL), 0)
-        for tile in (w1_sc_raw, v1_sc):
-            nc.gpsimd.memset(tile[:].bitcast(I32), 0)
+        nc.vector.memset(v1_sc[:].bitcast(I32), 0)
+        nc.gpsimd.memset(w1_sc_raw[:].bitcast(I32), 0)
 
         def load_arrival_rows(tile, src):
             nc.sync.dma_start(rows_i32(tile, ARRIVAL, QUAD), src.rearrange("a g n -> g a n").bitcast(I32))
@@ -149,11 +149,11 @@ def tile_list_shower_deposit_weave_kernel(
         load_gain("pho", 1, 0, BANK)
         tab2_w = load_words("tab2_w", tab2_words[0], "page3")
         load_scale_rows(nc.gpsimd, w1_sc_raw, w1_scales)
-        for tile in (v2_sc, w3_sc):
-            nc.gpsimd.memset(tile[:].bitcast(I32), 0)
         v1_sc_rows = slot("v1_sc_rows", [P, S], U8)
         gather(v1_sc_rows[:], tab_sc[:], idx1, 0, S)
         place_rows(nc.gpsimd, v1_sc, v1_sc_rows, PASSES)
+        for tile in (v2_sc, w3_sc):
+            nc.gpsimd.memset(tile[:].bitcast(I32), 0)
         load_gain("pho", 0, FIRST, S)
         load_gain("pho", 1, BANK, S)
         w2_raw = [load_w2(0, "resp0")]
@@ -189,7 +189,8 @@ def tile_list_shower_deposit_weave_kernel(
         gather(v1_w[:, 0, :], tab_w[0][:].bitcast(U32), idx1, 0, S)
         gather(v1_w[:, 1, 0:FIRST], tab_w[1][:].bitcast(U32), idx1, 0, FIRST)
         gather(v1_w[:, 1, FIRST:S], tab_w[1][:].bitcast(U32), idx1, FIRST, S)
-        reorder_w1(0, 0, LAG)
+        for t in range(LAG):
+            reorder_w1(0, t, t + 1)
 
         last = PAGES - 1
         units = [("pho", i) for i in range(LAG)]

@@ -69,7 +69,7 @@ def tile_list_shower_deposit_weave_kernel(
         banks = [ps.tile([P, BANK], F32, name="bank%d" % j, tag="bank%d" % j) for j in range(BANKS)]
 
         tab_sc = slot("tab_sc", [P, T], U8)
-        tab2_sc = slot("tab2_sc", [P, T], U8, "v1_w")
+        tab2_sc = slot("tab2_sc", [P, T], U8)
         w1_sc_raw = slot("w1_sc_raw", [P, PASSES * H], U8)
         v1_sc = slot("v1_sc", [P, PASSES * S], U8)
         v2_sc = slot("v2_sc", [P, S], U8)
@@ -163,9 +163,9 @@ def tile_list_shower_deposit_weave_kernel(
         load_gain("pho", 2)
         idx4 = load_list("idx4", offs4)
         load_gain("had", 0)
+        w2_raw.append(load_w2(1, "w2_codes1"))
         load_gain("pho", 3)
         w1_raw.append(load_w1(1))
-        w2_raw.append(load_w2(1, "woven_0"))
         for t in range(1, PACK):
             load_gain("had", t)
         w3_codes = slot("w3_codes", [P, PASSES * N], I32)
@@ -175,8 +175,8 @@ def tile_list_shower_deposit_weave_kernel(
 
         w1_parts = {}
 
-        def reorder_w1(b, t0, t1):
-            words = slot("w1_words%d_%d" % (b, t0), [P, (t1 - t0) * PASSES * 2 * P], U8)
+        def reorder_w1(b, t0, t1, host=None):
+            words = slot("w1_words%d_%d" % (b, t0), [P, (t1 - t0) * PASSES * 2 * P], U8, host)
             nc.gpsimd.tensor_copy(words[:].bitcast(U16).rearrange("p (t a m) -> p t a m", a=PASSES, m=P),
                                   w1_raw[b][:].bitcast(U16).rearrange("p (a m t) -> p t a m", t=PACK, m=P)[:, t0:t1, :, :])
             scales = slot("w1_sc%d_%d" % (b, t0), [P, (t1 - t0) * PASSES * P], U8, "w1_raw%d" % b if t1 == PACK else None)
@@ -189,8 +189,8 @@ def tile_list_shower_deposit_weave_kernel(
         gather(v1_w[:, 0, :], tab_w[0][:].bitcast(U32), idx1, 0, S)
         gather(v1_w[:, 1, 0:FIRST], tab_w[1][:].bitcast(U32), idx1, 0, FIRST)
         gather(v1_w[:, 1, FIRST:S], tab_w[1][:].bitcast(U32), idx1, FIRST, S)
-        for t in range(LAG):
-            reorder_w1(0, t, t + 1)
+        reorder_w1(0, 0, 1)
+        reorder_w1(0, 1, 2, "v2_w")
 
         last = PAGES - 1
         units = [("pho", i) for i in range(LAG)]
@@ -213,8 +213,8 @@ def tile_list_shower_deposit_weave_kernel(
 
         after_page = {u + 3: i for u, (stream, i) in enumerate(units) if stream == "had" and i < PACK}
         raw_hosts = {u: "resp%d" % (i % RESP_SLOTS) for u, i in after_page.items()}
-        raw_hosts.update({first_hadron: "resp0", first_hadron + 1: "resp1"})
-        feat_hosts = {0: "w1_words1_0", 1: "w2_codes0", first_hadron - 1: "resp2", first_hadron: "w2_codes1"}
+        raw_hosts.update({first_hadron - 1: "resp0", first_hadron: "resp0", first_hadron + 1: "w2_codes1"})
+        feat_hosts = {0: "feat0", 1: "w1_words1_0", first_hadron - 1: "resp2", first_hadron: "resp1"}
 
         def staging(u):
             if u in raw_hosts:
@@ -241,11 +241,8 @@ def tile_list_shower_deposit_weave_kernel(
 
         def produce(u):
             stream, i = units[u]
-            in_place = u < first_hadron
-            raw = None if in_place else staging(u)
+            raw = staging(u)
             feats[u] = slot("feat_%d" % u, [P, S], F32, feat_hosts.get(u, "feat%d" % (u % FEAT_SLOTS)))
-            if in_place:
-                raw = split(feats[u][:], P)
             for bank, cols in zip(banks, halves):
                 if stream == "had":
                     hadron_sums(bank[:], i, cols)
@@ -296,8 +293,8 @@ def tile_list_shower_deposit_weave_kernel(
         w2_codes = {}
         w2_sc = slot("w2_sc", [P, H], U8)
 
-        def round_w2(b, host):
-            w2_bf[b] = slot("w2_bf%d" % b, [P, PACK * K_PASS], BF16, host)
+        def round_w2(b):
+            w2_bf[b] = slot("w2_bf%d" % b, [P, PACK * K_PASS], BF16, "w2_bf")
             nc.scalar.copy(w2_bf[b][:].rearrange("p (t m j) -> p m t j", m=P, j=PACK),
                            w2_raw[b][:].rearrange("p j (m t) -> p m t j", t=PACK))
 
@@ -317,47 +314,48 @@ def tile_list_shower_deposit_weave_kernel(
                 nc.scalar.activation(raw[:, cols.start - lo : cols.stop - lo], sums, ACT.Relu)
 
         cuts = [FIRST, BANK]
-        for i, host in enumerate(("raw_0", "v2_w")):
-            raw = slot("raw_%d" % i, [P, cuts[i]], F32, host)
+        for i in range(LAG):
+            raw = slot("raw_%d" % i, [P, cuts[i]], F32)
             raw_features(raw, i, 0, cuts[i])
             pages[i] = slot("page_%d" % i, [P, T2], F32, "page%d" % i)
             nc.vector.tensor_tensor(pages[i][:].indirect(entries(idx3, 0, cuts[i])),
                                     raw[:], gains[("pho", i)][:, 0 : cuts[i]], MULT)
+        rests = []
+        for i, host in enumerate(("w1_words0_2", "w2_codes0")):
+            rests.append(slot("rest_%d" % i, [P, S - cuts[i]], F32, host))
+            raw_features(rests[i], i, cuts[i], S)
         v2_w = slot("v2_w", [P, S], U32)
         gather(v2_w[:], tab2_w[:].bitcast(U32), idx2, 0, S)
-        for i, host in enumerate(("w1_words0_2", "raw_0")):
-            raw = slot("rest_%d" % i, [P, S - cuts[i]], F32, host)
-            raw_features(raw, i, cuts[i], S)
+        for i, raw in enumerate(rests):
             feats[i] = slot("feat_%d" % i, [P, S - cuts[i]], F32, feat_hosts[i])
             nc.gpsimd.tensor_tensor(feats[i][:], raw[:], gains[("pho", i)][:, cuts[i] : S], MULT)
             nc.vector.tensor_copy(pages[i][:].indirect(entries(idx3, cuts[i], S)), feats[i][:])
         reorder_w1(0, LAG, PACK)
+        round_w2(0)
         produce(2)
         reorder_w1(1, 0, PACK)
-        round_w2(0, "page2")
         quantize_w2(0)
         produce(first_hadron)
-        round_w2(1, "page3")
+        round_w2(1)
         load_squared_resp(0)
 
         for u in range(AHEAD, last_unit):
             stream, i = units[u]
             ahead = u + AHEAD
-            if u == first_hadron + 1:
-                quantize_w2(1)
             if ahead < last_unit - 1:
                 produce(ahead)
             if ahead == last_unit - 2:
                 produce(last_unit - 1)
             if ahead == last_unit - 1:
                 produce_last()
-            if ahead == first_hadron + 1:
-                load_squared_resp(1)
             if ahead in after_page:
                 load_squared_resp(after_page[ahead] + RESP_SLOTS)
             scatter(u)
             if u == first_hadron - 1:
                 load_squared_resp(2)
+            if u == first_hadron:
+                quantize_w2(1)
+                load_squared_resp(1)
             if stream == "had":
                 weigh(i)
                 if i == PACK:

@@ -15,6 +15,7 @@ FP8X4 = mybir.dt.float8_e4m3fn_x4
 FP4X4 = mybir.dt.float4_e2m1fn_x4
 ACT = mybir.ActivationFunctionType
 MULT = mybir.AluOpType.mult
+ADD = mybir.AluOpType.add
 
 P = 128
 PACK = 4
@@ -156,22 +157,17 @@ def tile_list_shower_deposit_weave_kernel(
             nc.gpsimd.memset(tile[:].bitcast(I32), 0)
         load_gain("pho", 0, FIRST, S)
         load_gain("pho", 1, BANK, S)
-        w2_raw = [load_w2(0, "resp0")]
+        load_gain("pho", 2)
+        w2_raw = [load_w2(0, "page2")]
         v2_sc_rows = slot("v2_sc_rows", [P, S], U8)
         gather(v2_sc_rows[:], tab2_sc[:], idx2, 0, S)
         place_rows(nc.sync, v2_sc, v2_sc_rows, 1)
-        load_gain("pho", 2)
         idx4 = load_list("idx4", offs4)
         load_gain("had", 0)
-        w2_raw.append(load_w2(1, "w2_codes1"))
+        w2_raw.append(load_w2(1, "page3"))
         load_gain("pho", 3)
+        load_gain("had", 1)
         w1_raw.append(load_w1(1))
-        for t in range(1, PACK):
-            load_gain("had", t)
-        w3_codes = slot("w3_codes", [P, PASSES * N], I32)
-        nc.sync.dma_start(w3_codes[:].rearrange("p (a n) -> p a n", a=PASSES),
-                          w3_words.rearrange("a p n i -> p a (n i)").bitcast(I32))
-        load_scale_rows(nc.sync, w3_sc, w3_scales)
 
         w1_parts = {}
 
@@ -213,8 +209,8 @@ def tile_list_shower_deposit_weave_kernel(
 
         after_page = {u + 3: i for u, (stream, i) in enumerate(units) if stream == "had" and i < PACK}
         raw_hosts = {u: "resp%d" % (i % RESP_SLOTS) for u, i in after_page.items()}
-        raw_hosts.update({first_hadron - 1: "resp0", first_hadron: "resp0", first_hadron + 1: "w2_codes1"})
-        feat_hosts = {0: "feat0", 1: "w1_words1_0", first_hadron - 1: "resp2", first_hadron: "resp1"}
+        raw_hosts.update({first_hadron - 1: "w2_bf0", first_hadron + 1: "resp1"})
+        feat_hosts = {0: "feat0", 1: "feat1", first_hadron - 1: "resp2", first_hadron: "w1_words1_0"}
 
         def staging(u):
             if u in raw_hosts:
@@ -251,6 +247,14 @@ def tile_list_shower_deposit_weave_kernel(
                 nc.scalar.activation(raw[:, cols.start // P : cols.stop // P, :], split(bank[:], P),
                                      ACT.Square if stream == "had" else ACT.Relu)
             nc.gpsimd.tensor_tensor(split(feats[u][:], P), raw, split(gains[(stream, i % PACK)][:], P), MULT)
+
+        def produce_first_hadron():
+            feats[first_hadron] = slot("feat_had", [P, S], F32, feat_hosts[first_hadron])
+            for bank, cols, host in zip(banks, halves, ("resp0", "w2_bf1")):
+                raw = slot("raw_had_%d" % cols.start, [P, BANK], F32, host)
+                hadron_sums(bank[:], 0, cols)
+                nc.scalar.activation(raw[:], bank[:], ACT.Square)
+                nc.gpsimd.tensor_tensor(feats[first_hadron][:, cols], raw[:], gains[("had", 0)][:, cols], MULT)
 
         def produce_last():
             raw = slot("raw_last", [P, S], F32)
@@ -294,9 +298,14 @@ def tile_list_shower_deposit_weave_kernel(
         w2_sc = slot("w2_sc", [P, H], U8)
 
         def round_w2(b):
-            w2_bf[b] = slot("w2_bf%d" % b, [P, PACK * K_PASS], BF16, "w2_bf")
-            nc.scalar.copy(w2_bf[b][:].rearrange("p (t m j) -> p m t j", m=P, j=PACK),
-                           w2_raw[b][:].rearrange("p j (m t) -> p m t j", t=PACK))
+            w2_bf[b] = slot("w2_bf%d" % b, [P, PACK * K_PASS], BF16)
+            rounded = w2_bf[b][:].rearrange("p (t m j) -> p m t j", m=P, j=PACK)
+            values = w2_raw[b][:].rearrange("p j (m t) -> p m t j", t=PACK)
+            if b == 0:
+                nc.scalar.copy(rounded[:, :, 0:2, :], values[:, :, 0:2, :])
+                nc.gpsimd.tensor_scalar(rounded[:, :, 2:PACK, :], values[:, :, 2:PACK, :], 1.0, 0.0, MULT, ADD)
+            else:
+                nc.scalar.copy(rounded, values)
 
         def quantize_w2(b):
             w2_codes[b] = slot("w2_codes%d" % b, [P, K_PASS], U32)
@@ -321,7 +330,7 @@ def tile_list_shower_deposit_weave_kernel(
             nc.vector.tensor_tensor(pages[i][:].indirect(entries(idx3, 0, cuts[i])),
                                     raw[:], gains[("pho", i)][:, 0 : cuts[i]], MULT)
         rests = []
-        for i, host in enumerate(("w1_words0_2", "w2_codes0")):
+        for i, host in enumerate(("w1_words0_2", "rest_1")):
             rests.append(slot("rest_%d" % i, [P, S - cuts[i]], F32, host))
             raw_features(rests[i], i, cuts[i], S)
         v2_w = slot("v2_w", [P, S], U32)
@@ -331,13 +340,18 @@ def tile_list_shower_deposit_weave_kernel(
             nc.gpsimd.tensor_tensor(feats[i][:], raw[:], gains[("pho", i)][:, cuts[i] : S], MULT)
             nc.vector.tensor_copy(pages[i][:].indirect(entries(idx3, cuts[i], S)), feats[i][:])
         reorder_w1(0, LAG, PACK)
-        round_w2(0)
         produce(2)
-        reorder_w1(1, 0, PACK)
+        round_w2(0)
         quantize_w2(0)
-        produce(first_hadron)
+        produce_first_hadron()
         round_w2(1)
         load_squared_resp(0)
+        for t in range(2, PACK):
+            load_gain("had", t)
+        w3_codes = slot("w3_codes", [P, PASSES * N], I32)
+        nc.sync.dma_start(w3_codes[:].rearrange("p (a n) -> p a n", a=PASSES),
+                          w3_words.rearrange("a p n i -> p a (n i)").bitcast(I32))
+        load_scale_rows(nc.sync, w3_sc, w3_scales)
 
         for u in range(AHEAD, last_unit):
             stream, i = units[u]
@@ -348,6 +362,8 @@ def tile_list_shower_deposit_weave_kernel(
                 produce(last_unit - 1)
             if ahead == last_unit - 1:
                 produce_last()
+            if ahead == first_hadron + 1:
+                load_squared_resp(1)
             if ahead in after_page:
                 load_squared_resp(after_page[ahead] + RESP_SLOTS)
             scatter(u)
@@ -355,7 +371,7 @@ def tile_list_shower_deposit_weave_kernel(
                 load_squared_resp(2)
             if u == first_hadron:
                 quantize_w2(1)
-                load_squared_resp(1)
+                reorder_w1(1, 0, PACK)
             if stream == "had":
                 weigh(i)
                 if i == PACK:

@@ -81,7 +81,7 @@ def tile_list_shower_deposit_weave_kernel(
         nc.gpsimd.memset(w1_sc_raw[:].bitcast(I32), 0)
 
         def load_arrival_rows(tile, src):
-            nc.sync.dma_start(rows_i32(tile, ARRIVAL, QUAD), src.rearrange("a g n -> g a n").bitcast(I32))
+            nc.scalar.dma_start(rows_i32(tile, ARRIVAL, QUAD), src.rearrange("a g n -> g a n").bitcast(I32))
 
         def place_rows(queue, placed, arrived, passes):
             for q in range(QUADS):
@@ -143,8 +143,9 @@ def tile_list_shower_deposit_weave_kernel(
         load_arrival_rows(tab_sc, tab_scales)
         idx2 = load_list("idx2", offs2)
         load_arrival_rows(tab2_sc, tab2_scales.broadcast_to([PASSES, QUADS * ROWS, T]))
+        tab_w = [load_words("tab_w0", tab_words[0], "resp2")]
         idx3 = load_list("idx3", offs3)
-        tab_w = [load_words("tab_w0", tab_words[0], "resp2"), load_words("tab_w1", tab_words[1], "page1")]
+        tab_w.append(load_words("tab_w1", tab_words[1], "page1"))
         w1_raw = [load_w1(0)]
         load_gain("pho", 0, 0, FIRST)
         load_gain("pho", 1, 0, BANK)
@@ -384,10 +385,10 @@ def tile_list_shower_deposit_weave_kernel(
         spans = [slice(lo, hi) for lo, hi in zip(EDGES, EDGES[1:])]
 
         woven_hosts = ["planes", "page0", "page1", "resp2"]
-        first_hosts = ["last_unit"] + woven_hosts[:-1]
+        first_hosts = ["resp%d" % ((last - 1) % RESP_SLOTS)] + woven_hosts[:-1]
         woven_quarters = [slot("woven_1_%d" % j, [P, PACK * BANK], BF16, host) for j, host in enumerate(woven_hosts)]
         first_codes = []
-        second_codes = slot("z_codes1", [P, T2], U32, "resp%d" % ((last - 1) % RESP_SLOTS))
+        second_codes = slot("z_codes1", [P, T2], U32, "v1_w")
         z_sc = [slot("z_sc%d" % b, [P, T2], U8) for b in range(PASSES)]
 
         def codes(b, cols):
@@ -485,10 +486,10 @@ def tile_list_shower_deposit_weave_kernel(
         quantize_z(1, spans[3])
         finish(3)
         weave_pairs(6, 7, *on_vector)
-        open_spans(4, 6)
         weigh_last(7, 8)
-        quantize_z(1, spans[4])
+        open_spans(4, 6)
         weave_pairs(7, 8, *on_vector)
+        quantize_z(1, spans[4])
         quantize_z(1, spans[5])
         finish(4)
         finish(5)

@@ -210,7 +210,7 @@ def tile_list_shower_deposit_weave_kernel(
 
         after_page = {u + 3: i for u, (stream, i) in enumerate(units) if stream == "had" and i < PACK}
         raw_hosts = {u: "resp%d" % (i % RESP_SLOTS) for u, i in after_page.items()}
-        raw_hosts.update({first_hadron - 1: "w2_bf0", first_hadron + 1: "resp1"})
+        raw_hosts.update({first_hadron - 1: "w2_bf0", first_hadron + 1: "resp1", last_unit - 1: "woven_0"})
         feat_hosts = {0: "feat0", 1: "feat1", first_hadron - 1: "resp2", first_hadron: "w1_words1_0"}
 
         def staging(u):
@@ -275,18 +275,18 @@ def tile_list_shower_deposit_weave_kernel(
 
         half_chunks = [slice(0, CHUNKS // 2), slice(CHUNKS // 2, CHUNKS)]
 
-        def weigh(i):
+        def weigh(i, rounded):
             for chunks in half_chunks:
                 cols = slice(CHUNK * chunks.start, CHUNK * chunks.stop)
-                nc.gpsimd.tensor_tensor(plane(i)[:, chunks, :], split(pages[i][:, cols], CHUNK),
+                nc.gpsimd.tensor_tensor(rounded[:, chunks, :], split(pages[i][:, cols], CHUNK),
                                         split(resp2[i][:, cols], CHUNK), MULT)
 
         def weave_first_pass():
             woven = slot("woven_0", [P, T2 * PACK], BF16)
-            for lo in range(0, T2, BANK):
+            for lo, hi in zip(EDGES, EDGES[1:]):
                 nc.scalar.copy(
-                    woven[:, PACK * lo : PACK * (lo + BANK)].rearrange("p (n e t) -> p n t e", t=PACK, e=RUN),
-                    planes[:, :, lo : lo + BANK].rearrange("p t (n e) -> p n t e", e=RUN))
+                    woven[:, PACK * lo : PACK * hi].rearrange("p (n e t) -> p n t e", t=PACK, e=RUN),
+                    planes[:, :, lo:hi].rearrange("p t (n e) -> p n t e", e=RUN))
             return woven
 
         def pair_planes():
@@ -374,28 +374,34 @@ def tile_list_shower_deposit_weave_kernel(
                 quantize_w2(1)
                 reorder_w1(1, 0, PACK)
             if stream == "had":
-                weigh(i)
+                if i == last - 1:
+                    sixth = split(slot("plane_6", [P, T2], BF16, "v1_w")[:], CHUNK)
+                    weigh(i, sixth)
+                    for chunks in half_chunks:
+                        nc.scalar.copy(plane(i)[:, chunks, :], sixth[:, chunks, :])
+                else:
+                    weigh(i, plane(i))
                 if i == PACK:
                     woven_first = weave_first_pass()
                 if i == PACK + 1:
                     pair_planes()
                 if i == last - 1:
-                    load_squared_resp(last, "page%d" % (i % PAGE_SLOTS))
+                    load_squared_resp(last, "v1_w")
 
         spans = [slice(lo, hi) for lo, hi in zip(EDGES, EDGES[1:])]
 
         woven_hosts = ["planes", "page0", "page1", "resp2"]
-        first_hosts = ["resp%d" % ((last - 1) % RESP_SLOTS)] + woven_hosts[:-1]
+        first_hosts = {0: None, 1: "resp%d" % ((last - 1) % RESP_SLOTS), 2: "planes", 3: "page0", 4: "page1"}
         woven_quarters = [slot("woven_1_%d" % j, [P, PACK * BANK], BF16, host) for j, host in enumerate(woven_hosts)]
-        first_codes = []
-        second_codes = slot("z_codes1", [P, T2], U32, "v1_w")
+        first_codes = {}
+        second_codes = slot("z_codes1", [P, T2], U32, "page%d" % ((last - 1) % PAGE_SLOTS))
         z_sc = [slot("z_sc%d" % b, [P, T2], U8) for b in range(PASSES)]
 
         def codes(b, cols):
             if b == 1:
                 return second_codes[:, cols]
-            j, first = divmod(cols.start, BANK)
-            return first_codes[j][:, first : first + cols.stop - cols.start]
+            first = max(lo for lo in first_codes if lo <= cols.start)
+            return first_codes[first][:, cols.start - first : cols.stop - first]
 
         def woven_cols(b, cols):
             if b == 0:
@@ -442,10 +448,9 @@ def tile_list_shower_deposit_weave_kernel(
             nc.vector.quantize_mx(out=codes(b, cols).bitcast(FP8X4), scales=z_sc[b][:, cols], in_=woven_cols(b, cols))
 
         def open_spans(c0, c1):
-            j, first = divmod(spans[c0].start, BANK)
-            if first == 0:
-                first_codes.append(slot("z_codes0_%d" % j, [P, BANK], U32, first_hosts[j]))
-            quantize_z(0, slice(spans[c0].start, spans[c1 - 1].stop))
+            cols = slice(spans[c0].start, spans[c1 - 1].stop)
+            first_codes[cols.start] = slot("z_codes0_%d" % c0, [P, cols.stop - cols.start], U32, first_hosts[c0])
+            quantize_z(0, cols)
             for c in range(c0, c1):
                 accumulate(c, 0)
 
@@ -459,8 +464,9 @@ def tile_list_shower_deposit_weave_kernel(
             copy(dst.bitcast(word).rearrange("p (k n h) -> p k n h", h=2, n=CHUNK),
                  pairs[:, k0:k1, :, :].bitcast(word).rearrange("p k h n -> p k n h"))
 
-        scatter(last_unit)
         open_spans(0, 1)
+        scatter(last_unit)
+        open_spans(1, 2)
         on_vector = (nc.vector.tensor_copy, I32)
         on_scalar = (nc.scalar.copy, U32)
         weigh_last(0, 1)
@@ -471,7 +477,6 @@ def tile_list_shower_deposit_weave_kernel(
         weave_pairs(2, 3, *on_scalar)
         quantize_z(1, spans[0])
         finish(0)
-        open_spans(1, 2)
         weigh_last(3, 4)
         quantize_z(1, spans[1])
         finish(1)

@@ -170,24 +170,30 @@ def tile_list_shower_deposit_weave_kernel(
         load_gain("had", 1)
         w1_raw.append(load_w1(1))
 
-        w1_parts = {}
+        w1_word_parts = {}
+        w1_scale_parts = {}
 
-        def reorder_w1(b, t0, t1, host=None):
+        def reorder_words(b, t0, t1, host=None):
             words = slot("w1_words%d_%d" % (b, t0), [P, (t1 - t0) * PASSES * 2 * P], U8, host)
             nc.gpsimd.tensor_copy(words[:].bitcast(U16).rearrange("p (t a m) -> p t a m", a=PASSES, m=P),
                                   w1_raw[b][:].bitcast(U16).rearrange("p (a m t) -> p t a m", t=PACK, m=P)[:, t0:t1, :, :])
-            scales = slot("w1_sc%d_%d" % (b, t0), [P, (t1 - t0) * PASSES * P], U8, "w1_raw%d" % b if t1 == PACK else None)
-            nc.gpsimd.tensor_copy(scales[:].rearrange("p (t a m) -> p t a m", a=PASSES, m=P),
+            for t in range(t0, t1):
+                w1_word_parts[PACK * b + t] = words[:, PASSES * 2 * P * (t - t0) : PASSES * 2 * P * (t - t0 + 1)]
+
+        def reorder_scales(scales, b, t0, t1):
+            nc.gpsimd.tensor_copy(scales.rearrange("p (t a m) -> p t a m", a=PASSES, m=P),
                                   w1_sc_raw[:].rearrange("p (a b m t) -> p b t a m", a=PASSES, t=PACK, m=P)[:, b, t0:t1, :, :])
             for t in range(t0, t1):
-                w1_parts[PACK * b + t] = (words, scales, PASSES * P * (t - t0))
+                w1_scale_parts[PACK * b + t] = scales[:, PASSES * P * (t - t0) : PASSES * P * (t - t0 + 1)]
 
         v1_w = slot("v1_w", [P, PASSES, S], U32)
         gather(v1_w[:, 0, :], tab_w[0][:].bitcast(U32), idx1, 0, S)
         gather(v1_w[:, 1, 0:FIRST], tab_w[1][:].bitcast(U32), idx1, 0, FIRST)
         gather(v1_w[:, 1, FIRST:S], tab_w[1][:].bitcast(U32), idx1, FIRST, S)
-        reorder_w1(0, 0, 1)
-        reorder_w1(0, 1, 2, "v2_w")
+        reorder_scales(slot("w1_sc0", [P, PASSES * P], U8)[:], 0, 0, 1)
+        reorder_words(0, 0, 1)
+        reorder_scales(slot("w1_sc1", [P, 2 * PASSES * P], U8)[:], 0, 1, 3)
+        reorder_words(0, 1, 2, "v2_w")
 
         last = PAGES - 1
         units = [("pho", i) for i in range(LAG)]
@@ -210,8 +216,8 @@ def tile_list_shower_deposit_weave_kernel(
 
         after_page = {u + 3: i for u, (stream, i) in enumerate(units) if stream == "had" and i < PACK}
         raw_hosts = {u: "resp%d" % (i % RESP_SLOTS) for u, i in after_page.items()}
-        raw_hosts.update({first_hadron - 1: "w2_bf0", first_hadron + 1: "resp1", last_unit - 1: "woven_0"})
-        feat_hosts = {0: "feat0", 1: "feat1", first_hadron - 1: "resp2", first_hadron: "w1_words1_0"}
+        raw_hosts.update({first_hadron - 1: "w2_bf0", first_hadron: ("resp0", "w2_bf1"), first_hadron + 1: ("resp1", "w1_words1_0"), last_unit - 1: "woven_0"})
+        feat_hosts = {0: "feat0", 1: "feat1", first_hadron - 1: "resp2"}
 
         def staging(u):
             if u in raw_hosts:
@@ -224,11 +230,9 @@ def tile_list_shower_deposit_weave_kernel(
                                 rhs=v2_w[:, cols].bitcast(FP8X4), rhs_scale=v2_sc[:, cols], start=True, stop=True)
 
         def photon_sums(sums, i, cols):
-            words, scales, first = w1_parts[i]
             for a in range(PASSES):
-                c0 = first + P * a
-                nc.tensor.matmul_mx(out=sums, lhsT=words[:, 2 * c0 : 2 * (c0 + P)].bitcast(FP4X4),
-                                    lhsT_scale=scales[:, c0 : c0 + P],
+                nc.tensor.matmul_mx(out=sums, lhsT=w1_word_parts[i][:, 2 * P * a : 2 * P * (a + 1)].bitcast(FP4X4),
+                                    lhsT_scale=w1_scale_parts[i][:, P * a : P * (a + 1)],
                                     rhs=v1_w[:, a, cols].bitcast(FP8X4),
                                     rhs_scale=v1_sc[:, S * a + cols.start : S * a + cols.stop],
                                     start=(a == 0), stop=(a == PASSES - 1))
@@ -249,13 +253,17 @@ def tile_list_shower_deposit_weave_kernel(
                                      ACT.Square if stream == "had" else ACT.Relu)
             nc.gpsimd.tensor_tensor(split(feats[u][:], P), raw, split(gains[(stream, i % PACK)][:], P), MULT)
 
-        def produce_first_hadron():
-            feats[first_hadron] = slot("feat_had", [P, S], F32, feat_hosts[first_hadron])
-            for bank, cols, host in zip(banks, halves, ("resp0", "w2_bf1")):
-                raw = slot("raw_had_%d" % cols.start, [P, BANK], F32, host)
-                hadron_sums(bank[:], 0, cols)
-                nc.scalar.activation(raw[:], bank[:], ACT.Square)
-                nc.gpsimd.tensor_tensor(feats[first_hadron][:, cols], raw[:], gains[("had", 0)][:, cols], MULT)
+        def produce_by_banks(u):
+            stream, i = units[u]
+            feats[u] = slot("feat_%d" % u, [P, S], F32, "feat%d" % u)
+            for bank, cols, host in zip(banks, halves, raw_hosts[u]):
+                raw = slot("raw_%d_%d" % (u, cols.start), [P, BANK], F32, host)
+                if stream == "had":
+                    hadron_sums(bank[:], i, cols)
+                else:
+                    photon_sums(bank[:], i, cols)
+                nc.scalar.activation(raw[:], bank[:], ACT.Square if stream == "had" else ACT.Relu)
+                nc.gpsimd.tensor_tensor(feats[u][:, cols], raw[:], gains[(stream, i % PACK)][:, cols], MULT)
 
         def produce_last():
             raw = slot("raw_last", [P, S], F32)
@@ -340,11 +348,15 @@ def tile_list_shower_deposit_weave_kernel(
             feats[i] = slot("feat_%d" % i, [P, S - cuts[i]], F32, feat_hosts[i])
             nc.gpsimd.tensor_tensor(feats[i][:], raw[:], gains[("pho", i)][:, cuts[i] : S], MULT)
             nc.vector.tensor_copy(pages[i][:].indirect(entries(idx3, cuts[i], S)), feats[i][:])
-        reorder_w1(0, LAG, PACK)
+        reorder_words(0, 2, 3)
         produce(2)
         round_w2(0)
         quantize_w2(0)
-        produce_first_hadron()
+        reorder_words(0, 3, PACK, "w2_bf0")
+        late_scales = slot("w1_sc_late", [P, (PACK + 1) * PASSES * P], U8, "w1_raw0")
+        reorder_scales(late_scales[:, 0 : PASSES * P], 0, 3, PACK)
+        reorder_scales(late_scales[:, PASSES * P :], 1, 0, PACK)
+        produce_by_banks(first_hadron)
         round_w2(1)
         load_squared_resp(0)
         for t in range(2, PACK):
@@ -357,8 +369,12 @@ def tile_list_shower_deposit_weave_kernel(
         for u in range(AHEAD, last_unit):
             stream, i = units[u]
             ahead = u + AHEAD
-            if ahead < last_unit - 1:
+            if ahead == first_hadron + 1:
+                produce_by_banks(ahead)
+            elif ahead < last_unit - 1:
                 produce(ahead)
+            if u == first_hadron:
+                reorder_words(1, 0, PACK)
             if ahead == last_unit - 2:
                 produce(last_unit - 1)
             if ahead == last_unit - 1:
@@ -372,7 +388,6 @@ def tile_list_shower_deposit_weave_kernel(
                 load_squared_resp(2)
             if u == first_hadron:
                 quantize_w2(1)
-                reorder_w1(1, 0, PACK)
             if stream == "had":
                 if i == last - 1:
                     sixth = split(slot("plane_6", [P, T2], BF16, "v1_w")[:], CHUNK)
@@ -488,9 +503,9 @@ def tile_list_shower_deposit_weave_kernel(
         open_spans(3, 4)
         weave_pairs(4, 6, *on_vector)
         weigh_last(6, 7)
+        weave_pairs(6, 7, *on_scalar)
         quantize_z(1, spans[3])
         finish(3)
-        weave_pairs(6, 7, *on_vector)
         weigh_last(7, 8)
         open_spans(4, 6)
         weave_pairs(7, 8, *on_vector)

@@ -106,9 +106,9 @@ def tile_list_shower_deposit_weave_kernel(
                               w1_words[:, :, 2 * K_PASS * b : 2 * K_PASS * (b + 1)].rearrange("a p n -> p a n").bitcast(I32))
             return raw
 
-        def load_w2(b, tag):
-            raw = slot("w2_raw%d" % b, [P, PACK, K_PASS], F32, tag)
-            nc.sync.dma_start(raw[:], w2[:, K_PASS * b : K_PASS * (b + 1)].rearrange("(p j) c -> p j c", j=PACK))
+        def load_w2(lo, hi, tag):
+            raw = slot("w2_raw%d" % lo, [P, PACK, hi - lo], F32, tag)
+            nc.sync.dma_start(raw[:], w2[:, lo:hi].rearrange("(p j) c -> p j c", j=PACK))
             return raw
 
         gains = {}
@@ -158,14 +158,14 @@ def tile_list_shower_deposit_weave_kernel(
             nc.gpsimd.memset(tile[:].bitcast(I32), 0)
         load_gain("pho", 0, FIRST, S)
         load_gain("pho", 1, BANK, S)
-        load_gain("pho", 2)
-        w2_raw = [load_w2(0, "page2")]
         v2_sc_rows = slot("v2_sc_rows", [P, S], U8)
         gather(v2_sc_rows[:], tab2_sc[:], idx2, 0, S)
         place_rows(nc.sync, v2_sc, v2_sc_rows, 1)
+        load_gain("pho", 2)
+        w2_raw = [load_w2(0, K_PASS // 2, "woven_0"), load_w2(K_PASS // 2, K_PASS, "page2")]
         idx4 = load_list("idx4", offs4)
         load_gain("had", 0)
-        w2_raw.append(load_w2(1, "page3"))
+        w2_raw.append(load_w2(K_PASS, H, "page3"))
         load_gain("pho", 3)
         load_gain("had", 1)
         w1_raw.append(load_w1(1))
@@ -216,8 +216,8 @@ def tile_list_shower_deposit_weave_kernel(
 
         after_page = {u + 3: i for u, (stream, i) in enumerate(units) if stream == "had" and i < PACK}
         raw_hosts = {u: "resp%d" % (i % RESP_SLOTS) for u, i in after_page.items()}
-        raw_hosts.update({first_hadron - 1: "w2_bf0", first_hadron: ("resp0", "w2_bf1"), first_hadron + 1: ("resp1", "w1_words1_0"), last_unit - 1: "woven_0"})
-        feat_hosts = {0: "feat0", 1: "feat1", first_hadron - 1: "resp2"}
+        raw_hosts.update({first_hadron - 1: "w2_bf0", first_hadron: ("resp0", "w2_bf1"), first_hadron + 1: "resp1", last_unit - 1: "woven_0"})
+        feat_hosts = {0: "feat0", 1: "feat1", first_hadron - 1: "resp2", first_hadron: "w1_words1_0"}
 
         def staging(u):
             if u in raw_hosts:
@@ -255,7 +255,7 @@ def tile_list_shower_deposit_weave_kernel(
 
         def produce_by_banks(u):
             stream, i = units[u]
-            feats[u] = slot("feat_%d" % u, [P, S], F32, "feat%d" % u)
+            feats[u] = slot("feat_%d" % u, [P, S], F32, feat_hosts[u])
             for bank, cols, host in zip(banks, halves, raw_hosts[u]):
                 raw = slot("raw_%d_%d" % (u, cols.start), [P, BANK], F32, host)
                 if stream == "had":
@@ -309,12 +309,13 @@ def tile_list_shower_deposit_weave_kernel(
         def round_w2(b):
             w2_bf[b] = slot("w2_bf%d" % b, [P, PACK * K_PASS], BF16)
             rounded = w2_bf[b][:].rearrange("p (t m j) -> p m t j", m=P, j=PACK)
-            values = w2_raw[b][:].rearrange("p j (m t) -> p m t j", t=PACK)
+            values = [raw[:].rearrange("p j (m t) -> p m t j", t=PACK) for raw in w2_raw]
             if b == 0:
-                nc.scalar.copy(rounded[:, :, 0:2, :], values[:, :, 0:2, :])
-                nc.gpsimd.tensor_scalar(rounded[:, :, 2:PACK, :], values[:, :, 2:PACK, :], 1.0, 0.0, MULT, ADD)
+                nc.scalar.copy(rounded[:, 0 : P // 2, :, :], values[0])
+                nc.scalar.copy(rounded[:, P // 2 : P, 0:2, :], values[1][:, :, 0:2, :])
+                nc.gpsimd.tensor_scalar(rounded[:, P // 2 : P, 2:PACK, :], values[1][:, :, 2:PACK, :], 1.0, 0.0, MULT, ADD)
             else:
-                nc.scalar.copy(rounded, values)
+                nc.scalar.copy(rounded, values[2])
 
         def quantize_w2(b):
             w2_codes[b] = slot("w2_codes%d" % b, [P, K_PASS], U32)
@@ -353,9 +354,7 @@ def tile_list_shower_deposit_weave_kernel(
         round_w2(0)
         quantize_w2(0)
         reorder_words(0, 3, PACK, "w2_bf0")
-        late_scales = slot("w1_sc_late", [P, (PACK + 1) * PASSES * P], U8, "w1_raw0")
-        reorder_scales(late_scales[:, 0 : PASSES * P], 0, 3, PACK)
-        reorder_scales(late_scales[:, PASSES * P :], 1, 0, PACK)
+        reorder_scales(slot("w1_sc3", [P, PASSES * P], U8, "w1_raw0")[:], 0, 3, PACK)
         produce_by_banks(first_hadron)
         round_w2(1)
         load_squared_resp(0)
@@ -369,12 +368,8 @@ def tile_list_shower_deposit_weave_kernel(
         for u in range(AHEAD, last_unit):
             stream, i = units[u]
             ahead = u + AHEAD
-            if ahead == first_hadron + 1:
-                produce_by_banks(ahead)
-            elif ahead < last_unit - 1:
+            if ahead < last_unit - 1:
                 produce(ahead)
-            if u == first_hadron:
-                reorder_words(1, 0, PACK)
             if ahead == last_unit - 2:
                 produce(last_unit - 1)
             if ahead == last_unit - 1:
@@ -388,6 +383,8 @@ def tile_list_shower_deposit_weave_kernel(
                 load_squared_resp(2)
             if u == first_hadron:
                 quantize_w2(1)
+                reorder_words(1, 0, PACK)
+                reorder_scales(slot("w1_sc4", [P, PACK * PASSES * P], U8, "w1_raw1")[:], 1, 0, PACK)
             if stream == "had":
                 if i == last - 1:
                     sixth = split(slot("plane_6", [P, T2], BF16, "v1_w")[:], CHUNK)
@@ -503,9 +500,9 @@ def tile_list_shower_deposit_weave_kernel(
         open_spans(3, 4)
         weave_pairs(4, 6, *on_vector)
         weigh_last(6, 7)
-        weave_pairs(6, 7, *on_scalar)
         quantize_z(1, spans[3])
         finish(3)
+        weave_pairs(6, 7, *on_vector)
         weigh_last(7, 8)
         open_spans(4, 6)
         weave_pairs(7, 8, *on_vector)

@@ -153,7 +153,7 @@ def tile_list_shower_deposit_weave_kernel(
         load_scale_rows(nc.gpsimd, w1_sc_raw, w1_scales)
         v1_sc_rows = slot("v1_sc_rows", [P, S], U8)
         gather(v1_sc_rows[:], tab_sc[:], idx1, 0, S)
-        place_rows(nc.gpsimd, v1_sc, v1_sc_rows, PASSES)
+        place_rows(nc.scalar, v1_sc, v1_sc_rows, PASSES)
         for tile in (v2_sc, w3_sc):
             nc.gpsimd.memset(tile[:].bitcast(I32), 0)
         load_gain("pho", 0, FIRST, S)

@@ -41,7 +41,8 @@ ARRIVAL = P - QUAD
 QUAD_ORDER = (0, 2, 1, 3)
 CHUNK = 256
 CHUNKS = T2 // CHUNK
-EDGES = [0, CHUNK, BANK, 2 * BANK, 3 * BANK, T2 - CHUNK, T2]
+EDGES = [0, CHUNK, BANK, 2 * BANK, 3 * BANK, T2]
+EARLY = 2
 
 
 def tile_list_shower_deposit_weave_kernel(
@@ -421,50 +422,39 @@ def tile_list_shower_deposit_weave_kernel(
             j, first = divmod(cols.start, BANK)
             return woven_quarters[j][:, PACK * first : PACK * (first + cols.stop - cols.start)]
 
-        def sums(c, n):
+        def multiply(c, b, n):
+            w0 = N * b + P * n
             width = spans[c].stop - spans[c].start
-            bank, col = divmod((N // P) * (spans[c].start % HALF) + n * width, BANK)
-            return banks[bank], col, width
-
-        def accumulate(c, b):
-            for n in range(N // P):
-                w0 = N * b + P * n
-                bank, col, width = sums(c, n)
-                nc.tensor.matmul_mx(out=bank[:, col : col + width],
-                                    lhsT=w3_codes[:, w0 : w0 + P].bitcast(FP8X4), lhsT_scale=w3_sc[:, w0 : w0 + P],
-                                    rhs=codes(b, spans[c]).bitcast(FP8X4), rhs_scale=z_sc[b][:, spans[c]],
-                                    start=(b == 0 and col == 0), stop=(b == PASSES - 1 and col + width == BANK))
+            sums = banks[(N // P) * (c % 2) + n][:, 0:width]
+            nc.tensor.matmul_mx(out=sums, lhsT=w3_codes[:, w0 : w0 + P].bitcast(FP8X4), lhsT_scale=w3_sc[:, w0 : w0 + P],
+                                rhs=codes(b, spans[c]).bitcast(FP8X4), rhs_scale=z_sc[b][:, spans[c]],
+                                start=(b == 0), stop=(b == PASSES - 1))
+            return sums
 
         stages = []
-        vector_banks = [(len(spans) - 2, 2), (len(spans) - 1, 0)]
 
         def finish(c):
-            accumulate(c, 1)
             for n in range(N // P):
-                bank, col, width = sums(c, n)
+                if c >= EARLY:
+                    multiply(c, 0, n)
+                sums = multiply(c, 1, n)
+                width = spans[c].stop - spans[c].start
                 if n % 2 == 0:
                     stages.append(slot("stage_%d_%d" % (c, n), [P, 2 * width], F32, "feat%d" % (len(stages) % FEAT_SLOTS)))
-                if width == BANK or (c == 0 and n < 2):
-                    count = 1
-                elif n % 2 == 0:
-                    count = 2
-                else:
-                    continue
-                part = stages[-1][:, width * (n % 2) : width * (n % 2 + count)]
-                copy = nc.vector.tensor_copy if (c, n) in vector_banks else nc.scalar.copy
-                copy(part, bank[:, col : col + count * width])
-                rows = out[P * n : P * (n + count), spans[c]]
-                nc.sync.dma_start(rows.rearrange("(n p) c -> p n c", p=P), split(part, width))
+                part = stages[-1][:, width * (n % 2) : width * (n % 2 + 1)]
+                copy = nc.vector.tensor_copy if c == len(spans) - 1 and n % 2 == 1 else nc.scalar.copy
+                copy(part, sums)
+                nc.sync.dma_start(out[P * n : P * (n + 1), spans[c]], part)
 
         def quantize_z(b, cols):
             nc.vector.quantize_mx(out=codes(b, cols).bitcast(FP8X4), scales=z_sc[b][:, cols], in_=woven_cols(b, cols))
 
-        def open_spans(c0, c1):
-            cols = slice(spans[c0].start, spans[c1 - 1].stop)
-            first_codes[cols.start] = slot("z_codes0_%d" % c0, [P, cols.stop - cols.start], U32, first_hosts[c0])
-            quantize_z(0, cols)
-            for c in range(c0, c1):
-                accumulate(c, 0)
+        def open_span(c):
+            first_codes[spans[c].start] = slot("z_codes0_%d" % c, [P, spans[c].stop - spans[c].start], U32, first_hosts[c])
+            quantize_z(0, spans[c])
+            if c < EARLY:
+                for n in range(N // P):
+                    multiply(c, 0, n)
 
         def weigh_last(k0, k1):
             cols = slice(CHUNK * k0, CHUNK * k1)
@@ -476,9 +466,9 @@ def tile_list_shower_deposit_weave_kernel(
             copy(dst.bitcast(word).rearrange("p (k n h) -> p k n h", h=2, n=CHUNK),
                  pairs[:, k0:k1, :, :].bitcast(word).rearrange("p k h n -> p k n h"))
 
-        open_spans(0, 1)
+        open_span(0)
         scatter(last_unit)
-        open_spans(1, 2)
+        open_span(1)
         on_vector = (nc.vector.tensor_copy, I32)
         on_scalar = (nc.scalar.copy, U32)
         weigh_last(0, 1)
@@ -493,20 +483,18 @@ def tile_list_shower_deposit_weave_kernel(
         quantize_z(1, spans[1])
         finish(1)
         weave_pairs(3, 4, *on_vector)
-        open_spans(2, 3)
+        open_span(2)
         quantize_z(1, spans[2])
         finish(2)
         weigh_last(4, 6)
-        open_spans(3, 4)
+        open_span(3)
         weave_pairs(4, 6, *on_vector)
         weigh_last(6, 7)
         quantize_z(1, spans[3])
         finish(3)
-        weave_pairs(6, 7, *on_vector)
         weigh_last(7, 8)
-        open_spans(4, 6)
+        weave_pairs(6, 7, *on_vector)
         weave_pairs(7, 8, *on_vector)
+        open_span(4)
         quantize_z(1, spans[4])
-        quantize_z(1, spans[5])
         finish(4)
-        finish(5)

@@ -149,16 +149,16 @@ def tile_list_shower_deposit_weave_kernel(
         tab_w.append(load_words("tab_w1", tab_words[1], "page1"))
         w1_raw = [load_w1(0)]
         load_gain("pho", 0, 0, FIRST)
-        load_gain("pho", 1, 0, BANK)
+        load_gain("pho", 1, 0, FIRST)
         tab2_w = load_words("tab2_w", tab2_words[0], "page3")
-        load_scale_rows(nc.gpsimd, w1_sc_raw, w1_scales)
+        load_scale_rows(nc.scalar, w1_sc_raw, w1_scales)
         v1_sc_rows = slot("v1_sc_rows", [P, S], U8)
         gather(v1_sc_rows[:], tab_sc[:], idx1, 0, S)
         place_rows(nc.scalar, v1_sc, v1_sc_rows, PASSES)
         for tile in (v2_sc, w3_sc):
             nc.gpsimd.memset(tile[:].bitcast(I32), 0)
         load_gain("pho", 0, FIRST, S)
-        load_gain("pho", 1, BANK, S)
+        load_gain("pho", 1, FIRST, S)
         v2_sc_rows = slot("v2_sc_rows", [P, S], U8)
         gather(v2_sc_rows[:], tab2_sc[:], idx2, 0, S)
         place_rows(nc.sync, v2_sc, v2_sc_rows, 1)
@@ -333,7 +333,7 @@ def tile_list_shower_deposit_weave_kernel(
                 photon_sums(sums, i, cols)
                 nc.scalar.activation(raw[:, cols.start - lo : cols.stop - lo], sums, ACT.Relu)
 
-        cuts = [FIRST, BANK]
+        cuts = [FIRST, FIRST]
         for i in range(LAG):
             raw = slot("raw_%d" % i, [P, cuts[i]], F32)
             raw_features(raw, i, 0, cuts[i])
@@ -486,15 +486,12 @@ def tile_list_shower_deposit_weave_kernel(
         open_span(2)
         quantize_z(1, spans[2])
         finish(2)
-        weigh_last(4, 6)
-        open_span(3)
-        weave_pairs(4, 6, *on_vector)
-        weigh_last(6, 7)
-        quantize_z(1, spans[3])
-        finish(3)
-        weigh_last(7, 8)
-        weave_pairs(6, 7, *on_vector)
-        weave_pairs(7, 8, *on_vector)
-        open_span(4)
-        quantize_z(1, spans[4])
-        finish(4)
+        for c in range(3, len(spans)):
+            chunks = range(spans[c].start // CHUNK, spans[c].stop // CHUNK)
+            for k in chunks:
+                weigh_last(k, k + 1)
+            for k in chunks:
+                weave_pairs(k, k + 1, *on_vector)
+            open_span(c)
+            quantize_z(1, spans[c])
+            finish(c)

@@ -116,7 +116,8 @@ def tile_list_shower_deposit_weave_kernel(
 
         def load_gain(stream, t, lo=0, hi=S):
             if (stream, t) not in gains:
-                gains[(stream, t)] = slot("gain_%s%d" % (stream, t), [P, S], F32)
+                host = "woven_0" if (stream, t) == ("had", (PAGES - 2) % PACK) else None
+                gains[(stream, t)] = slot("gain_%s%d" % (stream, t), [P, S], F32, host)
             src = wg2 if stream == "had" else wg1
             rows = src.rearrange("(m t) j -> m t j", t=PACK)[:, t, :]
             for q in QUAD_ORDER:
@@ -217,7 +218,7 @@ def tile_list_shower_deposit_weave_kernel(
 
         after_page = {u + 3: i for u, (stream, i) in enumerate(units) if stream == "had" and i < PACK}
         raw_hosts = {u: "resp%d" % (i % RESP_SLOTS) for u, i in after_page.items()}
-        raw_hosts.update({first_hadron - 1: "w2_bf0", first_hadron: ("resp0", "w2_bf1"), first_hadron + 1: "resp1", last_unit - 1: "woven_0"})
+        raw_hosts.update({first_hadron - 1: "w2_bf0", first_hadron: ("resp0", "w2_bf1"), first_hadron + 1: "resp1", last_unit - 1: "w2_bf0"})
         feat_hosts = {0: "feat0", 1: "feat1", first_hadron - 1: "resp2", first_hadron: "w1_words1_0"}
 
         def staging(u):
@@ -375,6 +376,7 @@ def tile_list_shower_deposit_weave_kernel(
                 produce(last_unit - 1)
             if ahead == last_unit - 1:
                 produce_last()
+                woven_first = weave_first_pass()
             if ahead == first_hadron + 1:
                 load_squared_resp(1)
             if ahead in after_page:
@@ -394,8 +396,6 @@ def tile_list_shower_deposit_weave_kernel(
                         nc.scalar.copy(plane(i)[:, chunks, :], sixth[:, chunks, :])
                 else:
                     weigh(i, plane(i))
-                if i == PACK:
-                    woven_first = weave_first_pass()
                 if i == PACK + 1:
                     pair_planes()
                 if i == last - 1:
@@ -404,7 +404,7 @@ def tile_list_shower_deposit_weave_kernel(
         spans = [slice(lo, hi) for lo, hi in zip(EDGES, EDGES[1:])]
 
         woven_hosts = ["planes", "page0", "page1", "resp2"]
-        first_hosts = {0: None, 1: "resp%d" % ((last - 1) % RESP_SLOTS), 2: "planes", 3: "page0", 4: "page1"}
+        first_hosts = {0: "gain_pho%d" % (last % PACK), 1: "resp%d" % ((last - 1) % RESP_SLOTS), 2: "planes", 3: "page0", 4: "page1"}
         woven_quarters = [slot("woven_1_%d" % j, [P, PACK * BANK], BF16, host) for j, host in enumerate(woven_hosts)]
         first_codes = {}
         second_codes = slot("z_codes1", [P, T2], U32, "page%d" % ((last - 1) % PAGE_SLOTS))

from contextlib import ExitStack

import concourse.mybir as mybir

K, K2, H, N, T, S, T2 = 1024, 512, 1024, 512, 2048, 1024, 2048
FLOPS = 2 * (K * H * S + K2 * H * S + H * N * T2)

F32 = mybir.dt.float32
BF16 = mybir.dt.bfloat16
I32 = mybir.dt.int32
U32 = mybir.dt.uint32
U16 = mybir.dt.uint16
U8 = mybir.dt.uint8
FP8X4 = mybir.dt.float8_e4m3fn_x4
FP4X4 = mybir.dt.float4_e2m1fn_x4
ACT = mybir.ActivationFunctionType
MULT = mybir.AluOpType.mult
ADD = mybir.AluOpType.add

P = 128
PACK = 4
K_PASS = P * PACK
BANK = 512
BANKS = 8
QUAD = 32
QUADS = P // QUAD
ROWS = 4
PASSES = 2
PAGES = H // P
HALF = T2 // 2
PER_COL = 16
RUN = 4

LAG = 2
PAGE_SLOTS = LAG + 2
RESP_SLOTS = 3
FEAT_SLOTS = 6
AHEAD = 2
FIRST = 256
ARRIVAL = P - QUAD
QUAD_ORDER = (0, 2, 1, 3)
CHUNK = 256
CHUNKS = T2 // CHUNK
EDGES = [0, CHUNK, BANK, 2 * BANK, 3 * BANK, T2]
EARLY = 2


def tile_list_shower_deposit_weave_kernel(
    tc, tab_words, tab_scales, tab2_words, tab2_scales, w1_words, w1_scales, w2,
    w3_words, w3_scales, resp, wg1, wg2, offs, offs2, offs3, offs4, out,
):
    nc = tc.nc
    with ExitStack() as ctx:
        sb = ctx.enter_context(tc.tile_pool(name="sb", bufs=1))
        ps = ctx.enter_context(tc.psum_pool(name="ps", bufs=1))

        def slot(name, shape, dtype, tag=None):
            return sb.tile(shape, dtype, name=name, tag=tag or name, align_bytes=64)

        def load_list(name, src):
            lst = slot(name, [P, S // PER_COL], U16)
            nc.sync.dma_start(lst[:], src)
            return lst

        def rows_i32(tile, first, count):
            return tile[first : first + count, :].bitcast(I32)

        def split(ap, width):
            return ap.rearrange("p (c n) -> p c n", n=width)

        banks = [ps.tile([P, BANK], F32, name="bank%d" % j, tag="bank%d" % j) for j in range(BANKS)]

        tab_sc = slot("tab_sc", [P, T], U8)
        tab2_sc = slot("tab2_sc", [P, T], U8)
        w1_sc_raw = slot("w1_sc_raw", [P, PASSES * H], U8)
        v1_sc = slot("v1_sc", [P, PASSES * S], U8)
        v2_sc = slot("v2_sc", [P, S], U8)
        w3_sc = slot("w3_sc", [P, PASSES * N], U8)
        for tile in (tab_sc, tab2_sc):
            nc.vector.memset(rows_i32(tile, 0, ARRIVAL), 0)
        nc.vector.memset(v1_sc[:].bitcast(I32), 0)
        nc.gpsimd.memset(w1_sc_raw[:].bitcast(I32), 0)

        def load_arrival_rows(tile, src):
            nc.scalar.dma_start(rows_i32(tile, ARRIVAL, QUAD), src.rearrange("a g n -> g a n").bitcast(I32))

        def place_rows(queue, placed, arrived, passes):
            for q in range(QUADS):
                first = ARRIVAL + PASSES * ROWS * q
                queue.dma_start(rows_i32(placed, QUAD * q, ROWS),
                                arrived[first : first + PASSES * ROWS : PASSES // passes, :].bitcast(I32))

        def load_words(name, src, tag):
            words = slot(name, [P, T], I32, tag)
            nc.sync.dma_start(words[:], src.rearrange("p n i -> p (n i)").bitcast(I32))
            return words

        def load_scale_rows(queue, tile, src):
            for q in range(QUADS):
                queue.dma_start(
                    rows_i32(tile, QUAD * q, ROWS).rearrange("r (a n) -> r a n", a=src.shape[0]),
                    src[:, ROWS * q : ROWS * (q + 1), :].rearrange("a r n -> r a n").bitcast(I32))

        def load_w1(b):
            raw = slot("w1_raw%d" % b, [P, PASSES * 2 * K_PASS], U8)
            nc.sync.dma_start(raw[:].bitcast(I32).rearrange("p (a n) -> p a n", a=PASSES),
                              w1_words[:, :, 2 * K_PASS * b : 2 * K_PASS * (b + 1)].rearrange("a p n -> p a n").bitcast(I32))
            return raw

        def load_w2(lo, hi, tag):
            raw = slot("w2_raw%d" % lo, [P, PACK, hi - lo], F32, tag)
            nc.sync.dma_start(raw[:], w2[:, lo:hi].rearrange("(p j) c -> p j c", j=PACK))
            return raw

        gains = {}

        def load_gain(stream, t, lo=0, hi=S):
            if (stream, t) not in gains:
                host = "woven_0" if (stream, t) == ("had", (PAGES - 2) % PACK) else None
                gains[(stream, t)] = slot("gain_%s%d" % (stream, t), [P, S], F32, host)
            src = wg2 if stream == "had" else wg1
            rows = src.rearrange("(m t) j -> m t j", t=PACK)[:, t, :]
            for q in QUAD_ORDER:
                nc.sync.dma_start(gains[(stream, t)][QUAD * q : QUAD * (q + 1), lo:hi], rows[:, lo:hi])

        resp2 = {}

        def load_squared_resp(i, host=None):
            b, t = divmod(i, PACK)
            tile = slot("resp_%d" % i, [P, T2], F32, "resp%d" % (i % RESP_SLOTS))
            rows = resp[K_PASS * b : K_PASS * (b + 1), :].rearrange("(p t) n -> p t n", t=PACK)[:, t, :]
            nc.sync.dma_start(tile[:], rows)
            resp2[i] = slot("resp2_%d" % i, [P, T2], F32, host) if host else tile
            for h in range(2):
                cols = slice(HALF * h, HALF * (h + 1))
                nc.scalar.activation(resp2[i][:, cols], tile[:, cols], ACT.Square)

        def entries(lst, lo, hi):
            return lst[:, lo // PER_COL : hi // PER_COL]

        def gather(picked, window, lst, lo, hi):
            nc.vector.tensor_copy(picked, window.indirect(entries(lst, lo, hi)))

        idx1 = load_list("idx1", offs)
        load_arrival_rows(tab_sc, tab_scales)
        idx2 = load_list("idx2", offs2)
        load_arrival_rows(tab2_sc, tab2_scales.broadcast_to([PASSES, QUADS * ROWS, T]))
        tab_w = [load_words("tab_w0", tab_words[0], "resp2")]
        idx3 = load_list("idx3", offs3)
        tab_w.append(load_words("tab_w1", tab_words[1], "page1"))
        w1_raw = [load_w1(0)]
        load_gain("pho", 0, 0, FIRST)
        load_gain("pho", 1, 0, FIRST)
        tab2_w = load_words("tab2_w", tab2_words[0], "page3")
        load_scale_rows(nc.scalar, w1_sc_raw, w1_scales)
        v1_sc_rows = slot("v1_sc_rows", [P, S], U8)
        gather(v1_sc_rows[:], tab_sc[:], idx1, 0, S)
        place_rows(nc.scalar, v1_sc, v1_sc_rows, PASSES)
        for tile in (v2_sc, w3_sc):
            nc.gpsimd.memset(tile[:].bitcast(I32), 0)
        load_gain("pho", 0, FIRST, S)
        load_gain("pho", 1, FIRST, S)
        v2_sc_rows = slot("v2_sc_rows", [P, S], U8)
        gather(v2_sc_rows[:], tab2_sc[:], idx2, 0, S)
        place_rows(nc.sync, v2_sc, v2_sc_rows, 1)
        load_gain("pho", 2)
        w2_raw = [load_w2(0, K_PASS // 2, "woven_0"), load_w2(K_PASS // 2, K_PASS, "page2")]
        idx4 = load_list("idx4", offs4)
        load_gain("had", 0)
        w2_raw.append(load_w2(K_PASS, H, "page3"))
        load_gain("pho", 3)
        load_gain("had", 1)
        w1_raw.append(load_w1(1))

        w1_word_parts = {}
        w1_scale_parts = {}

        def reorder_words(b, t0, t1, host=None):
            words = slot("w1_words%d_%d" % (b, t0), [P, (t1 - t0) * PASSES * 2 * P], U8, host)
            nc.gpsimd.tensor_copy(words[:].bitcast(U16).rearrange("p (t a m) -> p t a m", a=PASSES, m=P),
                                  w1_raw[b][:].bitcast(U16).rearrange("p (a m t) -> p t a m", t=PACK, m=P)[:, t0:t1, :, :])
            for t in range(t0, t1):
                w1_word_parts[PACK * b + t] = words[:, PASSES * 2 * P * (t - t0) : PASSES * 2 * P * (t - t0 + 1)]

        def reorder_scales(scales, b, t0, t1):
            nc.gpsimd.tensor_copy(scales.rearrange("p (t a m) -> p t a m", a=PASSES, m=P),
                                  w1_sc_raw[:].rearrange("p (a b m t) -> p b t a m", a=PASSES, t=PACK, m=P)[:, b, t0:t1, :, :])
            for t in range(t0, t1):
                w1_scale_parts[PACK * b + t] = scales[:, PASSES * P * (t - t0) : PASSES * P * (t - t0 + 1)]

        v1_w = slot("v1_w", [P, PASSES, S], U32)
        gather(v1_w[:, 0, :], tab_w[0][:].bitcast(U32), idx1, 0, S)
        gather(v1_w[:, 1, 0:FIRST], tab_w[1][:].bitcast(U32), idx1, 0, FIRST)
        gather(v1_w[:, 1, FIRST:S], tab_w[1][:].bitcast(U32), idx1, FIRST, S)
        reorder_scales(slot("w1_sc0", [P, PASSES * P], U8)[:], 0, 0, 1)
        reorder_words(0, 0, 1)
        reorder_scales(slot("w1_sc1", [P, 2 * PASSES * P], U8)[:], 0, 1, 3)
        reorder_words(0, 1, 2, "v2_w")

        last = PAGES - 1
        units = [("pho", i) for i in range(LAG)]
        for i in range(LAG, last):
            units += [("pho", i), ("had", i - LAG)]
        units += [("had", i) for i in range(last - LAG, last)] + [("pho", last), ("had", last)]
        last_unit = len(units) - 1
        first_hadron = units.index(("had", 0))

        planes = slot("planes", [P, PACK, T2], BF16)
        pairs = slot("pairs", [P, CHUNKS, 2, 2 * CHUNK], BF16)

        def plane(i):
            b, t = divmod(i, PACK)
            if b == 0:
                return split(planes[:, t, :], CHUNK)
            if t < 2:
                return pairs[:, :, 1, CHUNK * t : CHUNK * (t + 1)]
            return pairs[:, :, 1, :].rearrange("p c (n e) -> p c n e", e=2)[:, :, :, t - 2]

        after_page = {u + 3: i for u, (stream, i) in enumerate(units) if stream == "had" and i < PACK}
        raw_hosts = {u: "resp%d" % (i % RESP_SLOTS) for u, i in after_page.items()}
        raw_hosts.update({first_hadron - 1: "w2_bf0", first_hadron: ("resp0", "w2_bf1"), first_hadron + 1: "resp1", last_unit - 1: "w2_bf0"})
        feat_hosts = {0: "feat0", 1: "feat1", first_hadron - 1: "resp2", first_hadron: "w1_words1_0"}

        def staging(u):
            if u in raw_hosts:
                return split(slot("raw_%d" % u, [P, S], F32, raw_hosts[u])[:], P)
            return plane(units[u - AHEAD][1]).bitcast(F32)

        def hadron_sums(sums, i, cols):
            m0 = P * i
            nc.tensor.matmul_mx(out=sums, lhsT=w2_codes[i // PACK][:, m0 % K_PASS : m0 % K_PASS + P].bitcast(FP8X4), lhsT_scale=w2_sc[:, m0 : m0 + P],
                                rhs=v2_w[:, cols].bitcast(FP8X4), rhs_scale=v2_sc[:, cols], start=True, stop=True)

        def photon_sums(sums, i, cols):
            for a in range(PASSES):
                nc.tensor.matmul_mx(out=sums, lhsT=w1_word_parts[i][:, 2 * P * a : 2 * P * (a + 1)].bitcast(FP4X4),
                                    lhsT_scale=w1_scale_parts[i][:, P * a : P * (a + 1)],
                                    rhs=v1_w[:, a, cols].bitcast(FP8X4),
                                    rhs_scale=v1_sc[:, S * a + cols.start : S * a + cols.stop],
                                    start=(a == 0), stop=(a == PASSES - 1))

        halves = [slice(0, BANK), slice(BANK, S)]
        feats = {}

        def produce(u):
            stream, i = units[u]
            raw = staging(u)
            feats[u] = slot("feat_%d" % u, [P, S], F32, feat_hosts.get(u, "feat%d" % (u % FEAT_SLOTS)))
            for bank, cols in zip(banks, halves):
                if stream == "had":
                    hadron_sums(bank[:], i, cols)
                else:
                    photon_sums(bank[:], i, cols)
                nc.scalar.activation(raw[:, cols.start // P : cols.stop // P, :], split(bank[:], P),
                                     ACT.Square if stream == "had" else ACT.Relu)
            nc.gpsimd.tensor_tensor(split(feats[u][:], P), raw, split(gains[(stream, i % PACK)][:], P), MULT)

        def produce_by_banks(u):
            stream, i = units[u]
            feats[u] = slot("feat_%d" % u, [P, S], F32, feat_hosts[u])
            for bank, cols, host in zip(banks, halves, raw_hosts[u]):
                raw = slot("raw_%d_%d" % (u, cols.start), [P, BANK], F32, host)
                if stream == "had":
                    hadron_sums(bank[:], i, cols)
                else:
                    photon_sums(bank[:], i, cols)
                nc.scalar.activation(raw[:], bank[:], ACT.Square if stream == "had" else ACT.Relu)
                nc.gpsimd.tensor_tensor(feats[u][:, cols], raw[:], gains[(stream, i % PACK)][:, cols], MULT)

        def produce_last():
            raw = slot("raw_last", [P, S], F32)
            for bank, cols in zip(banks, halves):
                hadron_sums(bank[:], last, cols)
                nc.scalar.activation(raw[:, cols], bank[:], ACT.Square)
            feats[last_unit] = slot("feat_last", [P, S], F32, "last_unit")
            nc.gpsimd.tensor_tensor(feats[last_unit][:], raw[:], gains[("had", last % PACK)][:], MULT)

        pages = {}

        def scatter(u):
            stream, i = units[u]
            if stream == "pho":
                pages[i] = slot("page_%d" % i, [P, T2], F32, "page%d" % (i % PAGE_SLOTS))
            nc.vector.tensor_copy(pages[i][:].indirect((idx4 if stream == "had" else idx3)[:]), feats[u][:])

        half_chunks = [slice(0, CHUNKS // 2), slice(CHUNKS // 2, CHUNKS)]

        def weigh(i, rounded):
            for chunks in half_chunks:
                cols = slice(CHUNK * chunks.start, CHUNK * chunks.stop)
                nc.gpsimd.tensor_tensor(rounded[:, chunks, :], split(pages[i][:, cols], CHUNK),
                                        split(resp2[i][:, cols], CHUNK), MULT)

        def weave_first_pass():
            woven = slot("woven_0", [P, T2 * PACK], BF16)
            for lo, hi in zip(EDGES, EDGES[1:]):
                nc.scalar.copy(
                    woven[:, PACK * lo : PACK * hi].rearrange("p (n e t) -> p n t e", t=PACK, e=RUN),
                    planes[:, :, lo:hi].rearrange("p t (n e) -> p n t e", e=RUN))
            return woven

        def pair_planes():
            for chunks in half_chunks:
                nc.scalar.copy(pairs[:, chunks, 0, :].rearrange("p c (n e) -> p c n e", e=2),
                               pairs[:, chunks, 1, :].rearrange("p c (e n) -> p c n e", e=2))

        w2_bf = {}
        w2_codes = {}
        w2_sc = slot("w2_sc", [P, H], U8)

        def round_w2(b):
            w2_bf[b] = slot("w2_bf%d" % b, [P, PACK * K_PASS], BF16)
            rounded = w2_bf[b][:].rearrange("p (t m j) -> p m t j", m=P, j=PACK)
            values = [raw[:].rearrange("p j (m t) -> p m t j", t=PACK) for raw in w2_raw]
            if b == 0:
                nc.scalar.copy(rounded[:, 0 : P // 2, :, :], values[0])
                nc.scalar.copy(rounded[:, P // 2 : P, 0:2, :], values[1][:, :, 0:2, :])
                nc.gpsimd.tensor_scalar(rounded[:, P // 2 : P, 2:PACK, :], values[1][:, :, 2:PACK, :], 1.0, 0.0, MULT, ADD)
            else:
                nc.scalar.copy(rounded, values[2])

        def quantize_w2(b):
            w2_codes[b] = slot("w2_codes%d" % b, [P, K_PASS], U32)
            nc.vector.quantize_mx(out=w2_codes[b][:].bitcast(FP8X4), scales=w2_sc[:, K_PASS * b : K_PASS * (b + 1)],
                                  in_=w2_bf[b][:])

        turns = []

        def raw_features(raw, i, lo, hi):
            for first in range(lo, hi, BANK):
                cols = slice(first, min(first + BANK, hi))
                sums = banks[len(turns) % 2][:, 0 : cols.stop - cols.start]
                turns.append(cols)
                photon_sums(sums, i, cols)
                nc.scalar.activation(raw[:, cols.start - lo : cols.stop - lo], sums, ACT.Relu)

        cuts = [FIRST, FIRST]
        for i in range(LAG):
            raw = slot("raw_%d" % i, [P, cuts[i]], F32)
            raw_features(raw, i, 0, cuts[i])
            pages[i] = slot("page_%d" % i, [P, T2], F32, "page%d" % i)
            nc.vector.tensor_tensor(pages[i][:].indirect(entries(idx3, 0, cuts[i])),
                                    raw[:], gains[("pho", i)][:, 0 : cuts[i]], MULT)
        rests = []
        for i, host in enumerate(("w1_words0_2", "rest_1")):
            rests.append(slot("rest_%d" % i, [P, S - cuts[i]], F32, host))
            raw_features(rests[i], i, cuts[i], S)
        v2_w = slot("v2_w", [P, S], U32)
        gather(v2_w[:], tab2_w[:].bitcast(U32), idx2, 0, S)
        for i, raw in enumerate(rests):
            feats[i] = slot("feat_%d" % i, [P, S - cuts[i]], F32, feat_hosts[i])
            nc.gpsimd.tensor_tensor(feats[i][:], raw[:], gains[("pho", i)][:, cuts[i] : S], MULT)
            nc.vector.tensor_copy(pages[i][:].indirect(entries(idx3, cuts[i], S)), feats[i][:])
        reorder_words(0, 2, 3)
        produce(2)
        round_w2(0)
        quantize_w2(0)
        reorder_words(0, 3, PACK, "w2_bf0")
        reorder_scales(slot("w1_sc3", [P, PASSES * P], U8, "w1_raw0")[:], 0, 3, PACK)
        produce_by_banks(first_hadron)
        round_w2(1)
        load_squared_resp(0)
        for t in range(2, PACK):
            load_gain("had", t)
        w3_codes = slot("w3_codes", [P, PASSES * N], I32)
        nc.sync.dma_start(w3_codes[:].rearrange("p (a n) -> p a n", a=PASSES),
                          w3_words.rearrange("a p n i -> p a (n i)").bitcast(I32))
        load_scale_rows(nc.sync, w3_sc, w3_scales)

        for u in range(AHEAD, last_unit):
            stream, i = units[u]
            ahead = u + AHEAD
            if ahead < last_unit - 1:
                produce(ahead)
            if ahead == last_unit - 2:
                produce(last_unit - 1)
            if ahead == last_unit - 1:
                produce_last()
                woven_first = weave_first_pass()
            if ahead == first_hadron + 1:
                load_squared_resp(1)
            if ahead in after_page:
                load_squared_resp(after_page[ahead] + RESP_SLOTS)
            scatter(u)
            if u == first_hadron - 1:
                load_squared_resp(2)
            if u == first_hadron:
                quantize_w2(1)
                reorder_words(1, 0, PACK)
                reorder_scales(slot("w1_sc4", [P, PACK * PASSES * P], U8, "w1_raw1")[:], 1, 0, PACK)
            if stream == "had":
                if i == last - 1:
                    sixth = split(slot("plane_6", [P, T2], BF16, "v1_w")[:], CHUNK)
                    weigh(i, sixth)
                    for chunks in half_chunks:
                        nc.scalar.copy(plane(i)[:, chunks, :], sixth[:, chunks, :])
                else:
                    weigh(i, plane(i))
                if i == PACK + 1:
                    pair_planes()
                if i == last - 1:
                    load_squared_resp(last, "v1_w")

        spans = [slice(lo, hi) for lo, hi in zip(EDGES, EDGES[1:])]

        woven_hosts = ["planes", "page0", "page1", "resp2"]
        first_hosts = {0: "gain_pho%d" % (last % PACK), 1: "resp%d" % ((last - 1) % RESP_SLOTS), 2: "planes", 3: "page0", 4: "page1"}
        woven_quarters = [slot("woven_1_%d" % j, [P, PACK * BANK], BF16, host) for j, host in enumerate(woven_hosts)]
        first_codes = {}
        second_codes = slot("z_codes1", [P, T2], U32, "page%d" % ((last - 1) % PAGE_SLOTS))
        z_sc = [slot("z_sc%d" % b, [P, T2], U8) for b in range(PASSES)]

        def codes(b, cols):
            if b == 1:
                return second_codes[:, cols]
            first = max(lo for lo in first_codes if lo <= cols.start)
            return first_codes[first][:, cols.start - first : cols.stop - first]

        def woven_cols(b, cols):
            if b == 0:
                return woven_first[:, PACK * cols.start : PACK * cols.stop]
            j, first = divmod(cols.start, BANK)
            return woven_quarters[j][:, PACK * first : PACK * (first + cols.stop - cols.start)]

        def multiply(c, b, n):
            w0 = N * b + P * n
            width = spans[c].stop - spans[c].start
            sums = banks[(N // P) * (c % 2) + n][:, 0:width]
            nc.tensor.matmul_mx(out=sums, lhsT=w3_codes[:, w0 : w0 + P].bitcast(FP8X4), lhsT_scale=w3_sc[:, w0 : w0 + P],
                                rhs=codes(b, spans[c]).bitcast(FP8X4), rhs_scale=z_sc[b][:, spans[c]],
                                start=(b == 0), stop=(b == PASSES - 1))
            return sums

        stages = []

        def finish(c):
            for n in range(N // P):
                if c >= EARLY:
                    multiply(c, 0, n)
                sums = multiply(c, 1, n)
                width = spans[c].stop - spans[c].start
                if n % 2 == 0:
                    stages.append(slot("stage_%d_%d" % (c, n), [P, 2 * width], F32, "feat%d" % (len(stages) % FEAT_SLOTS)))
                part = stages[-1][:, width * (n % 2) : width * (n % 2 + 1)]
                copy = nc.vector.tensor_copy if c == len(spans) - 1 and n % 2 == 1 else nc.scalar.copy
                copy(part, sums)
                nc.sync.dma_start(out[P * n : P * (n + 1), spans[c]], part)

        def quantize_z(b, cols):
            nc.vector.quantize_mx(out=codes(b, cols).bitcast(FP8X4), scales=z_sc[b][:, cols], in_=woven_cols(b, cols))

        def open_span(c):
            first_codes[spans[c].start] = slot("z_codes0_%d" % c, [P, spans[c].stop - spans[c].start], U32, first_hosts[c])
            quantize_z(0, spans[c])
            if c < EARLY:
                for n in range(N // P):
                    multiply(c, 0, n)

        def weigh_last(k0, k1):
            cols = slice(CHUNK * k0, CHUNK * k1)
            nc.vector.tensor_tensor(plane(last)[:, k0:k1, :], split(pages[last][:, cols], CHUNK),
                                    split(resp2[last][:, cols], CHUNK), MULT)

        def weave_pairs(k0, k1, copy, word):
            dst = woven_cols(1, slice(CHUNK * k0, CHUNK * k1))
            copy(dst.bitcast(word).rearrange("p (k n h) -> p k n h", h=2, n=CHUNK),
                 pairs[:, k0:k1, :, :].bitcast(word).rearrange("p k h n -> p k n h"))

        open_span(0)
        scatter(last_unit)
        open_span(1)
        on_vector = (nc.vector.tensor_copy, I32)
        on_scalar = (nc.scalar.copy, U32)
        weigh_last(0, 1)
        weigh_last(1, 2)
        weave_pairs(0, 1, *on_vector)
        weave_pairs(1, 2, *on_scalar)
        weigh_last(2, 3)
        weave_pairs(2, 3, *on_scalar)
        quantize_z(1, spans[0])
        finish(0)
        weigh_last(3, 4)
        quantize_z(1, spans[1])
        finish(1)
        weave_pairs(3, 4, *on_vector)
        open_span(2)
        quantize_z(1, spans[2])
        finish(2)
        for c in range(3, len(spans)):
            chunks = range(spans[c].start // CHUNK, spans[c].stop // CHUNK)
            for k in chunks:
                weigh_last(k, k + 1)
            for k in chunks:
                weave_pairs(k, k + 1, *on_vector)
            open_span(c)
            quantize_z(1, spans[c])
            finish(c)
